import numpy as np
import ml_dtypes


def mxq(x, axis, fmt="e4m3"):
    dtype, down = {"e4m3": (ml_dtypes.float8_e4m3fn, 7), "e5m2": (ml_dtypes.float8_e5m2, 14)}[fmt]
    v = np.moveaxis(np.asarray(x, np.float32).astype(ml_dtypes.bfloat16).astype(np.float64), axis, -1)
    blocks = v.reshape(v.shape[:-1] + (-1, 32))
    amax = np.abs(blocks).max(-1, keepdims=True)
    byte = np.maximum(np.where(amax > 0, np.frexp(amax)[1] - 1 + 127, 0) - down, 1)
    scale = np.exp2(byte - 127.0)
    codes = (blocks / scale).astype(np.float32).astype(dtype).astype(np.float64)
    return np.moveaxis((codes * scale).reshape(v.shape), -1, axis)


WIDE = False


def mx_kscale(k):
    if not WIDE:
        return np.ones(k)
    levels = np.array([24, -24, 12, -12, 0])
    if k % 512:
        return np.exp2(np.random.permutation(np.resize(levels, k // 32))).repeat(32)
    a = np.empty((k // 512, 16))
    for p in range(k // 512):
        a[p, :8] = np.random.permutation(np.resize(levels, 8))
        for g in range(8):
            far = levels[np.abs(levels - a[p, g]) >= 10]
            a[p, g + 8] = far[np.random.randint(len(far))]
    return np.exp2(a.ravel()).repeat(32)


def f64(x):
    return np.asarray(x).astype(np.float64)


def striped8(idx):
    return np.concatenate([v.reshape(-1, 16).T for v in idx]).astype(np.uint16)


def unstriped8(offs):
    return np.stack([offs[16 * g:16 * g + 16].T.reshape(-1) for g in range(8)]).astype(np.int64)


E2M1 = np.array([0.0, 0.5, 1.0, 1.5, 2.0, 3.0, 4.0, 6.0, -0.0, -0.5, -1.0, -1.5, -2.0, -3.0, -4.0, -6.0])


def pack_weight(w, fmt):
    k, n = w.shape
    w = f64(np.asarray(w, np.float32).astype(ml_dtypes.bfloat16)).reshape(k // 32, 32, n)
    amax = np.abs(w).max(1)
    if fmt == "e4m3":
        byte = np.frexp(amax)[1] - 1 + 127 - 7
    else:
        mant, ex = np.frexp(amax / 6.0)
        byte = np.where(mant > 0.5, ex, ex - 1) + 127
    byte = np.clip(np.where(amax > 0, byte, 1), 1, 254)
    scaled = (w * np.exp2(127.0 - byte)[:, None, :]).reshape(k, n).astype(np.float32)
    by_word = np.ascontiguousarray(scaled.reshape(k // 512, 128, 4, n).transpose(0, 1, 3, 2))
    if fmt == "e4m3":
        words = by_word.astype(ml_dtypes.float8_e4m3fn).view(np.uint8)
    else:
        c = by_word.astype(ml_dtypes.float4_e2m1fn).view(np.uint8) & 0xF
        words = (c[..., 0::2] | (c[..., 1::2] << 4)).reshape(k // 512, 128, 2 * n)
    return np.ascontiguousarray(words), np.ascontiguousarray(byte.astype(np.uint8).reshape(k // 512, 16, n))


def unpack_weight(words, scales, fmt):
    g, _, n = scales.shape
    words = np.ascontiguousarray(words).reshape(g, 128, n, -1)
    if fmt == "e4m3":
        vals = words.view(ml_dtypes.float8_e4m3fn).astype(np.float64)
    else:
        nib = np.empty((g, 128, n, 4), np.uint8)
        nib[..., 0::2] = words & 0xF
        nib[..., 1::2] = words >> 4
        vals = E2M1[nib]
    vals = vals * np.repeat(np.exp2(scales.astype(np.float64) - 127.0), 8, axis=1)[..., None]
    return vals.transpose(0, 1, 3, 2).reshape(g * 512, n)


def silu(f):
    return f / (1.0 + np.exp(-np.maximum(f, -700.0)))


K, L, N, T, J = 1024, 512, 512, 2048, 1024


def setup_inputs():
    n = np.random.standard_normal
    s = mx_kscale(K)[:, None]
    s2 = mx_kscale(L)[:, None]
    p_wt4 = pack_weight(n((K, N)) / np.sqrt(K) / s, "e2m1")
    p_wx = pack_weight(n((L, N)) / np.sqrt(L) / s2, "e4m3")
    return {
        "xT": (n((K, T)) * s).astype(np.float32),
        "wgt": np.repeat(np.random.uniform(0.5, 2.0, (8, J)), 16, axis=0).astype(np.float32),
        "wt4_words": p_wt4[0],
        "wt4_scales": p_wt4[1],
        "wtd": (0.4 * (n((K, N)) / np.sqrt(K) / s)).astype(np.float32),
        "c": (n((L, J)) * s2).astype(np.float32),
        "wx_words": p_wx[0],
        "wx_scales": p_wx[1],
        "b": (0.3 * n(N)).astype(np.float32),
        "offs": striped8(np.stack([np.random.permutation(T)[:J] for _ in range(8)])),
    }


def reference(xT, wgt, wt4_words, wt4_scales, wtd, c, wx_words, wx_scales, b, offs):
    idx = unstriped8(offs)
    rows = np.arange(K)
    xg = f64(wgt)[rows // 4 % 128] * f64(xT)[rows[:, None], idx[rows % 512 // 64]]
    xT_ = mxq(xg, 0, "e4m3")
    wt4_ = unpack_weight(wt4_words, wt4_scales, "e2m1")
    wtd_ = mxq(f64(wtd), 0, "e4m3")
    c_q_ = mxq(f64(c), 0, "e4m3")
    c_r_ = mxq(f64(c) - c_q_, 0, "e4m3")
    wx_ = unpack_weight(wx_words, wx_scales, "e4m3")
    y = wt4_.T @ xT_ + wtd_.T @ xT_ + wx_.T @ c_q_ + wx_.T @ c_r_
    return silu(y + f64(b)[:, None])

@@ -1,0 +1,257 @@
+from contextlib import ExitStack
+
+import concourse.mybir as mybir
+from concourse.masks import make_identity
+
+K, L, N, T, J = 1024, 512, 512, 2048, 1024
+FLOPS = 2 * (2 * K + 2 * L) * N * J + 2 * L * L * J
+
+F32 = mybir.dt.float32
+BF16 = mybir.dt.bfloat16
+I32 = mybir.dt.int32
+U32 = mybir.dt.uint32
+U16 = mybir.dt.uint16
+U8 = mybir.dt.uint8
+FP8X4 = mybir.dt.float8_e4m3fn_x4
+FP4X4 = mybir.dt.float4_e2m1fn_x4
+ALU = mybir.AluOpType
+ACT = mybir.ActivationFunctionType
+
+P = 128
+PACK = 4
+HALF = 512
+CHUNK = 256
+NT = 128
+
+
+def tile_list_dl_silu_kernel(
+    tc, xT, wgt, wt4_words, wt4_scales, wtd, c, wx_words, wx_scales, b, offs, out
+):
+    nc = tc.nc
+    with ExitStack() as ctx:
+        keep = ctx.enter_context(tc.tile_pool(name="keep", bufs=1))
+        ring = ctx.enter_context(tc.tile_pool(name="ring", bufs=3))
+        psum = ctx.enter_context(tc.psum_pool(name="psum", bufs=1))
+
+        offsets = keep.tile([P, J // 16], U16, name="offsets")
+        wgt_sb = keep.tile([P, J], F32, name="wgt_sb")
+        planes = [keep.tile([P, T], F32, name="plane%d" % u) for u in range(8)]
+        picked = [[keep.tile([P, PACK, HALF], F32, name="picked%d%d" % (a, h)) for h in range(2)] for a in range(2)]
+        c_raw = keep.tile([P, PACK, J], F32, name="c_raw")
+        wtd_raw = keep.tile([P, 2, PACK, N], F32, name="wtd_raw")
+        bias = keep.tile([P, N // NT], F32, name="bias")
+        wt4_codes = keep.tile([P, 2, 2 * N], U8, name="wt4_codes", align_bytes=64)
+        wx_codes = keep.tile([P, N], U32, name="wx_codes", align_bytes=64)
+        w_scales = keep.tile([P, 3, N], U8, name="w_scales", align_bytes=64)
+        wtd_codes = keep.tile([P, 2, N], U32, name="wtd_codes", align_bytes=64)
+        wtd_scales = keep.tile([P, 2, N], U8, name="wtd_scales", align_bytes=64)
+        xg_codes = keep.tile([P, 2, J], U32, name="xg_codes", align_bytes=64)
+        xg_scales = keep.tile([P, 2, J], U8, name="xg_scales", align_bytes=64)
+        cq_codes = keep.tile([P, J], U32, name="cq_codes", align_bytes=64)
+        cq_scales = keep.tile([P, J], U8, name="cq_scales", align_bytes=64)
+        cr_codes = keep.tile([P, J], U32, name="cr_codes", align_bytes=64)
+        cr_scales = keep.tile([P, J], U8, name="cr_scales", align_bytes=64)
+        eye = keep.tile([P, P], BF16, name="eye")
+        eye4 = keep.tile([P, PACK, P, PACK], BF16, name="eye4", align_bytes=64)
+        eye_codes = keep.tile([P, PACK * P], U32, name="eye_codes", align_bytes=64)
+        eye_scales = keep.tile([P, PACK * P], U8, name="eye_scales", align_bytes=64)
+        warm = keep.tile([P, 1], F32, name="warm")
+
+        x_rows = xT.rearrange("(a p i) t -> a i p t", p=P, i=PACK)
+        c_rows = c.rearrange("(p i) j -> p i j", i=PACK)
+        wtd_rows = wtd.rearrange("(a p i) n -> a p i n", p=P, i=PACK)
+
+        def quantize(codes, scales, grouped):
+            nc.vector.quantize_mx(out=codes.bitcast(FP8X4), scales=scales, in_=grouped.rearrange("p w i -> p (w i)"))
+
+        def interleave(engine, grouped, raw):
+            dst = grouped.rearrange("p (w e) i -> p w i e", e=4)
+            src = raw.rearrange("p i (w e) -> p w i e", e=4)
+            if engine == "scalar":
+                nc.scalar.copy(out=dst, in_=src)
+            else:
+                nc.vector.tensor_copy(out=dst, in_=src)
+
+        def load_x(u):
+            nc.sync.dma_start(out=planes[u][:], in_=x_rows[u // PACK, u % PACK])
+
+        def load_c(j0, j1):
+            nc.sync.dma_start(out=c_raw[:, :, j0:j1], in_=c_rows[:, :, j0:j1])
+
+        def load_wgt(h):
+            nc.sync.dma_start(out=wgt_sb[:, h * HALF : (h + 1) * HALF], in_=wgt[:, h * HALF : (h + 1) * HALF])
+
+        def load_wtd(a, g):
+            nc.sync.dma_start(out=wtd_raw[:, a, :, g * CHUNK : (g + 1) * CHUNK], in_=wtd_rows[a, :, :, g * CHUNK : (g + 1) * CHUNK])
+
+        def gather(u, h):
+            cols = slice(h * HALF, (h + 1) * HALF)
+            nc.vector.tensor_tensor(
+                out=picked[u // PACK][h][:, u % PACK, :],
+                in0=planes[u][:].indirect(offsets[:, h * HALF // 16 : (h + 1) * HALF // 16]),
+                in1=wgt_sb[:, cols],
+                op=ALU.mult,
+            )
+
+        def xg_chunk(a, q):
+            h, r = divmod(q * CHUNK, HALF)
+            cols = slice(q * CHUNK, (q + 1) * CHUNK)
+            grouped = ring.tile([P, CHUNK, PACK], BF16, name="xg_grouped", align_bytes=64)
+            interleave("scalar", grouped[:], picked[a][h][:, :, r : r + CHUNK])
+            quantize(xg_codes[:, a, cols], xg_scales[:, a, cols], grouped[:])
+
+        def wtd_chunk(a, g, engine):
+            cols = slice(g * CHUNK, (g + 1) * CHUNK)
+            grouped = ring.tile([P, CHUNK, PACK], BF16, name="wtd_grouped", align_bytes=64)
+            interleave(engine, grouped[:], wtd_raw[:, a, :, cols])
+            quantize(wtd_codes[:, a, cols], wtd_scales[:, a, cols], grouped[:])
+
+        def c_chunk(q):
+            cols = slice(q * CHUNK, (q + 1) * CHUNK)
+            grouped = ring.tile([P, CHUNK, PACK], BF16, name="c_grouped", align_bytes=64)
+            interleave("scalar", grouped[:], c_raw[:, :, cols])
+            quantize(cq_codes[:, cols], cq_scales[:, cols], grouped[:])
+            rest = ring.tile([P, CHUNK, PACK], BF16, name="rest", align_bytes=64)
+            for s in range(CHUNK // P):
+                j0 = q * CHUNK + s * P
+                sub = slice(j0, j0 + P)
+                bank = psum.tile([P, PACK, P], F32, name="bank%d" % (4 + (j0 // P) % 4))
+                for i in range(PACK):
+                    nc.tensor.matmul_mx(
+                        out=bank[:, i, :],
+                        lhsT=eye_codes[:, i * P : (i + 1) * P].bitcast(FP8X4),
+                        lhsT_scale=eye_scales[:, i * P : (i + 1) * P],
+                        rhs=cq_codes[:, sub].bitcast(FP8X4),
+                        rhs_scale=cq_scales[:, sub],
+                        start=True,
+                        stop=True,
+                    )
+                nc.vector.tensor_tensor(
+                    out=rest[:, s * P : (s + 1) * P, :].rearrange("p (w e) i -> p w i e", e=4),
+                    in0=c_raw[:, :, sub].rearrange("p i (w e) -> p w i e", e=4),
+                    in1=bank[:].rearrange("p i (w e) -> p w i e", e=4),
+                    op=ALU.subtract,
+                )
+            quantize(cr_codes[:, cols], cr_scales[:, cols], rest[:])
+
+        sums = {}
+
+        def add_pass(h, nt, kind):
+            cols = slice(h * HALF, (h + 1) * HALF)
+            ncols = slice(nt * NT, (nt + 1) * NT)
+            if kind == "cr":
+                sums[h, nt] = psum.tile([P, HALF], F32, name="bank%d" % (4 * h + nt))
+            if kind == "cr" or kind == "cq":
+                lhsT, lhsT_scale = wx_codes[:, ncols].bitcast(FP8X4), w_scales[:, 2, ncols]
+                codes, scales = (cr_codes, cr_scales) if kind == "cr" else (cq_codes, cq_scales)
+                rhs, rhs_scale = codes[:, cols], scales[:, cols]
+            else:
+                name, a = kind
+                rhs, rhs_scale = xg_codes[:, a, cols], xg_scales[:, a, cols]
+                if name == "wt4":
+                    lhsT, lhsT_scale = wt4_codes[:, a, 2 * nt * NT : 2 * (nt + 1) * NT].bitcast(FP4X4), w_scales[:, a, ncols]
+                else:
+                    lhsT, lhsT_scale = wtd_codes[:, a, ncols].bitcast(FP8X4), wtd_scales[:, a, ncols]
+            nc.tensor.matmul_mx(
+                out=sums[h, nt][:],
+                lhsT=lhsT,
+                lhsT_scale=lhsT_scale,
+                rhs=rhs.bitcast(FP8X4),
+                rhs_scale=rhs_scale,
+                start=(kind == "cr"),
+                stop=(kind == ("wtd", 1)),
+            )
+
+        def finish(h, nt):
+            result = keep.tile([P, HALF], F32, name="result%d%d" % (h, nt))
+            nc.scalar.activation(out=result[:], in_=sums[h, nt][:], func=ACT.Silu, bias=bias[:, nt : nt + 1])
+            nc.sync.dma_start(out=out[nt * NT : (nt + 1) * NT, h * HALF : (h + 1) * HALF], in_=result[:])
+
+        nc.sync.dma_start(offsets[:], offs)
+        load_c(0, CHUNK)
+        load_wgt(0)
+        load_x(0)
+        load_wgt(1)
+        load_x(1)
+        load_c(CHUNK, HALF)
+        load_x(2)
+        with nc.allow_non_contiguous_dma(reason="one bias value for each partition and output tile"):
+            nc.sync.dma_start(out=bias[:], in_=b.rearrange("(t p) -> p t", p=P))
+        nc.sync.dma_start(out=wx_codes[:].bitcast(I32), in_=wx_words[0].rearrange("p n i -> p (n i)").bitcast(I32))
+        load_x(3)
+        load_c(HALF, J)
+        nc.sync.dma_start(out=wt4_codes[:].bitcast(I32), in_=wt4_words.rearrange("a p n -> p a n").bitcast(I32))
+        for u in range(4, 8):
+            load_x(u)
+        for g in range(2):
+            for a in range(2):
+                load_wtd(a, g)
+
+        nc.vector.memset(warm[:], 0.0)
+        nc.scalar.activation(out=warm[:], in_=warm[:], func=ACT.Silu)
+        make_identity(nc, eye[:])
+        nc.vector.memset(eye4[:], 0.0)
+        nc.vector.memset(w_scales[:].bitcast(I32), 0)
+        for i in range(PACK):
+            nc.vector.tensor_copy(out=eye4[:, i, :, i], in_=eye[:])
+        quantize(eye_codes[:], eye_scales[:], eye4[:].rearrange("p t m i -> p (t m) i"))
+        for q in range(4):
+            nc.gpsimd.dma_start(
+                out=w_scales[32 * q : 32 * q + 4, 2, :].bitcast(I32), in_=wx_scales[0, 4 * q : 4 * q + 4, :].bitcast(I32)
+            )
+        for q in range(4):
+            nc.gpsimd.dma_start(
+                out=w_scales[32 * q : 32 * q + 4, 0:2, :].bitcast(I32),
+                in_=wt4_scales[:, 4 * q : 4 * q + 4, :].rearrange("a r n -> r a n").bitcast(I32),
+            )
+
+        c_chunk(0)
+        gather(0, 0)
+        gather(0, 1)
+        gather(1, 0)
+        gather(1, 1)
+        c_chunk(1)
+        gather(2, 0)
+        gather(2, 1)
+        for nt in range(4):
+            add_pass(0, nt, "cr")
+            add_pass(0, nt, "cq")
+        gather(3, 0)
+        gather(3, 1)
+        xg_chunk(0, 0)
+        xg_chunk(0, 1)
+        c_chunk(2)
+        c_chunk(3)
+        xg_chunk(0, 2)
+        xg_chunk(0, 3)
+        for nt in range(4):
+            add_pass(0, nt, ("wt4", 0))
+        for nt in range(4):
+            add_pass(1, nt, "cr")
+            add_pass(1, nt, "cq")
+            add_pass(1, nt, ("wt4", 0))
+        for h in range(2):
+            for u in range(4, 8):
+                gather(u, h)
+            xg_chunk(1, 2 * h)
+            xg_chunk(1, 2 * h + 1)
+            for nt in range(4):
+                add_pass(h, nt, ("wt4", 1))
+            if h == 0:
+                wtd_chunk(0, 0, "vector")
+                wtd_chunk(1, 0, "vector")
+                for nt in range(2):
+                    add_pass(0, nt, ("wtd", 0))
+                    add_pass(0, nt, ("wtd", 1))
+                    finish(0, nt)
+        for nt in range(2):
+            add_pass(1, nt, ("wtd", 0))
+            add_pass(1, nt, ("wtd", 1))
+            finish(1, nt)
+        wtd_chunk(0, 1, "vector")
+        wtd_chunk(1, 1, "vector")
+        for h in range(2):
+            for nt in range(2, 4):
+                add_pass(h, nt, ("wtd", 0))
+                add_pass(h, nt, ("wtd", 1))
+                finish(h, nt)

@@ -1,7 +1,6 @@
 from contextlib import ExitStack
 
 import concourse.mybir as mybir
-from concourse.masks import make_identity
 
 K, L, N, T, J = 1024, 512, 512, 2048, 1024
 FLOPS = 2 * (2 * K + 2 * L) * N * J + 2 * L * L * J
@@ -18,10 +17,17 @@ ALU = mybir.AluOpType
 ACT = mybir.ActivationFunctionType
 
 P = 128
+QUAD = 32
 PACK = 4
+LIST_ROWS = 16
 HALF = 512
-CHUNK = 256
-NT = 128
+QUARTER = 256
+N_TILES = N // P
+WX_SCALES = 2
+
+C_PIECES = ((0, QUARTER), (QUARTER, QUARTER), (HALF, HALF))
+PICKS = ((0, 0, HALF), (0, HALF, HALF), (1, 0, HALF), (1, HALF, QUARTER), (1, HALF + QUARTER, QUARTER))
+HELD_BACK = ((5, HALF), (6, HALF), (6, HALF + QUARTER))
 
 
 def tile_list_dl_silu_kernel(
@@ -30,16 +36,23 @@ def tile_list_dl_silu_kernel(
     nc = tc.nc
     with ExitStack() as ctx:
         keep = ctx.enter_context(tc.tile_pool(name="keep", bufs=1))
-        ring = ctx.enter_context(tc.tile_pool(name="ring", bufs=3))
         psum = ctx.enter_context(tc.psum_pool(name="psum", bufs=1))
 
-        offsets = keep.tile([P, J // 16], U16, name="offsets")
+        offsets = keep.tile([P, J // LIST_ROWS], U16, name="offsets")
         wgt_sb = keep.tile([P, J], F32, name="wgt_sb")
-        planes = [keep.tile([P, T], F32, name="plane%d" % u) for u in range(8)]
-        picked = [[keep.tile([P, PACK, HALF], F32, name="picked%d%d" % (a, h)) for h in range(2)] for a in range(2)]
-        c_raw = keep.tile([P, PACK, J], F32, name="c_raw")
-        wtd_raw = keep.tile([P, 2, PACK, N], F32, name="wtd_raw")
-        bias = keep.tile([P, N // NT], F32, name="bias")
+        planes = [keep.tile([P, T], F32, name="plane%d" % u) for u in range(2 * PACK)]
+        picked = {(a, j0): keep.tile([P, PACK, width], F32, name="picked%d_%d" % (a, j0)) for a, j0, width in PICKS}
+        c_raw = {j0: keep.tile([P, PACK, width], F32, name="c_raw%d" % j0) for j0, width in C_PIECES}
+        c_grouped = keep.tile([P, J, PACK], BF16, name="c_grouped", align_bytes=64)
+        wtd_raw = {
+            (a, n0): keep.tile([P, PACK, QUARTER], F32, name="wtd_raw%d_%d" % (a, n0))
+            for n0 in (0, QUARTER)
+            for a in range(2)
+        }
+        wgt_late = {j0: keep.tile([P, QUARTER], F32, name="wgt_late%d" % j0) for j0 in (HALF, HALF + QUARTER)}
+        wtd_grouped = [keep.tile([P, N, PACK], BF16, name="wtd_grouped%d" % a, align_bytes=64) for a in range(2)]
+        xg_grouped = [keep.tile([P, J, PACK], BF16, name="xg_grouped%d" % a, align_bytes=64) for a in range(2)]
+        bias = keep.tile([P, N_TILES], F32, name="bias")
         wt4_codes = keep.tile([P, 2, 2 * N], U8, name="wt4_codes", align_bytes=64)
         wx_codes = keep.tile([P, N], U32, name="wx_codes", align_bytes=64)
         w_scales = keep.tile([P, 3, N], U8, name="w_scales", align_bytes=64)
@@ -51,8 +64,10 @@ def tile_list_dl_silu_kernel(
         cq_scales = keep.tile([P, J], U8, name="cq_scales", align_bytes=64)
         cr_codes = keep.tile([P, J], U32, name="cr_codes", align_bytes=64)
         cr_scales = keep.tile([P, J], U8, name="cr_scales", align_bytes=64)
-        eye = keep.tile([P, P], BF16, name="eye")
-        eye4 = keep.tile([P, PACK, P, PACK], BF16, name="eye4", align_bytes=64)
+        ones = keep.tile([P, QUAD], F32, name="ones")
+        ramp = keep.tile([P, QUAD], F32, name="ramp", align_bytes=64)
+        lane = keep.tile([P, QUAD], F32, name="lane", align_bytes=64)
+        eye = keep.tile([P, PACK * (PACK * P + 1)], BF16, name="eye", align_bytes=64)
         eye_codes = keep.tile([P, PACK * P], U32, name="eye_codes", align_bytes=64)
         eye_scales = keep.tile([P, PACK * P], U8, name="eye_scales", align_bytes=64)
         warm = keep.tile([P, 1], F32, name="warm")
@@ -61,64 +76,61 @@ def tile_list_dl_silu_kernel(
         c_rows = c.rearrange("(p i) j -> p i j", i=PACK)
         wtd_rows = wtd.rearrange("(a p i) n -> a p i n", p=P, i=PACK)
 
+        def load_planes(*us):
+            for u in us:
+                nc.sync.dma_start(out=planes[u][:], in_=x_rows[u // PACK, u % PACK])
+
+        def load_c(piece):
+            j0, width = C_PIECES[piece]
+            nc.sync.dma_start(out=c_raw[j0][:], in_=c_rows[:, :, j0 : j0 + width])
+
+        def load_wgt(j0):
+            nc.sync.dma_start(out=wgt_sb[:, j0 : j0 + HALF], in_=wgt[:, j0 : j0 + HALF])
+
+        def load_wgt_late(j0):
+            nc.sync.dma_start(out=wgt_late[j0][:], in_=wgt[:, j0 : j0 + QUARTER])
+
+        def load_wtd(a, n0):
+            nc.sync.dma_start(out=wtd_raw[a, n0][:], in_=wtd_rows[a, :, :, n0 : n0 + QUARTER])
+
+        def load_wx():
+            for q in range(P // QUAD):
+                nc.sync.dma_start(
+                    out=w_scales[QUAD * q : QUAD * q + 4, WX_SCALES, :].bitcast(I32),
+                    in_=wx_scales[0, 4 * q : 4 * q + 4, :].bitcast(I32),
+                )
+            nc.sync.dma_start(out=wx_codes[:].bitcast(I32), in_=wx_words[0].rearrange("p n i -> p (n i)").bitcast(I32))
+
+        def load_wt4():
+            for q in range(P // QUAD):
+                nc.sync.dma_start(
+                    out=w_scales[QUAD * q : QUAD * q + 4, 0:WX_SCALES, :].bitcast(I32),
+                    in_=wt4_scales[:, 4 * q : 4 * q + 4, :].rearrange("a r n -> r a n").bitcast(I32),
+                )
+            nc.sync.dma_start(out=wt4_codes[:].bitcast(I32), in_=wt4_words.rearrange("a p n -> p a n").bitcast(I32))
+
+        def by_word(ap, planar):
+            return ap.rearrange("p i (w e) -> p w i e" if planar else "p (w e) i -> p w i e", e=4)
+
+        def group_on_scalar(grouped, raw):
+            nc.scalar.copy(out=by_word(grouped, False), in_=by_word(raw, True))
+
+        def group_on_vector(grouped, raw):
+            nc.vector.tensor_copy(out=by_word(grouped, False), in_=by_word(raw, True))
+
         def quantize(codes, scales, grouped):
             nc.vector.quantize_mx(out=codes.bitcast(FP8X4), scales=scales, in_=grouped.rearrange("p w i -> p (w i)"))
 
-        def interleave(engine, grouped, raw):
-            dst = grouped.rearrange("p (w e) i -> p w i e", e=4)
-            src = raw.rearrange("p i (w e) -> p w i e", e=4)
-            if engine == "scalar":
-                nc.scalar.copy(out=dst, in_=src)
-            else:
-                nc.vector.tensor_copy(out=dst, in_=src)
-
-        def load_x(u):
-            nc.sync.dma_start(out=planes[u][:], in_=x_rows[u // PACK, u % PACK])
-
-        def load_c(j0, j1):
-            nc.sync.dma_start(out=c_raw[:, :, j0:j1], in_=c_rows[:, :, j0:j1])
-
-        def load_wgt(h):
-            nc.sync.dma_start(out=wgt_sb[:, h * HALF : (h + 1) * HALF], in_=wgt[:, h * HALF : (h + 1) * HALF])
-
-        def load_wtd(a, g):
-            nc.sync.dma_start(out=wtd_raw[:, a, :, g * CHUNK : (g + 1) * CHUNK], in_=wtd_rows[a, :, :, g * CHUNK : (g + 1) * CHUNK])
-
-        def gather(u, h):
-            cols = slice(h * HALF, (h + 1) * HALF)
-            nc.vector.tensor_tensor(
-                out=picked[u // PACK][h][:, u % PACK, :],
-                in0=planes[u][:].indirect(offsets[:, h * HALF // 16 : (h + 1) * HALF // 16]),
-                in1=wgt_sb[:, cols],
-                op=ALU.mult,
-            )
-
-        def xg_chunk(a, q):
-            h, r = divmod(q * CHUNK, HALF)
-            cols = slice(q * CHUNK, (q + 1) * CHUNK)
-            grouped = ring.tile([P, CHUNK, PACK], BF16, name="xg_grouped", align_bytes=64)
-            interleave("scalar", grouped[:], picked[a][h][:, :, r : r + CHUNK])
-            quantize(xg_codes[:, a, cols], xg_scales[:, a, cols], grouped[:])
-
-        def wtd_chunk(a, g, engine):
-            cols = slice(g * CHUNK, (g + 1) * CHUNK)
-            grouped = ring.tile([P, CHUNK, PACK], BF16, name="wtd_grouped", align_bytes=64)
-            interleave(engine, grouped[:], wtd_raw[:, a, :, cols])
-            quantize(wtd_codes[:, a, cols], wtd_scales[:, a, cols], grouped[:])
-
-        def c_chunk(q):
-            cols = slice(q * CHUNK, (q + 1) * CHUNK)
-            grouped = ring.tile([P, CHUNK, PACK], BF16, name="c_grouped", align_bytes=64)
-            interleave("scalar", grouped[:], c_raw[:, :, cols])
-            quantize(cq_codes[:, cols], cq_scales[:, cols], grouped[:])
-            rest = ring.tile([P, CHUNK, PACK], BF16, name="rest", align_bytes=64)
-            for s in range(CHUNK // P):
-                j0 = q * CHUNK + s * P
-                sub = slice(j0, j0 + P)
-                bank = psum.tile([P, PACK, P], F32, name="bank%d" % (4 + (j0 // P) % 4))
+        def two_tiers(j0, width):
+            cols = slice(j0, j0 + width)
+            group_on_scalar(c_grouped[:, cols, :], c_raw[j0][:])
+            quantize(cq_codes[:, cols], cq_scales[:, cols], c_grouped[:, cols, :])
+            for r in range(0, width, P):
+                sub = slice(j0 + r, j0 + r + P)
+                values = psum.tile([P, PACK, P], F32, name="bank%d" % (N_TILES + (j0 + r) // P % N_TILES))
                 for i in range(PACK):
                     nc.tensor.matmul_mx(
-                        out=bank[:, i, :],
+                        out=values[:, i, :],
                         lhsT=eye_codes[:, i * P : (i + 1) * P].bitcast(FP8X4),
                         lhsT_scale=eye_scales[:, i * P : (i + 1) * P],
                         rhs=cq_codes[:, sub].bitcast(FP8X4),
@@ -127,131 +139,134 @@ def tile_list_dl_silu_kernel(
                         stop=True,
                     )
                 nc.vector.tensor_tensor(
-                    out=rest[:, s * P : (s + 1) * P, :].rearrange("p (w e) i -> p w i e", e=4),
-                    in0=c_raw[:, :, sub].rearrange("p i (w e) -> p w i e", e=4),
-                    in1=bank[:].rearrange("p i (w e) -> p w i e", e=4),
+                    out=by_word(c_grouped[:, sub, :], False),
+                    in0=by_word(c_raw[j0][:, :, r : r + P], True),
+                    in1=by_word(values[:], True),
                     op=ALU.subtract,
                 )
-            quantize(cr_codes[:, cols], cr_scales[:, cols], rest[:])
+            quantize(cr_codes[:, cols], cr_scales[:, cols], c_grouped[:, cols, :])
 
-        sums = {}
-
-        def add_pass(h, nt, kind):
-            cols = slice(h * HALF, (h + 1) * HALF)
-            ncols = slice(nt * NT, (nt + 1) * NT)
-            if kind == "cr":
-                sums[h, nt] = psum.tile([P, HALF], F32, name="bank%d" % (4 * h + nt))
-            if kind == "cr" or kind == "cq":
-                lhsT, lhsT_scale = wx_codes[:, ncols].bitcast(FP8X4), w_scales[:, 2, ncols]
-                codes, scales = (cr_codes, cr_scales) if kind == "cr" else (cq_codes, cq_scales)
-                rhs, rhs_scale = codes[:, cols], scales[:, cols]
-            else:
-                name, a = kind
-                rhs, rhs_scale = xg_codes[:, a, cols], xg_scales[:, a, cols]
-                if name == "wt4":
-                    lhsT, lhsT_scale = wt4_codes[:, a, 2 * nt * NT : 2 * (nt + 1) * NT].bitcast(FP4X4), w_scales[:, a, ncols]
-                else:
-                    lhsT, lhsT_scale = wtd_codes[:, a, ncols].bitcast(FP8X4), wtd_scales[:, a, ncols]
-            nc.tensor.matmul_mx(
-                out=sums[h, nt][:],
-                lhsT=lhsT,
-                lhsT_scale=lhsT_scale,
-                rhs=rhs.bitcast(FP8X4),
-                rhs_scale=rhs_scale,
-                start=(kind == "cr"),
-                stop=(kind == ("wtd", 1)),
+        def gather(u, j0):
+            target = picked[u // PACK, j0][:, u % PACK, :]
+            width = target.shape[1]
+            nc.vector.tensor_tensor(
+                out=target,
+                in0=planes[u][:].indirect(offsets[:, j0 // LIST_ROWS : (j0 + width) // LIST_ROWS]),
+                in1=wgt_late[j0][:] if (u, j0) in HELD_BACK else wgt_sb[:, j0 : j0 + width],
+                op=ALU.mult,
             )
 
-        def finish(h, nt):
-            result = keep.tile([P, HALF], F32, name="result%d%d" % (h, nt))
-            nc.scalar.activation(out=result[:], in_=sums[h, nt][:], func=ACT.Silu, bias=bias[:, nt : nt + 1])
-            nc.sync.dma_start(out=out[nt * NT : (nt + 1) * NT, h * HALF : (h + 1) * HALF], in_=result[:])
+        def quantize_xg(a, j0, width):
+            cols = slice(j0, j0 + width)
+            quantize(xg_codes[:, a, cols], xg_scales[:, a, cols], xg_grouped[a][:, cols, :])
+
+        def quantize_wtd(a, n0):
+            cols = slice(n0, n0 + QUARTER)
+            group_on_scalar(wtd_grouped[a][:, cols, :], wtd_raw[a, n0][:])
+            quantize(wtd_codes[:, a, cols], wtd_scales[:, a, cols], wtd_grouped[a][:, cols, :])
+
+        def wx_tile(t):
+            return wx_codes[:, t * P : (t + 1) * P].bitcast(FP8X4), w_scales[:, WX_SCALES, t * P : (t + 1) * P]
+
+        def wtd_tile(a, t):
+            return wtd_codes[:, a, t * P : (t + 1) * P].bitcast(FP8X4), wtd_scales[:, a, t * P : (t + 1) * P]
+
+        def wt4_tile(a, t):
+            return wt4_codes[:, a, 2 * t * P : 2 * (t + 1) * P].bitcast(FP4X4), w_scales[:, a, t * P : (t + 1) * P]
+
+        def add_pass(acc, stationary, codes, scales, start=False, stop=False):
+            nc.tensor.matmul_mx(
+                out=acc[:],
+                lhsT=stationary[0],
+                lhsT_scale=stationary[1],
+                rhs=codes.bitcast(FP8X4),
+                rhs_scale=scales,
+                start=start,
+                stop=stop,
+            )
+
+        nc.vector.memset(ones[:], 1.0)
+        nc.vector.memset(w_scales[:].bitcast(I32), 0)
+        nc.vector.memset(eye[:].bitcast(I32), 0)
 
         nc.sync.dma_start(offsets[:], offs)
-        load_c(0, CHUNK)
+        load_c(0)
+        load_c(1)
+        load_wgt(HALF)
+        load_planes(0, 1, 2)
         load_wgt(0)
-        load_x(0)
-        load_wgt(1)
-        load_x(1)
-        load_c(CHUNK, HALF)
-        load_x(2)
+        load_c(2)
+        load_planes(3, 4, 5)
+        load_wx()
+        load_wtd(1, 0)
+        load_planes(6)
+        load_wtd(0, 0)
+        load_wtd(0, QUARTER)
+        load_planes(7)
+        load_wt4()
+        load_wtd(1, QUARTER)
+        load_wgt_late(HALF + QUARTER)
+        load_wgt_late(HALF)
         with nc.allow_non_contiguous_dma(reason="one bias value for each partition and output tile"):
             nc.sync.dma_start(out=bias[:], in_=b.rearrange("(t p) -> p t", p=P))
-        nc.sync.dma_start(out=wx_codes[:].bitcast(I32), in_=wx_words[0].rearrange("p n i -> p (n i)").bitcast(I32))
-        load_x(3)
-        load_c(HALF, J)
-        nc.sync.dma_start(out=wt4_codes[:].bitcast(I32), in_=wt4_words.rearrange("a p n -> p a n").bitcast(I32))
-        for u in range(4, 8):
-            load_x(u)
-        for g in range(2):
-            for a in range(2):
-                load_wtd(a, g)
 
-        nc.vector.memset(warm[:], 0.0)
-        nc.scalar.activation(out=warm[:], in_=warm[:], func=ACT.Silu)
-        make_identity(nc, eye[:])
-        nc.vector.memset(eye4[:], 0.0)
-        nc.vector.memset(w_scales[:].bitcast(I32), 0)
-        for i in range(PACK):
-            nc.vector.tensor_copy(out=eye4[:, i, :, i], in_=eye[:])
-        quantize(eye_codes[:], eye_scales[:], eye4[:].rearrange("p t m i -> p (t m) i"))
-        for q in range(4):
-            nc.gpsimd.dma_start(
-                out=w_scales[32 * q : 32 * q + 4, 2, :].bitcast(I32), in_=wx_scales[0, 4 * q : 4 * q + 4, :].bitcast(I32)
-            )
-        for q in range(4):
-            nc.gpsimd.dma_start(
-                out=w_scales[32 * q : 32 * q + 4, 0:2, :].bitcast(I32),
-                in_=wt4_scales[:, 4 * q : 4 * q + 4, :].rearrange("a r n -> r a n").bitcast(I32),
-            )
+        nc.scalar.activation(out=warm[:], in_=ones[:, 0:1], func=ACT.Silu)
 
-        c_chunk(0)
-        gather(0, 0)
-        gather(0, 1)
-        gather(1, 0)
-        gather(1, 1)
-        c_chunk(1)
-        gather(2, 0)
-        gather(2, 1)
-        for nt in range(4):
-            add_pass(0, nt, "cr")
-            add_pass(0, nt, "cq")
-        gather(3, 0)
-        gather(3, 1)
-        xg_chunk(0, 0)
-        xg_chunk(0, 1)
-        c_chunk(2)
-        c_chunk(3)
-        xg_chunk(0, 2)
-        xg_chunk(0, 3)
-        for nt in range(4):
-            add_pass(0, nt, ("wt4", 0))
-        for nt in range(4):
-            add_pass(1, nt, "cr")
-            add_pass(1, nt, "cq")
-            add_pass(1, nt, ("wt4", 0))
+        nc.vector.tensor_tensor_scan(out=ramp[:], data0=ones[:], data1=ones[:], initial=-1.0, op0=ALU.mult, op1=ALU.add)
+        nc.vector.transpose(out=lane[:], in_=ramp[:])
+        diagonal = eye[:].rearrange("p (i x) -> p i x", i=PACK)
+        for q in range(P // QUAD):
+            rows = slice(QUAD * q, QUAD * (q + 1))
+            nc.vector.tensor_tensor(
+                out=diagonal[rows, :, PACK * QUAD * q : PACK * QUAD * (q + 1) : PACK],
+                in0=lane[rows, :].unsqueeze(1).to_broadcast([QUAD, PACK, QUAD]),
+                in1=ramp[rows, :].unsqueeze(1).to_broadcast([QUAD, PACK, QUAD]),
+                op=ALU.is_equal,
+            )
+        nc.vector.quantize_mx(out=eye_codes[:].bitcast(FP8X4), scales=eye_scales[:], in_=eye[:, 0 : PACK * PACK * P])
+
+        for j0, width in C_PIECES:
+            two_tiers(j0, width)
+
+        for u in range(PACK):
+            gather(u, 0)
+            gather(u, HALF)
+        for u in range(PACK, 2 * PACK):
+            gather(u, 0)
+        for j0 in (0, HALF):
+            group_on_scalar(xg_grouped[0][:, j0 : j0 + HALF, :], picked[0, j0][:])
+            quantize_xg(0, j0, HALF)
+        group_on_scalar(xg_grouped[1][:, QUARTER:HALF, :], picked[1, 0][:, :, QUARTER:HALF])
+        group_on_vector(xg_grouped[1][:, 0:QUARTER, :], picked[1, 0][:, :, 0:QUARTER])
+        quantize_xg(1, 0, HALF)
+
+        for j0 in (HALF, HALF + QUARTER):
+            for u in range(PACK, 2 * PACK):
+                gather(u, j0)
+        for a, n0 in ((1, 0), (0, 0), (0, QUARTER), (1, QUARTER)):
+            quantize_wtd(a, n0)
+        group_on_scalar(xg_grouped[1][:, HALF + QUARTER : J, :], picked[1, HALF + QUARTER][:])
+        group_on_vector(xg_grouped[1][:, HALF : HALF + QUARTER, :], picked[1, HALF][:])
+        quantize_xg(1, HALF, QUARTER)
+        quantize_xg(1, HALF + QUARTER, QUARTER)
+
+        sums = {}
         for h in range(2):
-            for u in range(4, 8):
-                gather(u, h)
-            xg_chunk(1, 2 * h)
-            xg_chunk(1, 2 * h + 1)
-            for nt in range(4):
-                add_pass(h, nt, ("wt4", 1))
-            if h == 0:
-                wtd_chunk(0, 0, "vector")
-                wtd_chunk(1, 0, "vector")
-                for nt in range(2):
-                    add_pass(0, nt, ("wtd", 0))
-                    add_pass(0, nt, ("wtd", 1))
-                    finish(0, nt)
-        for nt in range(2):
-            add_pass(1, nt, ("wtd", 0))
-            add_pass(1, nt, ("wtd", 1))
-            finish(1, nt)
-        wtd_chunk(0, 1, "vector")
-        wtd_chunk(1, 1, "vector")
+            cols = slice(h * HALF, (h + 1) * HALF)
+            for t in range(N_TILES):
+                sums[h, t] = psum.tile([P, HALF], F32, name="bank%d" % (N_TILES * h + t))
+                add_pass(sums[h, t], wx_tile(t), cr_codes[:, cols], cr_scales[:, cols], start=True)
+            for t in range(N_TILES):
+                add_pass(sums[h, t], wx_tile(t), cq_codes[:, cols], cq_scales[:, cols])
+            for t in range(N_TILES):
+                add_pass(sums[h, t], wtd_tile(0, t), xg_codes[:, 0, cols], xg_scales[:, 0, cols])
+            for t in range(N_TILES):
+                add_pass(sums[h, t], wt4_tile(0, t), xg_codes[:, 0, cols], xg_scales[:, 0, cols])
         for h in range(2):
-            for nt in range(2, 4):
-                add_pass(h, nt, ("wtd", 0))
-                add_pass(h, nt, ("wtd", 1))
-                finish(h, nt)
+            cols = slice(h * HALF, (h + 1) * HALF)
+            for t in range(N_TILES):
+                add_pass(sums[h, t], wtd_tile(1, t), xg_codes[:, 1, cols], xg_scales[:, 1, cols])
+                add_pass(sums[h, t], wt4_tile(1, t), xg_codes[:, 1, cols], xg_scales[:, 1, cols], stop=True)
+                result = keep.tile([P, HALF], F32, name="result%d%d" % (h, t))
+                nc.scalar.activation(out=result[:], in_=sums[h, t][:], func=ACT.Silu, bias=bias[:, t : t + 1])
+                nc.sync.dma_start(out=out[t * P : (t + 1) * P, cols], in_=result[:])

@@ -21,13 +21,11 @@ QUAD = 32
 PACK = 4
 LIST_ROWS = 16
 HALF = 512
-QUARTER = 256
+BLOCK = 256
+BLOCKS = J // BLOCK
 N_TILES = N // P
 WX_SCALES = 2
-
-C_PIECES = ((0, QUARTER), (QUARTER, QUARTER), (HALF, HALF))
-PICKS = ((0, 0, HALF), (0, HALF, HALF), (1, 0, HALF), (1, HALF, QUARTER), (1, HALF + QUARTER, QUARTER))
-HELD_BACK = ((5, HALF), (6, HALF), (6, HALF + QUARTER))
+C_PIECES = ((0, 256), (256, 256), (512, 256), (768, 256))
 
 
 def tile_list_dl_silu_kernel(
@@ -40,23 +38,19 @@ def tile_list_dl_silu_kernel(
 
         offsets = keep.tile([P, J // LIST_ROWS], U16, name="offsets")
         wgt_sb = keep.tile([P, J], F32, name="wgt_sb")
-        planes = [keep.tile([P, T], F32, name="plane%d" % u) for u in range(2 * PACK)]
-        picked = {(a, j0): keep.tile([P, PACK, width], F32, name="picked%d_%d" % (a, j0)) for a, j0, width in PICKS}
+        planes = [keep.tile([P, T], F32, name="plane%d" % u, align_bytes=64) for u in range(2 * PACK)]
+        picked = [keep.tile([P, PACK, J], F32, name="picked0"), keep.tile([P, 2, J], F32, name="picked1")]
+        last_pair = {}
         c_raw = {j0: keep.tile([P, PACK, width], F32, name="c_raw%d" % j0) for j0, width in C_PIECES}
         c_grouped = keep.tile([P, J, PACK], BF16, name="c_grouped", align_bytes=64)
-        wtd_raw = {
-            (a, n0): keep.tile([P, PACK, QUARTER], F32, name="wtd_raw%d_%d" % (a, n0))
-            for n0 in (0, QUARTER)
-            for a in range(2)
-        }
-        wgt_late = {j0: keep.tile([P, QUARTER], F32, name="wgt_late%d" % j0) for j0 in (HALF, HALF + QUARTER)}
-        wtd_grouped = [keep.tile([P, N, PACK], BF16, name="wtd_grouped%d" % a, align_bytes=64) for a in range(2)]
-        xg_grouped = [keep.tile([P, J, PACK], BF16, name="xg_grouped%d" % a, align_bytes=64) for a in range(2)]
+        wtd_raw = {(a, n0): keep.tile([P, PACK, w], F32, name="wtd_raw%d_%d" % (a, n0), align_bytes=64) for a, n0, w in ((0, 0, 256), (0, 256, 256), (1, 0, 256), (1, 256, 256))}
+        wtd_grouped0 = keep.tile([P, N, PACK], BF16, name="wtd_grouped0", align_bytes=64)
+        xg_grouped = [keep.tile([P, J, PACK], BF16, name="xg_grouped%d" % a, tag="xg_grouped0" if a == 0 else "wtd_raw0_256", align_bytes=64) for a in range(2)]
         bias = keep.tile([P, N_TILES], F32, name="bias")
         wt4_codes = keep.tile([P, 2, 2 * N], U8, name="wt4_codes", align_bytes=64)
         wx_codes = keep.tile([P, N], U32, name="wx_codes", align_bytes=64)
         w_scales = keep.tile([P, 3, N], U8, name="w_scales", align_bytes=64)
-        wtd_codes = keep.tile([P, 2, N], U32, name="wtd_codes", align_bytes=64)
+        wtd_codes = [keep.tile([P, N], U32, name="wtd_codes%d" % a, tag="wtd_codes0" if a == 0 else "wtd_codes1", align_bytes=64) for a in range(2)]
         wtd_scales = keep.tile([P, 2, N], U8, name="wtd_scales", align_bytes=64)
         xg_codes = keep.tile([P, 2, J], U32, name="xg_codes", align_bytes=64)
         xg_scales = keep.tile([P, 2, J], U8, name="xg_scales", align_bytes=64)
@@ -65,9 +59,13 @@ def tile_list_dl_silu_kernel(
         cr_codes = keep.tile([P, J], U32, name="cr_codes", align_bytes=64)
         cr_scales = keep.tile([P, J], U8, name="cr_scales", align_bytes=64)
         ones = keep.tile([P, QUAD], F32, name="ones")
-        ramp = keep.tile([P, QUAD], F32, name="ramp", align_bytes=64)
+        count = keep.tile([P, QUAD], F32, name="count", align_bytes=64)
         lane = keep.tile([P, QUAD], F32, name="lane", align_bytes=64)
-        eye = keep.tile([P, PACK * (PACK * P + 1)], BF16, name="eye", align_bytes=64)
+        first_row = keep.tile([P, 1], F32, name="first_row")
+        own_column = keep.tile([P, 1], F32, name="own_column")
+        ramp = keep.tile([P, (PACK * P // QUAD + 1) * QUAD], F32, name="ramp", align_bytes=64)
+        eye = keep.tile([P, PACK, PACK * P], BF16, name="eye", align_bytes=64)
+        identity = rows_in = spread = None
         eye_codes = keep.tile([P, PACK * P], U32, name="eye_codes", align_bytes=64)
         eye_scales = keep.tile([P, PACK * P], U8, name="eye_scales", align_bytes=64)
         warm = keep.tile([P, 1], F32, name="warm")
@@ -84,30 +82,57 @@ def tile_list_dl_silu_kernel(
             j0, width = C_PIECES[piece]
             nc.sync.dma_start(out=c_raw[j0][:], in_=c_rows[:, :, j0 : j0 + width])
 
-        def load_wgt(j0):
-            nc.sync.dma_start(out=wgt_sb[:, j0 : j0 + HALF], in_=wgt[:, j0 : j0 + HALF])
-
-        def load_wgt_late(j0):
-            nc.sync.dma_start(out=wgt_late[j0][:], in_=wgt[:, j0 : j0 + QUARTER])
+        def load_wgt(j0, width):
+            nc.sync.dma_start(out=wgt_sb[:, j0 : j0 + width], in_=wgt[:, j0 : j0 + width])
 
         def load_wtd(a, n0):
-            nc.sync.dma_start(out=wtd_raw[a, n0][:], in_=wtd_rows[a, :, :, n0 : n0 + QUARTER])
+            raw = wtd_raw[a, n0]
+            nc.sync.dma_start(out=raw[:], in_=wtd_rows[a, :, :, n0 : n0 + raw.shape[2]])
 
-        def load_wx():
-            for q in range(P // QUAD):
+        def load_wx_scales(*qs):
+            for q in qs:
                 nc.sync.dma_start(
                     out=w_scales[QUAD * q : QUAD * q + 4, WX_SCALES, :].bitcast(I32),
                     in_=wx_scales[0, 4 * q : 4 * q + 4, :].bitcast(I32),
                 )
+
+        def load_wx():
             nc.sync.dma_start(out=wx_codes[:].bitcast(I32), in_=wx_words[0].rearrange("p n i -> p (n i)").bitcast(I32))
 
-        def load_wt4():
-            for q in range(P // QUAD):
+        def load_wt4_scales(*qs):
+            for q in qs:
                 nc.sync.dma_start(
                     out=w_scales[QUAD * q : QUAD * q + 4, 0:WX_SCALES, :].bitcast(I32),
                     in_=wt4_scales[:, 4 * q : 4 * q + 4, :].rearrange("a r n -> r a n").bitcast(I32),
                 )
+
+        def load_wt4():
             nc.sync.dma_start(out=wt4_codes[:].bitcast(I32), in_=wt4_words.rearrange("a p n -> p a n").bitcast(I32))
+
+        def load_bias():
+            with nc.allow_non_contiguous_dma(reason="one bias value for each partition and output tile"):
+                nc.sync.dma_start(out=bias[:], in_=b.rearrange("(t p) -> p t", p=P))
+
+        def load_rows():
+            heads = wgt.rearrange("(g q) (r s) -> q g r s", q=LIST_ROWS, s=P)[0]
+            nc.sync.dma_start(out=rows_in[0:64, :], in_=heads)
+            nc.sync.dma_start(out=rows_in[64 : 64 + N_TILES, :], in_=b.rearrange("(t p) -> t p", p=P))
+
+        def turn_rows():
+            turned = psum.tile([P, P], F32, name="bank7")
+            nc.tensor.transpose(turned[:], rows_in[:], identity[:])
+            nc.scalar.copy(
+                out=spread[:].rearrange("s r (g q) -> s r g q", q=LIST_ROWS),
+                in_=turned[:, 0:64].rearrange("s (g r) -> s r g", r=J // P).unsqueeze(3).to_broadcast([P, J // P, 8, LIST_ROWS]),
+            )
+            nc.scalar.copy(out=bias[:], in_=turned[:, 64 : 64 + N_TILES])
+
+        def spread_wgt():
+            for h in range(2):
+                back = psum.tile([P, PACK, P], F32, name="bank%d" % h)
+                for r in range(PACK):
+                    nc.tensor.transpose(back[:, r, :], spread[:, PACK * h + r, :], identity[:])
+                nc.scalar.copy(out=wgt_sb[:, h * HALF : (h + 1) * HALF], in_=back[:].rearrange("p r s -> p (r s)"))
 
         def by_word(ap, planar):
             return ap.rearrange("p i (w e) -> p w i e" if planar else "p (w e) i -> p w i e", e=4)
@@ -121,13 +146,24 @@ def tile_list_dl_silu_kernel(
         def quantize(codes, scales, grouped):
             nc.vector.quantize_mx(out=codes.bitcast(FP8X4), scales=scales, in_=grouped.rearrange("p w i -> p (w i)"))
 
-        def two_tiers(j0, width):
+        def first_tier(piece, group):
+            j0, width = C_PIECES[piece]
             cols = slice(j0, j0 + width)
-            group_on_scalar(c_grouped[:, cols, :], c_raw[j0][:])
+            group(c_grouped[:, cols, :], c_raw[j0][:])
+
+        def quantize_cq(j0, width):
+            cols = slice(j0, j0 + width)
             quantize(cq_codes[:, cols], cq_scales[:, cols], c_grouped[:, cols, :])
+
+        def quantize_cr(j0, width):
+            cols = slice(j0, j0 + width)
+            quantize(cr_codes[:, cols], cr_scales[:, cols], c_grouped[:, cols, :])
+
+        def second_tier(piece):
+            j0, width = C_PIECES[piece]
             for r in range(0, width, P):
                 sub = slice(j0 + r, j0 + r + P)
-                values = psum.tile([P, PACK, P], F32, name="bank%d" % (N_TILES + (j0 + r) // P % N_TILES))
+                values = psum.tile([P, PACK, P], F32, name="bank%d" % ((j0 + r) // P))
                 for i in range(PACK):
                     nc.tensor.matmul_mx(
                         out=values[:, i, :],
@@ -144,129 +180,205 @@ def tile_list_dl_silu_kernel(
                     in1=by_word(values[:], True),
                     op=ALU.subtract,
                 )
-            quantize(cr_codes[:, cols], cr_scales[:, cols], c_grouped[:, cols, :])
 
-        def gather(u, j0):
-            target = picked[u // PACK, j0][:, u % PACK, :]
-            width = target.shape[1]
+        def gather(u, j0, width):
             nc.vector.tensor_tensor(
-                out=target,
+                out=picked[u // PACK][:, u % PACK, j0 : j0 + width],
                 in0=planes[u][:].indirect(offsets[:, j0 // LIST_ROWS : (j0 + width) // LIST_ROWS]),
-                in1=wgt_late[j0][:] if (u, j0) in HELD_BACK else wgt_sb[:, j0 : j0 + width],
+                in1=wgt_sb[:, j0 : j0 + width],
                 op=ALU.mult,
             )
+
+        def gather_last(u, blk):
+            if blk not in last_pair:
+                last_pair[blk] = keep.tile([P, 3, BLOCK], F32, name="last_pair%d" % blk, align_bytes=64)
+            j0 = blk * BLOCK
+            nc.vector.tensor_tensor(
+                out=last_pair[blk][:, u % 2, :],
+                in0=planes[u][:].indirect(offsets[:, j0 // LIST_ROWS : (j0 + BLOCK) // LIST_ROWS]),
+                in1=wgt_sb[:, j0 : j0 + BLOCK],
+                op=ALU.mult,
+            )
+
+        def group_last(group, blk):
+            group(xg_grouped[1][:, blk * BLOCK : (blk + 1) * BLOCK, 2:PACK], last_pair[blk][:, 0:2, :])
+
+        def group_xg(group, a, j0, width, i0=0, i1=PACK):
+            cols = slice(j0, j0 + width)
+            group(xg_grouped[a][:, cols, i0:i1], picked[a][:, i0:i1, cols])
 
         def quantize_xg(a, j0, width):
             cols = slice(j0, j0 + width)
             quantize(xg_codes[:, a, cols], xg_scales[:, a, cols], xg_grouped[a][:, cols, :])
 
+        def wtd_grouped(a, n0):
+            if a == 0:
+                return wtd_grouped0[:, n0 : n0 + wtd_raw[a, n0].shape[2], :]
+            room = last_pair[2 + n0 // BLOCK][:, 1:3, :].rearrange("p s j -> p (s j)").bitcast(BF16)
+            return room.rearrange("p (n i) -> p n i", i=PACK)
+
+        def group_wtd(group, a, n0):
+            raw = wtd_raw[a, n0]
+            group(wtd_grouped(a, n0), raw[:])
+
         def quantize_wtd(a, n0):
-            cols = slice(n0, n0 + QUARTER)
-            group_on_scalar(wtd_grouped[a][:, cols, :], wtd_raw[a, n0][:])
-            quantize(wtd_codes[:, a, cols], wtd_scales[:, a, cols], wtd_grouped[a][:, cols, :])
+            cols = slice(n0, n0 + wtd_raw[a, n0].shape[2])
+            quantize(wtd_codes[a][:, cols], wtd_scales[:, a, cols], wtd_grouped(a, n0))
 
         def wx_tile(t):
             return wx_codes[:, t * P : (t + 1) * P].bitcast(FP8X4), w_scales[:, WX_SCALES, t * P : (t + 1) * P]
 
         def wtd_tile(a, t):
-            return wtd_codes[:, a, t * P : (t + 1) * P].bitcast(FP8X4), wtd_scales[:, a, t * P : (t + 1) * P]
+            return wtd_codes[a][:, t * P : (t + 1) * P].bitcast(FP8X4), wtd_scales[:, a, t * P : (t + 1) * P]
 
         def wt4_tile(a, t):
             return wt4_codes[:, a, 2 * t * P : 2 * (t + 1) * P].bitcast(FP4X4), w_scales[:, a, t * P : (t + 1) * P]
 
-        def add_pass(acc, stationary, codes, scales, start=False, stop=False):
-            nc.tensor.matmul_mx(
-                out=acc[:],
-                lhsT=stationary[0],
-                lhsT_scale=stationary[1],
-                rhs=codes.bitcast(FP8X4),
-                rhs_scale=scales,
-                start=start,
-                stop=stop,
-            )
+        sums = {}
+
+        def add_passes(blk, pair, tile_of, codes, scales, width=BLOCK, start=False, stop=False):
+            steps = [(s, r) for s in range(2) for r in range(0, BLOCK, width)]
+            for s, r in steps:
+                cols = slice(blk * BLOCK + r, blk * BLOCK + r + width)
+                stationary = tile_of(2 * pair + s)
+                nc.tensor.matmul_mx(
+                    out=sums[blk, pair][:, s, r : r + width],
+                    lhsT=stationary[0],
+                    lhsT_scale=stationary[1],
+                    rhs=codes[:, cols].bitcast(FP8X4),
+                    rhs_scale=scales[:, cols],
+                    start=start and (s, r) == steps[0],
+                    stop=stop and (s, r) == steps[-1],
+                )
+
+        def finish(blk, pair):
+            add_passes(blk, pair, lambda t: wt4_tile(1, t), xg_codes[:, 1, :], xg_scales[:, 1, :], width=P)
+            add_passes(blk, pair, lambda t: wtd_tile(1, t), xg_codes[:, 1, :], xg_scales[:, 1, :], stop=True)
+            result = keep.tile([P, 2, BLOCK], F32, name="result%d%d" % (blk, pair), tag="plane%d" % (2 * blk + pair) if 2 * blk + pair < 6 else "result%d" % pair, align_bytes=64)
+            for s in range(2):
+                t = 2 * pair + s
+                nc.scalar.activation(out=result[:, s, :], in_=sums[blk, pair][:, s, :], func=ACT.Silu, bias=bias[:, t : t + 1])
+            rows = out[2 * pair * P : 2 * (pair + 1) * P, blk * BLOCK : (blk + 1) * BLOCK]
+            nc.sync.dma_start(out=rows.rearrange("(s p) j -> p s j", p=P), in_=result[:])
 
         nc.vector.memset(ones[:], 1.0)
+
         nc.vector.memset(w_scales[:].bitcast(I32), 0)
-        nc.vector.memset(eye[:].bitcast(I32), 0)
 
         nc.sync.dma_start(offsets[:], offs)
         load_c(0)
         load_c(1)
-        load_wgt(HALF)
-        load_planes(0, 1, 2)
-        load_wgt(0)
         load_c(2)
-        load_planes(3, 4, 5)
+        load_c(3)
+        load_wgt(0, J)
+        load_planes(0)
+        load_wx_scales(0, 1, 2, 3)
         load_wx()
-        load_wtd(1, 0)
-        load_planes(6)
+        load_planes(1)
         load_wtd(0, 0)
-        load_wtd(0, QUARTER)
-        load_planes(7)
+        load_planes(2, 3)
+        load_planes(4, 5)
+        load_wtd(0, 256)
+        load_wt4_scales(0, 1, 2, 3)
         load_wt4()
-        load_wtd(1, QUARTER)
-        load_wgt_late(HALF + QUARTER)
-        load_wgt_late(HALF)
-        with nc.allow_non_contiguous_dma(reason="one bias value for each partition and output tile"):
-            nc.sync.dma_start(out=bias[:], in_=b.rearrange("(t p) -> p t", p=P))
+        load_bias()
+        load_planes(6)
+        load_planes(7)
+        load_wtd(1, 0)
+        load_wtd(1, 256)
 
         nc.scalar.activation(out=warm[:], in_=ones[:, 0:1], func=ACT.Silu)
 
-        nc.vector.tensor_tensor_scan(out=ramp[:], data0=ones[:], data1=ones[:], initial=-1.0, op0=ALU.mult, op1=ALU.add)
-        nc.vector.transpose(out=lane[:], in_=ramp[:])
-        diagonal = eye[:].rearrange("p (i x) -> p i x", i=PACK)
         for q in range(P // QUAD):
-            rows = slice(QUAD * q, QUAD * (q + 1))
-            nc.vector.tensor_tensor(
-                out=diagonal[rows, :, PACK * QUAD * q : PACK * QUAD * (q + 1) : PACK],
-                in0=lane[rows, :].unsqueeze(1).to_broadcast([QUAD, PACK, QUAD]),
-                in1=ramp[rows, :].unsqueeze(1).to_broadcast([QUAD, PACK, QUAD]),
-                op=ALU.is_equal,
+            nc.vector.memset(first_row[QUAD * q : QUAD * (q + 1), :], QUAD * q + 0.75)
+        nc.vector.tensor_tensor_scan(out=count[:], data0=ones[:], data1=ones[:], initial=-1.0, op0=ALU.mult, op1=ALU.add)
+        nc.vector.transpose(out=lane[:], in_=count[:])
+        runs = PACK * P // QUAD + 1
+        nc.vector.scalar_tensor_tensor(
+            out=ramp[:].rearrange("p (a b) -> p a b", b=QUAD),
+            in0=count[:, 0:runs].unsqueeze(2).to_broadcast([P, runs, QUAD]),
+            scalar=float(QUAD),
+            in1=count[:].unsqueeze(1).to_broadcast([P, runs, QUAD]),
+            op0=ALU.mult,
+            op1=ALU.add,
+        )
+        nc.vector.tensor_scalar(
+            out=own_column[:], in0=lane[:, 0:1], scalar1=first_row[:], scalar2=float(PACK), op0=ALU.add, op1=ALU.mult
+        )
+        for i in range(PACK):
+            s0 = PACK - 1 - i
+            nc.vector.tensor_scalar(
+                out=eye[:, i, :], in0=ramp[:, s0 : s0 + PACK * P], scalar1=own_column[:], scalar2=None, op0=ALU.is_equal
             )
-        nc.vector.quantize_mx(out=eye_codes[:].bitcast(FP8X4), scales=eye_scales[:], in_=eye[:, 0 : PACK * PACK * P])
+        nc.vector.quantize_mx(out=eye_codes[:].bitcast(FP8X4), scales=eye_scales[:], in_=eye[:].rearrange("p i x -> p (i x)"))
 
-        for j0, width in C_PIECES:
-            two_tiers(j0, width)
-
-        for u in range(PACK):
-            gather(u, 0)
-            gather(u, HALF)
-        for u in range(PACK, 2 * PACK):
-            gather(u, 0)
-        for j0 in (0, HALF):
-            group_on_scalar(xg_grouped[0][:, j0 : j0 + HALF, :], picked[0, j0][:])
-            quantize_xg(0, j0, HALF)
-        group_on_scalar(xg_grouped[1][:, QUARTER:HALF, :], picked[1, 0][:, :, QUARTER:HALF])
-        group_on_vector(xg_grouped[1][:, 0:QUARTER, :], picked[1, 0][:, :, 0:QUARTER])
-        quantize_xg(1, 0, HALF)
-
-        for j0 in (HALF, HALF + QUARTER):
-            for u in range(PACK, 2 * PACK):
-                gather(u, j0)
-        for a, n0 in ((1, 0), (0, 0), (0, QUARTER), (1, QUARTER)):
-            quantize_wtd(a, n0)
-        group_on_scalar(xg_grouped[1][:, HALF + QUARTER : J, :], picked[1, HALF + QUARTER][:])
-        group_on_vector(xg_grouped[1][:, HALF : HALF + QUARTER, :], picked[1, HALF][:])
-        quantize_xg(1, HALF, QUARTER)
-        quantize_xg(1, HALF + QUARTER, QUARTER)
-
-        sums = {}
-        for h in range(2):
-            cols = slice(h * HALF, (h + 1) * HALF)
-            for t in range(N_TILES):
-                sums[h, t] = psum.tile([P, HALF], F32, name="bank%d" % (N_TILES * h + t))
-                add_pass(sums[h, t], wx_tile(t), cr_codes[:, cols], cr_scales[:, cols], start=True)
-            for t in range(N_TILES):
-                add_pass(sums[h, t], wx_tile(t), cq_codes[:, cols], cq_scales[:, cols])
-            for t in range(N_TILES):
-                add_pass(sums[h, t], wtd_tile(0, t), xg_codes[:, 0, cols], xg_scales[:, 0, cols])
-            for t in range(N_TILES):
-                add_pass(sums[h, t], wt4_tile(0, t), xg_codes[:, 0, cols], xg_scales[:, 0, cols])
-        for h in range(2):
-            cols = slice(h * HALF, (h + 1) * HALF)
-            for t in range(N_TILES):
-                add_pass(sums[h, t], wtd_tile(1, t), xg_codes[:, 1, cols], xg_scales[:, 1, cols])
-                add_pass(sums[h, t], wt4_tile(1, t), xg_codes[:, 1, cols], xg_scales[:, 1, cols], stop=True)
-                result = keep.tile([P, HALF], F32, name="result%d%d" % (h, t))
-                nc.scalar.activation(out=result[:], in_=sums[h, t][:], func=ACT.Silu, bias=bias[:, t : t + 1])
-                nc.sync.dma_start(out=out[t * P : (t + 1) * P, cols], in_=result[:])
+        first_tier(0, group_on_scalar)
+        quantize_cq(0, 256)
+        first_tier(1, group_on_vector)
+        quantize_cq(256, 256)
+        second_tier(0)
+        first_tier(2, group_on_scalar)
+        quantize_cq(512, 256)
+        second_tier(1)
+        quantize_cr(0, 256)
+        first_tier(3, group_on_scalar)
+        quantize_cq(768, 256)
+        second_tier(2)
+        quantize_cr(256, 256)
+        second_tier(3)
+        quantize_cr(512, 256)
+        gather(0, 0, J)
+        quantize_cr(768, 256)
+        gather(1, 0, J)
+        gather(2, 0, J)
+        group_wtd(group_on_scalar, 0, 0)
+        quantize_wtd(0, 0)
+        gather(3, 0, HALF)
+        gather(3, HALF, HALF)
+        gather(4, 0, J)
+        gather(5, 0, J)
+        group_xg(group_on_scalar, 0, 0, HALF)
+        quantize_xg(0, 0, HALF)
+        group_xg(group_on_scalar, 0, HALF, HALF)
+        quantize_xg(0, HALF, HALF)
+        group_wtd(group_on_scalar, 0, 256)
+        quantize_wtd(0, 256)
+        for blk in range(BLOCKS):
+            gather_last(6, blk)
+        group_xg(group_on_scalar, 1, 0, HALF, 0, 2)
+        group_xg(group_on_scalar, 1, HALF, HALF, 0, 2)
+        for blk in range(BLOCKS):
+            for pair in range(2):
+                sums[blk, pair] = psum.tile([P, 2, BLOCK], F32, name="bank%d" % (2 * blk + pair))
+                add_passes(blk, pair, wx_tile, cr_codes, cr_scales, start=True)
+                add_passes(blk, pair, wx_tile, cq_codes, cq_scales)
+        for pair in range(2):
+            for blk in range(BLOCKS):
+                add_passes(blk, pair, lambda t: wtd_tile(0, t), xg_codes[:, 0, :], xg_scales[:, 0, :])
+        for blk in range(BLOCKS):
+            for pair in range(2):
+                add_passes(blk, pair, lambda t: wt4_tile(0, t), xg_codes[:, 0, :], xg_scales[:, 0, :], width=P)
+        gather_last(7, 0)
+        gather_last(7, 1)
+        group_last(group_on_vector, 0)
+        group_wtd(group_on_scalar, 1, 0)
+        quantize_xg(1, 0, 256)
+        quantize_wtd(1, 0)
+        group_last(group_on_vector, 1)
+        finish(0, 0)
+        quantize_xg(1, 256, 256)
+        group_wtd(group_on_scalar, 1, 256)
+        quantize_wtd(1, 256)
+        finish(1, 0)
+        finish(0, 1)
+        finish(1, 1)
+        gather_last(7, 2)
+        group_last(group_on_vector, 2)
+        quantize_xg(1, 512, 256)
+        gather_last(7, 3)
+        group_last(group_on_vector, 3)
+        quantize_xg(1, 768, 256)
+        finish(2, 0)
+        finish(2, 1)
+        finish(3, 0)
+        finish(3, 1)

@@ -25,7 +25,9 @@ BLOCK = 256
 BLOCKS = J // BLOCK
 N_TILES = N // P
 WX_SCALES = 2
-C_PIECES = ((0, 256), (256, 256), (512, 256), (768, 256))
+PE_FIRST = 512
+HOLD = {2: "wtd_last256"}
+C_PIECES = ((0, 256), (256, 256), (512, 512))
 
 
 def tile_list_dl_silu_kernel(
@@ -40,24 +42,30 @@ def tile_list_dl_silu_kernel(
         wgt_sb = keep.tile([P, J], F32, name="wgt_sb")
         planes = [keep.tile([P, T], F32, name="plane%d" % u, align_bytes=64) for u in range(2 * PACK)]
         picked = [keep.tile([P, PACK, J], F32, name="picked0"), keep.tile([P, 2, J], F32, name="picked1")]
-        last_pair = {}
+        last_pair = {blk: keep.tile([P, 1 + PACK if blk in (2, 3) else 2, BLOCK], F32, name="last_pair%d" % blk, align_bytes=64) for blk in range(BLOCKS)}
         c_raw = {j0: keep.tile([P, PACK, width], F32, name="c_raw%d" % j0) for j0, width in C_PIECES}
         c_grouped = keep.tile([P, J, PACK], BF16, name="c_grouped", align_bytes=64)
-        wtd_raw = {(a, n0): keep.tile([P, PACK, w], F32, name="wtd_raw%d_%d" % (a, n0), align_bytes=64) for a, n0, w in ((0, 0, 256), (0, 256, 256), (1, 0, 256), (1, 256, 256))}
-        wtd_grouped0 = keep.tile([P, N, PACK], BF16, name="wtd_grouped0", align_bytes=64)
-        xg_grouped = [keep.tile([P, J, PACK], BF16, name="xg_grouped%d" % a, tag="xg_grouped0" if a == 0 else "wtd_raw0_256", align_bytes=64) for a in range(2)]
+        wtd_raw = {(a, n0): keep.tile([P, PACK, w], F32, name="wtd_raw%d_%d" % (a, n0), align_bytes=64) for a, n0, w in ((0, 0, 512), (1, 0, 256), (1, 256, 256)) if a == 0 or 2 + n0 // BLOCK not in (2, 3)}
+        for blk in (2, 3):
+            wtd_raw[1, (blk - 2) * BLOCK] = last_pair[blk][:, 1 : 1 + PACK, :]
+        wtd_bf16 = [keep.tile([P, N, PACK], BF16, name="wtd_grouped0", align_bytes=64)]
+        wtd_last = {n0: keep.tile([P, BLOCK, PACK], BF16, name="wtd_last%d" % n0, align_bytes=64) for n0 in (0, BLOCK)}
+        xg_grouped = [keep.tile([P, J, PACK], BF16, name="xg_grouped%d" % a, tag="xg_grouped0" if a == 0 else "wtd_raw0_0", align_bytes=64) for a in range(2)]
         bias = keep.tile([P, N_TILES], F32, name="bias")
         wt4_codes = keep.tile([P, 2, 2 * N], U8, name="wt4_codes", align_bytes=64)
         wx_codes = keep.tile([P, N], U32, name="wx_codes", align_bytes=64)
         w_scales = keep.tile([P, 3, N], U8, name="w_scales", align_bytes=64)
         wtd_codes = [keep.tile([P, N], U32, name="wtd_codes%d" % a, tag="wtd_codes0" if a == 0 else "wtd_codes1", align_bytes=64) for a in range(2)]
         wtd_scales = keep.tile([P, 2, N], U8, name="wtd_scales", align_bytes=64)
-        xg_codes = keep.tile([P, 2, J], U32, name="xg_codes", align_bytes=64)
+        xg_codes = keep.tile([P, J], U32, name="xg_codes", align_bytes=64)
+        xg_last = {}
         xg_scales = keep.tile([P, 2, J], U8, name="xg_scales", align_bytes=64)
         cq_codes = keep.tile([P, J], U32, name="cq_codes", align_bytes=64)
         cq_scales = keep.tile([P, J], U8, name="cq_scales", align_bytes=64)
         cr_codes = keep.tile([P, J], U32, name="cr_codes", align_bytes=64)
         cr_scales = keep.tile([P, J], U8, name="cr_scales", align_bytes=64)
+        residual = keep.tile([P, J - PE_FIRST, 2], F32, name="residual", align_bytes=64)
+        cr_late = keep.tile([P, J - PE_FIRST], U32, name="cr_late", tag="plane4", align_bytes=64)
         ones = keep.tile([P, QUAD], F32, name="ones")
         count = keep.tile([P, QUAD], F32, name="count", align_bytes=64)
         lane = keep.tile([P, QUAD], F32, name="lane", align_bytes=64)
@@ -65,7 +73,8 @@ def tile_list_dl_silu_kernel(
         own_column = keep.tile([P, 1], F32, name="own_column")
         ramp = keep.tile([P, (PACK * P // QUAD + 1) * QUAD], F32, name="ramp", align_bytes=64)
         eye = keep.tile([P, PACK, PACK * P], BF16, name="eye", align_bytes=64)
-        identity = rows_in = spread = None
+        rows_in = keep.tile([P, P], F32, name="rows_in", align_bytes=64)
+        identity = keep.tile([P, P], F32, name="identity", align_bytes=64)
         eye_codes = keep.tile([P, PACK * P], U32, name="eye_codes", align_bytes=64)
         eye_scales = keep.tile([P, PACK * P], U8, name="eye_scales", align_bytes=64)
         warm = keep.tile([P, 1], F32, name="warm")
@@ -110,29 +119,12 @@ def tile_list_dl_silu_kernel(
             nc.sync.dma_start(out=wt4_codes[:].bitcast(I32), in_=wt4_words.rearrange("a p n -> p a n").bitcast(I32))
 
         def load_bias():
-            with nc.allow_non_contiguous_dma(reason="one bias value for each partition and output tile"):
-                nc.sync.dma_start(out=bias[:], in_=b.rearrange("(t p) -> p t", p=P))
+            nc.sync.dma_start(out=rows_in[0:N_TILES, :], in_=b.rearrange("(t p) -> t p", p=P))
 
-        def load_rows():
-            heads = wgt.rearrange("(g q) (r s) -> q g r s", q=LIST_ROWS, s=P)[0]
-            nc.sync.dma_start(out=rows_in[0:64, :], in_=heads)
-            nc.sync.dma_start(out=rows_in[64 : 64 + N_TILES, :], in_=b.rearrange("(t p) -> t p", p=P))
-
-        def turn_rows():
+        def turn_bias():
             turned = psum.tile([P, P], F32, name="bank7")
             nc.tensor.transpose(turned[:], rows_in[:], identity[:])
-            nc.scalar.copy(
-                out=spread[:].rearrange("s r (g q) -> s r g q", q=LIST_ROWS),
-                in_=turned[:, 0:64].rearrange("s (g r) -> s r g", r=J // P).unsqueeze(3).to_broadcast([P, J // P, 8, LIST_ROWS]),
-            )
-            nc.scalar.copy(out=bias[:], in_=turned[:, 64 : 64 + N_TILES])
-
-        def spread_wgt():
-            for h in range(2):
-                back = psum.tile([P, PACK, P], F32, name="bank%d" % h)
-                for r in range(PACK):
-                    nc.tensor.transpose(back[:, r, :], spread[:, PACK * h + r, :], identity[:])
-                nc.scalar.copy(out=wgt_sb[:, h * HALF : (h + 1) * HALF], in_=back[:].rearrange("p r s -> p (r s)"))
+            nc.scalar.copy(out=bias[:], in_=turned[:, 0:N_TILES])
 
         def by_word(ap, planar):
             return ap.rearrange("p i (w e) -> p w i e" if planar else "p (w e) i -> p w i e", e=4)
@@ -181,6 +173,40 @@ def tile_list_dl_silu_kernel(
                     op=ALU.subtract,
                 )
 
+        def second_tier_by_transposes(piece):
+            j0, width = C_PIECES[piece]
+            for r in range(0, width, P):
+                k = (j0 + r) // P
+                sub = slice(j0 + r, j0 + r + P)
+                values = psum.tile([P, PACK, P], F32, name="bank%d" % k)
+                for i in range(PACK):
+                    nc.tensor.matmul_mx(
+                        out=values[:, i, :],
+                        lhsT=eye_codes[:, i * P : (i + 1) * P].bitcast(FP8X4),
+                        lhsT_scale=eye_scales[:, i * P : (i + 1) * P],
+                        rhs=cq_codes[:, sub].bitcast(FP8X4),
+                        rhs_scale=cq_scales[:, sub],
+                        start=True,
+                        stop=True,
+                    )
+                negated = keep.tile([P, PACK, P], F32, name="negated", bufs=4, align_bytes=64)
+                nc.scalar.activation(out=negated[:], in_=values[:], func=ACT.Copy, scale=-1.0)
+                turned = psum.tile([P, PACK, P], F32, name="bank%d" % (k - 4))
+                for i in range(PACK):
+                    nc.tensor.matmul(turned[:, i, :], c_raw[j0][:, i, r : r + P], identity[:], start=True, stop=False, is_transpose=True)
+                    nc.tensor.matmul(turned[:, i, :], negated[:, i, :], identity[:], start=False, stop=True, is_transpose=True)
+                rounded = keep.tile([P, P, PACK], BF16, name="rounded", bufs=2, align_bytes=64)
+                nc.scalar.copy(out=rounded[:], in_=turned[:].rearrange("j i p -> j p i"))
+                words = rounded[:].rearrange("j p i -> j (p i)").bitcast(F32)
+                back = psum.tile([P, 2, P], F32, name="bank%d" % k)
+                for u in range(2):
+                    nc.tensor.transpose(back[:, u, :], words[:, u : 2 * P : 2], identity[:])
+                nc.scalar.copy(out=residual[:, j0 + r - PE_FIRST : j0 + r - PE_FIRST + P, :], in_=back[:].rearrange("p u j -> p j u"))
+
+        def quantize_turned():
+            grouped = residual[:].rearrange("p j u -> p (j u)").bitcast(BF16)
+            nc.vector.quantize_mx(out=cr_late[:].bitcast(FP8X4), scales=cr_scales[:, PE_FIRST:J], in_=grouped)
+
         def gather(u, j0, width):
             nc.vector.tensor_tensor(
                 out=picked[u // PACK][:, u % PACK, j0 : j0 + width],
@@ -190,8 +216,6 @@ def tile_list_dl_silu_kernel(
             )
 
         def gather_last(u, blk):
-            if blk not in last_pair:
-                last_pair[blk] = keep.tile([P, 3, BLOCK], F32, name="last_pair%d" % blk, align_bytes=64)
             j0 = blk * BLOCK
             nc.vector.tensor_tensor(
                 out=last_pair[blk][:, u % 2, :],
@@ -209,17 +233,22 @@ def tile_list_dl_silu_kernel(
 
         def quantize_xg(a, j0, width):
             cols = slice(j0, j0 + width)
-            quantize(xg_codes[:, a, cols], xg_scales[:, a, cols], xg_grouped[a][:, cols, :])
+            if a == 1:
+                blk = j0 // BLOCK
+                xg_last[blk] = keep.tile([P, BLOCK], U32, name="xg_last%d" % blk, tag=HOLD.get(blk, "xg_last%d" % blk), align_bytes=64)
+            quantize(xg_last[blk][:] if a else xg_codes[:, cols], xg_scales[:, a, cols], xg_grouped[a][:, cols, :])
 
         def wtd_grouped(a, n0):
-            if a == 0:
-                return wtd_grouped0[:, n0 : n0 + wtd_raw[a, n0].shape[2], :]
-            room = last_pair[2 + n0 // BLOCK][:, 1:3, :].rearrange("p s j -> p (s j)").bitcast(BF16)
-            return room.rearrange("p (n i) -> p n i", i=PACK)
+            return wtd_last[n0][:]
 
         def group_wtd(group, a, n0):
             raw = wtd_raw[a, n0]
             group(wtd_grouped(a, n0), raw[:])
+
+        def wtd_half(n0):
+            cols = slice(n0, n0 + BLOCK)
+            group_on_scalar(wtd_bf16[0][:, cols, :], wtd_raw[0, 0][:, :, cols])
+            quantize(wtd_codes[0][:, cols], wtd_scales[:, 0, cols], wtd_bf16[0][:, cols, :])
 
         def quantize_wtd(a, n0):
             cols = slice(n0, n0 + wtd_raw[a, n0].shape[2])
@@ -245,16 +274,16 @@ def tile_list_dl_silu_kernel(
                     out=sums[blk, pair][:, s, r : r + width],
                     lhsT=stationary[0],
                     lhsT_scale=stationary[1],
-                    rhs=codes[:, cols].bitcast(FP8X4),
+                    rhs=(cr_late[:, cols.start - PE_FIRST : cols.stop - PE_FIRST] if codes is cr_codes and cols.start >= PE_FIRST else codes[blk][:, r : r + width] if codes is xg_last else codes[:, cols]).bitcast(FP8X4),
                     rhs_scale=scales[:, cols],
                     start=start and (s, r) == steps[0],
                     stop=stop and (s, r) == steps[-1],
                 )
 
         def finish(blk, pair):
-            add_passes(blk, pair, lambda t: wt4_tile(1, t), xg_codes[:, 1, :], xg_scales[:, 1, :], width=P)
-            add_passes(blk, pair, lambda t: wtd_tile(1, t), xg_codes[:, 1, :], xg_scales[:, 1, :], stop=True)
-            result = keep.tile([P, 2, BLOCK], F32, name="result%d%d" % (blk, pair), tag="plane%d" % (2 * blk + pair) if 2 * blk + pair < 6 else "result%d" % pair, align_bytes=64)
+            add_passes(blk, pair, lambda t: wt4_tile(1, t), xg_last, xg_scales[:, 1, :], width=P)
+            add_passes(blk, pair, lambda t: wtd_tile(1, t), xg_last, xg_scales[:, 1, :], stop=True)
+            result = keep.tile([P, 2, BLOCK], F32, name="result%d%d" % (blk, pair), tag="plane%d" % (2 * blk + pair) if 2 * blk + pair < 4 else "result%d%d" % (blk, pair), align_bytes=64)
             for s in range(2):
                 t = 2 * pair + s
                 nc.scalar.activation(out=result[:, s, :], in_=sums[blk, pair][:, s, :], func=ACT.Silu, bias=bias[:, t : t + 1])
@@ -262,28 +291,31 @@ def tile_list_dl_silu_kernel(
             nc.sync.dma_start(out=rows.rearrange("(s p) j -> p s j", p=P), in_=result[:])
 
         nc.vector.memset(ones[:], 1.0)
+        nc.vector.memset(rows_in[:], 0.0)
 
         nc.vector.memset(w_scales[:].bitcast(I32), 0)
 
         nc.sync.dma_start(offsets[:], offs)
         load_c(0)
         load_c(1)
-        load_c(2)
-        load_c(3)
-        load_wgt(0, J)
-        load_planes(0)
-        load_wx_scales(0, 1, 2, 3)
-        load_wx()
-        load_planes(1)
-        load_wtd(0, 0)
-        load_planes(2, 3)
-        load_planes(4, 5)
-        load_wtd(0, 256)
-        load_wt4_scales(0, 1, 2, 3)
-        load_wt4()
         load_bias()
-        load_planes(6)
-        load_planes(7)
+        load_c(2)
+        load_wgt(0, J)
+        load_wx_scales(0)
+        load_planes(0)
+        load_wx_scales(1)
+        load_wt4_scales(0)
+        load_planes(1)
+        load_wx_scales(2)
+        load_wt4_scales(1)
+        load_planes(2)
+        load_wx_scales(3)
+        load_wx()
+        load_planes(3, 4, 5)
+        load_wtd(0, 0)
+        load_wt4_scales(2, 3)
+        load_wt4()
+        load_planes(6, 7)
         load_wtd(1, 0)
         load_wtd(1, 256)
 
@@ -311,38 +343,36 @@ def tile_list_dl_silu_kernel(
                 out=eye[:, i, :], in0=ramp[:, s0 : s0 + PACK * P], scalar1=own_column[:], scalar2=None, op0=ALU.is_equal
             )
         nc.vector.quantize_mx(out=eye_codes[:].bitcast(FP8X4), scales=eye_scales[:], in_=eye[:].rearrange("p i x -> p (i x)"))
+        nc.vector.tensor_scalar(
+            out=identity[:], in0=ramp[:, PACK - 1 : PACK - 1 + PACK * P : PACK], scalar1=own_column[:], scalar2=None, op0=ALU.is_equal
+        )
 
         first_tier(0, group_on_scalar)
         quantize_cq(0, 256)
-        first_tier(1, group_on_vector)
+        first_tier(1, group_on_scalar)
         quantize_cq(256, 256)
+        turn_bias()
         second_tier(0)
-        first_tier(2, group_on_scalar)
-        quantize_cq(512, 256)
         second_tier(1)
+        first_tier(2, group_on_scalar)
+        quantize_cq(512, 512)
         quantize_cr(0, 256)
-        first_tier(3, group_on_scalar)
-        quantize_cq(768, 256)
-        second_tier(2)
         quantize_cr(256, 256)
-        second_tier(3)
-        quantize_cr(512, 256)
         gather(0, 0, J)
-        quantize_cr(768, 256)
         gather(1, 0, J)
         gather(2, 0, J)
-        group_wtd(group_on_scalar, 0, 0)
-        quantize_wtd(0, 0)
+        second_tier_by_transposes(2)
         gather(3, 0, HALF)
         gather(3, HALF, HALF)
         gather(4, 0, J)
         gather(5, 0, J)
         group_xg(group_on_scalar, 0, 0, HALF)
         quantize_xg(0, 0, HALF)
+        quantize_turned()
         group_xg(group_on_scalar, 0, HALF, HALF)
         quantize_xg(0, HALF, HALF)
-        group_wtd(group_on_scalar, 0, 256)
-        quantize_wtd(0, 256)
+        wtd_half(0)
+        wtd_half(256)
         for blk in range(BLOCKS):
             gather_last(6, blk)
         group_xg(group_on_scalar, 1, 0, HALF, 0, 2)
@@ -354,28 +384,28 @@ def tile_list_dl_silu_kernel(
                 add_passes(blk, pair, wx_tile, cq_codes, cq_scales)
         for pair in range(2):
             for blk in range(BLOCKS):
-                add_passes(blk, pair, lambda t: wtd_tile(0, t), xg_codes[:, 0, :], xg_scales[:, 0, :])
+                add_passes(blk, pair, lambda t: wtd_tile(0, t), xg_codes, xg_scales[:, 0, :])
         for blk in range(BLOCKS):
             for pair in range(2):
-                add_passes(blk, pair, lambda t: wt4_tile(0, t), xg_codes[:, 0, :], xg_scales[:, 0, :], width=P)
+                add_passes(blk, pair, lambda t: wt4_tile(0, t), xg_codes, xg_scales[:, 0, :], width=P)
         gather_last(7, 0)
         gather_last(7, 1)
-        group_last(group_on_vector, 0)
-        group_wtd(group_on_scalar, 1, 0)
+        group_last(group_on_scalar, 0)
+        group_last(group_on_scalar, 1)
+        group_wtd(group_on_vector, 1, 0)
         quantize_xg(1, 0, 256)
         quantize_wtd(1, 0)
-        group_last(group_on_vector, 1)
         finish(0, 0)
+        gather_last(7, 2)
         quantize_xg(1, 256, 256)
+        finish(1, 0)
         group_wtd(group_on_scalar, 1, 256)
         quantize_wtd(1, 256)
-        finish(1, 0)
         finish(0, 1)
         finish(1, 1)
-        gather_last(7, 2)
         group_last(group_on_vector, 2)
-        quantize_xg(1, 512, 256)
         gather_last(7, 3)
+        quantize_xg(1, 512, 256)
         group_last(group_on_vector, 3)
         quantize_xg(1, 768, 256)
         finish(2, 0)

@@ -175,10 +175,12 @@ def tile_list_dl_silu_kernel(
 
         def second_tier_by_transposes(piece):
             j0, width = C_PIECES[piece]
-            for r in range(0, width, P):
-                k = (j0 + r) // P
+            runs = range(0, width, P)
+            negated = keep.tile([P, len(runs), PACK, P], F32, name="negated", align_bytes=64)
+            rounded = [keep.tile([P, P, PACK], BF16, name="rounded%d" % r, align_bytes=64) for r in runs]
+            for k, r in enumerate(runs):
                 sub = slice(j0 + r, j0 + r + P)
-                values = psum.tile([P, PACK, P], F32, name="bank%d" % k)
+                values = psum.tile([P, PACK, P], F32, name="bank%d" % (4 + k))
                 for i in range(PACK):
                     nc.tensor.matmul_mx(
                         out=values[:, i, :],
@@ -189,16 +191,17 @@ def tile_list_dl_silu_kernel(
                         start=True,
                         stop=True,
                     )
-                negated = keep.tile([P, PACK, P], F32, name="negated", bufs=4, align_bytes=64)
-                nc.scalar.activation(out=negated[:], in_=values[:], func=ACT.Copy, scale=-1.0)
-                turned = psum.tile([P, PACK, P], F32, name="bank%d" % (k - 4))
+                nc.scalar.activation(out=negated[:, k], in_=values[:], func=ACT.Copy, scale=-1.0)
+            for k, r in enumerate(runs):
+                turned = psum.tile([P, PACK, P], F32, name="bank%d" % k)
                 for i in range(PACK):
-                    nc.tensor.matmul(turned[:, i, :], c_raw[j0][:, i, r : r + P], identity[:], start=True, stop=False, is_transpose=True)
-                    nc.tensor.matmul(turned[:, i, :], negated[:, i, :], identity[:], start=False, stop=True, is_transpose=True)
-                rounded = keep.tile([P, P, PACK], BF16, name="rounded", bufs=2, align_bytes=64)
-                nc.scalar.copy(out=rounded[:], in_=turned[:].rearrange("j i p -> j p i"))
-                words = rounded[:].rearrange("j p i -> j (p i)").bitcast(F32)
-                back = psum.tile([P, 2, P], F32, name="bank%d" % k)
+                    nc.tensor.matmul(turned[:, i, :], c_raw[j0][:, i, r : r + P], identity[:], start=i == 0, stop=False, is_transpose=True)
+                for i in range(PACK):
+                    nc.tensor.matmul(turned[:, i, :], negated[:, k, i, :], identity[:], start=False, stop=i == PACK - 1, is_transpose=True)
+                nc.scalar.copy(out=rounded[k][:], in_=turned[:].rearrange("j i p -> j p i"))
+            for k, r in enumerate(runs):
+                words = rounded[k][:].rearrange("j p i -> j (p i)").bitcast(F32)
+                back = psum.tile([P, 2, P], F32, name="bank%d" % (4 + k))
                 for u in range(2):
                     nc.tensor.transpose(back[:, u, :], words[:, u : 2 * P : 2], identity[:])
                 nc.scalar.copy(out=residual[:, j0 + r - PE_FIRST : j0 + r - PE_FIRST + P, :], in_=back[:].rearrange("p u j -> p j u"))

@@ -20,14 +20,15 @@ P = 128
 QUAD = 32
 PACK = 4
 LIST_ROWS = 16
-HALF = 512
+HALF = J // 2
 BLOCK = 256
 BLOCKS = J // BLOCK
 N_TILES = N // P
+LAST_PLANE = 2 * PACK - 1
 WX_SCALES = 2
-PE_FIRST = 512
-HOLD = {2: "wtd_last256"}
-C_PIECES = ((0, 256), (256, 256), (512, 512))
+
+C_PIECES = ((0, BLOCK), (BLOCK, BLOCK), (HALF, HALF))
+LATE_PIECES = ((0, HALF), (HALF, BLOCK), (HALF + BLOCK, BLOCK))
 
 
 def tile_list_dl_silu_kernel(
@@ -38,46 +39,52 @@ def tile_list_dl_silu_kernel(
         keep = ctx.enter_context(tc.tile_pool(name="keep", bufs=1))
         psum = ctx.enter_context(tc.psum_pool(name="psum", bufs=1))
 
+        def sbuf(name, shape, dtype, bytes_of=None):
+            return keep.tile([P] + shape, dtype, name=name, tag=bytes_of or name, align_bytes=64)
+
+        def bank(number, shape):
+            return psum.tile([P] + shape, F32, name="bank%d" % number)
+
         offsets = keep.tile([P, J // LIST_ROWS], U16, name="offsets")
-        wgt_sb = keep.tile([P, J], F32, name="wgt_sb")
-        planes = [keep.tile([P, T], F32, name="plane%d" % u, align_bytes=64) for u in range(2 * PACK)]
-        picked = [keep.tile([P, PACK, J], F32, name="picked0"), keep.tile([P, 2, J], F32, name="picked1")]
-        last_pair = {blk: keep.tile([P, 1 + PACK if blk in (2, 3) else 2, BLOCK], F32, name="last_pair%d" % blk, align_bytes=64) for blk in range(BLOCKS)}
-        c_raw = {j0: keep.tile([P, PACK, width], F32, name="c_raw%d" % j0) for j0, width in C_PIECES}
-        c_grouped = keep.tile([P, J, PACK], BF16, name="c_grouped", align_bytes=64)
-        wtd_raw = {(a, n0): keep.tile([P, PACK, w], F32, name="wtd_raw%d_%d" % (a, n0), align_bytes=64) for a, n0, w in ((0, 0, 512), (1, 0, 256), (1, 256, 256)) if a == 0 or 2 + n0 // BLOCK not in (2, 3)}
-        for blk in (2, 3):
-            wtd_raw[1, (blk - 2) * BLOCK] = last_pair[blk][:, 1 : 1 + PACK, :]
-        wtd_bf16 = [keep.tile([P, N, PACK], BF16, name="wtd_grouped0", align_bytes=64)]
-        wtd_last = {n0: keep.tile([P, BLOCK, PACK], BF16, name="wtd_last%d" % n0, align_bytes=64) for n0 in (0, BLOCK)}
-        xg_grouped = [keep.tile([P, J, PACK], BF16, name="xg_grouped%d" % a, tag="xg_grouped0" if a == 0 else "wtd_raw0_0", align_bytes=64) for a in range(2)]
-        bias = keep.tile([P, N_TILES], F32, name="bias")
-        wt4_codes = keep.tile([P, 2, 2 * N], U8, name="wt4_codes", align_bytes=64)
-        wx_codes = keep.tile([P, N], U32, name="wx_codes", align_bytes=64)
-        w_scales = keep.tile([P, 3, N], U8, name="w_scales", align_bytes=64)
-        wtd_codes = [keep.tile([P, N], U32, name="wtd_codes%d" % a, tag="wtd_codes0" if a == 0 else "wtd_codes1", align_bytes=64) for a in range(2)]
-        wtd_scales = keep.tile([P, 2, N], U8, name="wtd_scales", align_bytes=64)
-        xg_codes = keep.tile([P, J], U32, name="xg_codes", align_bytes=64)
-        xg_last = {}
-        xg_scales = keep.tile([P, 2, J], U8, name="xg_scales", align_bytes=64)
-        cq_codes = keep.tile([P, J], U32, name="cq_codes", align_bytes=64)
-        cq_scales = keep.tile([P, J], U8, name="cq_scales", align_bytes=64)
-        cr_codes = keep.tile([P, J], U32, name="cr_codes", align_bytes=64)
-        cr_scales = keep.tile([P, J], U8, name="cr_scales", align_bytes=64)
-        residual = keep.tile([P, J - PE_FIRST, 2], F32, name="residual", align_bytes=64)
-        cr_late = keep.tile([P, J - PE_FIRST], U32, name="cr_late", tag="plane4", align_bytes=64)
-        ones = keep.tile([P, QUAD], F32, name="ones")
-        count = keep.tile([P, QUAD], F32, name="count", align_bytes=64)
-        lane = keep.tile([P, QUAD], F32, name="lane", align_bytes=64)
-        first_row = keep.tile([P, 1], F32, name="first_row")
-        own_column = keep.tile([P, 1], F32, name="own_column")
-        ramp = keep.tile([P, (PACK * P // QUAD + 1) * QUAD], F32, name="ramp", align_bytes=64)
-        eye = keep.tile([P, PACK, PACK * P], BF16, name="eye", align_bytes=64)
-        rows_in = keep.tile([P, P], F32, name="rows_in", align_bytes=64)
-        identity = keep.tile([P, P], F32, name="identity", align_bytes=64)
-        eye_codes = keep.tile([P, PACK * P], U32, name="eye_codes", align_bytes=64)
-        eye_scales = keep.tile([P, PACK * P], U8, name="eye_scales", align_bytes=64)
-        warm = keep.tile([P, 1], F32, name="warm")
+        wgt_sb = sbuf("wgt_sb", [J], F32)
+        planes = [sbuf("plane%d" % u, [T], F32) for u in range(2 * PACK)]
+        early_picks = sbuf("early_picks", [PACK, J], F32)
+        late_picks = {0: sbuf("late_picks0", [PACK, HALF], F32)}
+        for j0 in (HALF, HALF + BLOCK):
+            late_picks[j0] = sbuf("late_picks%d" % j0, [2 * PACK - 1, BLOCK], F32)
+        c_raw = {j0: sbuf("c_raw%d" % j0, [PACK, width], F32) for j0, width in C_PIECES}
+        c_grouped = sbuf("c_grouped", [J, PACK], BF16)
+        wtd_early = sbuf("wtd_early", [PACK, N], F32)
+        wtd_late = [late_picks[HALF + pair * BLOCK][:, PACK - 1 : 2 * PACK - 1, :] for pair in range(2)]
+        wtd_early_grouped = sbuf("wtd_early_grouped", [N, PACK], BF16)
+        wtd_late_grouped = [sbuf("wtd_late_grouped%d" % pair, [BLOCK, PACK], BF16) for pair in range(2)]
+        xg_grouped = [sbuf("xg_grouped%d" % a, [J, PACK], BF16) for a in range(2)]
+        bias = sbuf("bias", [N_TILES], F32)
+        wt4_codes = sbuf("wt4_codes", [2, 2 * N], U8)
+        wx_codes = sbuf("wx_codes", [N], U32)
+        w_scales = sbuf("w_scales", [3, N], U8)
+        wtd_codes = [sbuf("wtd_codes%d" % a, [N], U32) for a in range(2)]
+        wtd_scales = sbuf("wtd_scales", [2, N], U8)
+        xg_early_codes = sbuf("xg_early_codes", [J], U32)
+        xg_late_codes = {}
+        xg_scales = sbuf("xg_scales", [2, J], U8)
+        cq_codes = sbuf("cq_codes", [J], U32)
+        cq_scales = sbuf("cq_scales", [J], U8)
+        cr_scales = sbuf("cr_scales", [J], U8)
+        cr_codes = [sbuf("cr_codes0", [HALF], U32), sbuf("cr_codes1", [HALF], U32, bytes_of="plane4")]
+        residual_words = sbuf("residual_words", [HALF, 2], F32)
+        ones = sbuf("ones", [QUAD], F32)
+        count = sbuf("count", [QUAD], F32)
+        lane = sbuf("lane", [QUAD], F32)
+        quadrant_base = sbuf("quadrant_base", [1], F32)
+        own_column = sbuf("own_column", [1], F32)
+        ramp_runs = PACK * P // QUAD + 1
+        ramp = sbuf("ramp", [ramp_runs * QUAD], F32)
+        eye = sbuf("eye", [PACK, PACK * P], BF16)
+        bias_rows = sbuf("bias_rows", [P], F32)
+        identity = sbuf("identity", [P], F32)
+        eye_codes = sbuf("eye_codes", [PACK * P], U32)
+        eye_scales = sbuf("eye_scales", [PACK * P], U8)
 
         x_rows = xT.rearrange("(a p i) t -> a i p t", p=P, i=PACK)
         c_rows = c.rearrange("(p i) j -> p i j", i=PACK)
@@ -87,331 +94,300 @@ def tile_list_dl_silu_kernel(
             for u in us:
                 nc.sync.dma_start(out=planes[u][:], in_=x_rows[u // PACK, u % PACK])
 
-        def load_c(piece):
-            j0, width = C_PIECES[piece]
+        def load_c(j0, width):
             nc.sync.dma_start(out=c_raw[j0][:], in_=c_rows[:, :, j0 : j0 + width])
 
-        def load_wgt(j0, width):
-            nc.sync.dma_start(out=wgt_sb[:, j0 : j0 + width], in_=wgt[:, j0 : j0 + width])
+        def load_wx_scales(q):
+            nc.sync.dma_start(
+                out=w_scales[QUAD * q : QUAD * q + 4, WX_SCALES, :].bitcast(I32),
+                in_=wx_scales[0, 4 * q : 4 * q + 4, :].bitcast(I32),
+            )
 
-        def load_wtd(a, n0):
-            raw = wtd_raw[a, n0]
-            nc.sync.dma_start(out=raw[:], in_=wtd_rows[a, :, :, n0 : n0 + raw.shape[2]])
-
-        def load_wx_scales(*qs):
-            for q in qs:
-                nc.sync.dma_start(
-                    out=w_scales[QUAD * q : QUAD * q + 4, WX_SCALES, :].bitcast(I32),
-                    in_=wx_scales[0, 4 * q : 4 * q + 4, :].bitcast(I32),
-                )
-
-        def load_wx():
-            nc.sync.dma_start(out=wx_codes[:].bitcast(I32), in_=wx_words[0].rearrange("p n i -> p (n i)").bitcast(I32))
-
-        def load_wt4_scales(*qs):
-            for q in qs:
-                nc.sync.dma_start(
-                    out=w_scales[QUAD * q : QUAD * q + 4, 0:WX_SCALES, :].bitcast(I32),
-                    in_=wt4_scales[:, 4 * q : 4 * q + 4, :].rearrange("a r n -> r a n").bitcast(I32),
-                )
-
-        def load_wt4():
-            nc.sync.dma_start(out=wt4_codes[:].bitcast(I32), in_=wt4_words.rearrange("a p n -> p a n").bitcast(I32))
-
-        def load_bias():
-            nc.sync.dma_start(out=rows_in[0:N_TILES, :], in_=b.rearrange("(t p) -> t p", p=P))
-
-        def turn_bias():
-            turned = psum.tile([P, P], F32, name="bank7")
-            nc.tensor.transpose(turned[:], rows_in[:], identity[:])
-            nc.scalar.copy(out=bias[:], in_=turned[:, 0:N_TILES])
+        def load_wt4_scales(q):
+            nc.sync.dma_start(
+                out=w_scales[QUAD * q : QUAD * q + 4, 0:WX_SCALES, :].bitcast(I32),
+                in_=wt4_scales[:, 4 * q : 4 * q + 4, :].rearrange("a r n -> r a n").bitcast(I32),
+            )
 
         def by_word(ap, planar):
             return ap.rearrange("p i (w e) -> p w i e" if planar else "p (w e) i -> p w i e", e=4)
 
-        def group_on_scalar(grouped, raw):
-            nc.scalar.copy(out=by_word(grouped, False), in_=by_word(raw, True))
+        def group_on_scalar(grouped, planar):
+            nc.scalar.copy(out=by_word(grouped, False), in_=by_word(planar, True))
 
-        def group_on_vector(grouped, raw):
-            nc.vector.tensor_copy(out=by_word(grouped, False), in_=by_word(raw, True))
+        def group_on_vector(grouped, planar):
+            nc.vector.tensor_copy(out=by_word(grouped, False), in_=by_word(planar, True))
 
         def quantize(codes, scales, grouped):
             nc.vector.quantize_mx(out=codes.bitcast(FP8X4), scales=scales, in_=grouped.rearrange("p w i -> p (w i)"))
 
-        def first_tier(piece, group):
-            j0, width = C_PIECES[piece]
+        def first_tier(j0, width):
             cols = slice(j0, j0 + width)
-            group(c_grouped[:, cols, :], c_raw[j0][:])
-
-        def quantize_cq(j0, width):
-            cols = slice(j0, j0 + width)
+            group_on_scalar(c_grouped[:, cols, :], c_raw[j0][:])
             quantize(cq_codes[:, cols], cq_scales[:, cols], c_grouped[:, cols, :])
 
-        def quantize_cr(j0, width):
-            cols = slice(j0, j0 + width)
-            quantize(cr_codes[:, cols], cr_scales[:, cols], c_grouped[:, cols, :])
+        def first_tier_values(j0):
+            values = bank(j0 // P, [PACK, P])
+            for i in range(PACK):
+                nc.tensor.matmul_mx(
+                    out=values[:, i, :],
+                    lhsT=eye_codes[:, i * P : (i + 1) * P].bitcast(FP8X4),
+                    lhsT_scale=eye_scales[:, i * P : (i + 1) * P],
+                    rhs=cq_codes[:, j0 : j0 + P].bitcast(FP8X4),
+                    rhs_scale=cq_scales[:, j0 : j0 + P],
+                    start=True,
+                    stop=True,
+                )
+            return values
 
-        def second_tier(piece):
-            j0, width = C_PIECES[piece]
+        def subtract_on_vector(j0, width):
             for r in range(0, width, P):
-                sub = slice(j0 + r, j0 + r + P)
-                values = psum.tile([P, PACK, P], F32, name="bank%d" % ((j0 + r) // P))
-                for i in range(PACK):
-                    nc.tensor.matmul_mx(
-                        out=values[:, i, :],
-                        lhsT=eye_codes[:, i * P : (i + 1) * P].bitcast(FP8X4),
-                        lhsT_scale=eye_scales[:, i * P : (i + 1) * P],
-                        rhs=cq_codes[:, sub].bitcast(FP8X4),
-                        rhs_scale=cq_scales[:, sub],
-                        start=True,
-                        stop=True,
-                    )
+                values = first_tier_values(j0 + r)
                 nc.vector.tensor_tensor(
-                    out=by_word(c_grouped[:, sub, :], False),
+                    out=by_word(c_grouped[:, j0 + r : j0 + r + P, :], False),
                     in0=by_word(c_raw[j0][:, :, r : r + P], True),
                     in1=by_word(values[:], True),
                     op=ALU.subtract,
                 )
 
-        def second_tier_by_transposes(piece):
-            j0, width = C_PIECES[piece]
-            runs = range(0, width, P)
-            negated = keep.tile([P, len(runs), PACK, P], F32, name="negated", align_bytes=64)
-            rounded = [keep.tile([P, P, PACK], BF16, name="rounded%d" % r, align_bytes=64) for r in runs]
-            for k, r in enumerate(runs):
-                sub = slice(j0 + r, j0 + r + P)
-                values = psum.tile([P, PACK, P], F32, name="bank%d" % (4 + k))
-                for i in range(PACK):
-                    nc.tensor.matmul_mx(
-                        out=values[:, i, :],
-                        lhsT=eye_codes[:, i * P : (i + 1) * P].bitcast(FP8X4),
-                        lhsT_scale=eye_scales[:, i * P : (i + 1) * P],
-                        rhs=cq_codes[:, sub].bitcast(FP8X4),
-                        rhs_scale=cq_scales[:, sub],
-                        start=True,
-                        stop=True,
-                    )
-                nc.scalar.activation(out=negated[:, k], in_=values[:], func=ACT.Copy, scale=-1.0)
-            for k, r in enumerate(runs):
-                turned = psum.tile([P, PACK, P], F32, name="bank%d" % k)
-                for i in range(PACK):
-                    nc.tensor.matmul(turned[:, i, :], c_raw[j0][:, i, r : r + P], identity[:], start=i == 0, stop=False, is_transpose=True)
-                for i in range(PACK):
-                    nc.tensor.matmul(turned[:, i, :], negated[:, k, i, :], identity[:], start=False, stop=i == PACK - 1, is_transpose=True)
-                nc.scalar.copy(out=rounded[k][:], in_=turned[:].rearrange("j i p -> j p i"))
-            for k, r in enumerate(runs):
-                words = rounded[k][:].rearrange("j p i -> j (p i)").bitcast(F32)
-                back = psum.tile([P, 2, P], F32, name="bank%d" % (4 + k))
+        def subtract_by_transposes():
+            runs = range(HALF // P)
+            negated = sbuf("negated", [len(runs), PACK, P], F32)
+            rounded = [sbuf("rounded%d" % run, [P, PACK], BF16) for run in runs]
+            for run in runs:
+                values = first_tier_values(HALF + run * P)
+                nc.scalar.activation(out=negated[:, run], in_=values[:], func=ACT.Copy, scale=-1.0)
+            for run in runs:
+                turned = bank(run, [PACK, P])
+                for term, planar in enumerate((c_raw[HALF][:, :, run * P : (run + 1) * P], negated[:, run])):
+                    for i in range(PACK):
+                        nc.tensor.matmul(
+                            turned[:, i, :],
+                            planar[:, i, :],
+                            identity[:],
+                            start=(term, i) == (0, 0),
+                            stop=(term, i) == (1, PACK - 1),
+                            is_transpose=True,
+                        )
+                nc.scalar.copy(out=rounded[run][:], in_=turned[:].rearrange("j i p -> j p i"))
+            for run in runs:
+                words = rounded[run][:].rearrange("j p i -> j (p i)").bitcast(F32)
+                back = bank(HALF // P + run, [2, P])
                 for u in range(2):
                     nc.tensor.transpose(back[:, u, :], words[:, u : 2 * P : 2], identity[:])
-                nc.scalar.copy(out=residual[:, j0 + r - PE_FIRST : j0 + r - PE_FIRST + P, :], in_=back[:].rearrange("p u j -> p j u"))
+                nc.scalar.copy(
+                    out=residual_words[:, run * P : (run + 1) * P, :], in_=back[:].rearrange("p u j -> p j u")
+                )
 
-        def quantize_turned():
-            grouped = residual[:].rearrange("p j u -> p (j u)").bitcast(BF16)
-            nc.vector.quantize_mx(out=cr_late[:].bitcast(FP8X4), scales=cr_scales[:, PE_FIRST:J], in_=grouped)
+        def picks(a, j0, width):
+            if a == 0:
+                return early_picks[:, :, j0 : j0 + width]
+            first = j0 if j0 >= HALF else 0
+            return late_picks[first][:, 0:PACK, j0 - first : j0 - first + width]
 
         def gather(u, j0, width):
             nc.vector.tensor_tensor(
-                out=picked[u // PACK][:, u % PACK, j0 : j0 + width],
+                out=picks(u // PACK, j0, width)[:, u % PACK, :],
                 in0=planes[u][:].indirect(offsets[:, j0 // LIST_ROWS : (j0 + width) // LIST_ROWS]),
                 in1=wgt_sb[:, j0 : j0 + width],
                 op=ALU.mult,
             )
 
-        def gather_last(u, blk):
-            j0 = blk * BLOCK
-            nc.vector.tensor_tensor(
-                out=last_pair[blk][:, u % 2, :],
-                in0=planes[u][:].indirect(offsets[:, j0 // LIST_ROWS : (j0 + BLOCK) // LIST_ROWS]),
-                in1=wgt_sb[:, j0 : j0 + BLOCK],
-                op=ALU.mult,
-            )
+        def gather_late_plane(u):
+            for j0, width in LATE_PIECES:
+                gather(u, j0, width)
 
-        def group_last(group, blk):
-            group(xg_grouped[1][:, blk * BLOCK : (blk + 1) * BLOCK, 2:PACK], last_pair[blk][:, 0:2, :])
+        def early_xg(j0):
+            cols = slice(j0, j0 + HALF)
+            group_on_scalar(xg_grouped[0][:, cols, :], picks(0, j0, HALF))
+            quantize(xg_early_codes[:, cols], xg_scales[:, 0, cols], xg_grouped[0][:, cols, :])
 
-        def group_xg(group, a, j0, width, i0=0, i1=PACK):
-            cols = slice(j0, j0 + width)
-            group(xg_grouped[a][:, cols, i0:i1], picked[a][:, i0:i1, cols])
+        def early_wtd(pair):
+            cols = slice(pair * BLOCK, (pair + 1) * BLOCK)
+            group_on_scalar(wtd_early_grouped[:, cols, :], wtd_early[:, :, cols])
+            quantize(wtd_codes[0][:, cols], wtd_scales[:, 0, cols], wtd_early_grouped[:, cols, :])
 
-        def quantize_xg(a, j0, width):
-            cols = slice(j0, j0 + width)
-            if a == 1:
-                blk = j0 // BLOCK
-                xg_last[blk] = keep.tile([P, BLOCK], U32, name="xg_last%d" % blk, tag=HOLD.get(blk, "xg_last%d" % blk), align_bytes=64)
-            quantize(xg_last[blk][:] if a else xg_codes[:, cols], xg_scales[:, a, cols], xg_grouped[a][:, cols, :])
+        def gather_block(blk):
+            gather(LAST_PLANE, blk * BLOCK, BLOCK)
 
-        def wtd_grouped(a, n0):
-            return wtd_last[n0][:]
+        def group_block(group, blk):
+            group(xg_grouped[1][:, blk * BLOCK : (blk + 1) * BLOCK, :], picks(1, blk * BLOCK, BLOCK))
 
-        def group_wtd(group, a, n0):
-            raw = wtd_raw[a, n0]
-            group(wtd_grouped(a, n0), raw[:])
+        def quantize_block(blk, bytes_of=None):
+            cols = slice(blk * BLOCK, (blk + 1) * BLOCK)
+            xg_late_codes[blk] = sbuf("xg_late_codes%d" % blk, [BLOCK], U32, bytes_of=bytes_of)
+            quantize(xg_late_codes[blk][:], xg_scales[:, 1, cols], xg_grouped[1][:, cols, :])
 
-        def wtd_half(n0):
-            cols = slice(n0, n0 + BLOCK)
-            group_on_scalar(wtd_bf16[0][:, cols, :], wtd_raw[0, 0][:, :, cols])
-            quantize(wtd_codes[0][:, cols], wtd_scales[:, 0, cols], wtd_bf16[0][:, cols, :])
-
-        def quantize_wtd(a, n0):
-            cols = slice(n0, n0 + wtd_raw[a, n0].shape[2])
-            quantize(wtd_codes[a][:, cols], wtd_scales[:, a, cols], wtd_grouped(a, n0))
+        def quantize_late_wtd(pair):
+            cols = slice(pair * BLOCK, (pair + 1) * BLOCK)
+            quantize(wtd_codes[1][:, cols], wtd_scales[:, 1, cols], wtd_late_grouped[pair][:])
 
         def wx_tile(t):
             return wx_codes[:, t * P : (t + 1) * P].bitcast(FP8X4), w_scales[:, WX_SCALES, t * P : (t + 1) * P]
 
-        def wtd_tile(a, t):
-            return wtd_codes[a][:, t * P : (t + 1) * P].bitcast(FP8X4), wtd_scales[:, a, t * P : (t + 1) * P]
+        def wtd_tile(a):
+            return lambda t: (wtd_codes[a][:, t * P : (t + 1) * P].bitcast(FP8X4), wtd_scales[:, a, t * P : (t + 1) * P])
 
-        def wt4_tile(a, t):
-            return wt4_codes[:, a, 2 * t * P : 2 * (t + 1) * P].bitcast(FP4X4), w_scales[:, a, t * P : (t + 1) * P]
+        def wt4_tile(a):
+            return lambda t: (
+                wt4_codes[:, a, 2 * t * P : 2 * (t + 1) * P].bitcast(FP4X4),
+                w_scales[:, a, t * P : (t + 1) * P],
+            )
 
         sums = {}
 
-        def add_passes(blk, pair, tile_of, codes, scales, width=BLOCK, start=False, stop=False):
+        def add_passes(blk, pair, stationary, codes, scales, width=BLOCK, start=False, stop=False):
             steps = [(s, r) for s in range(2) for r in range(0, BLOCK, width)]
             for s, r in steps:
-                cols = slice(blk * BLOCK + r, blk * BLOCK + r + width)
-                stationary = tile_of(2 * pair + s)
+                lhs_codes, lhs_scales = stationary(2 * pair + s)
                 nc.tensor.matmul_mx(
                     out=sums[blk, pair][:, s, r : r + width],
-                    lhsT=stationary[0],
-                    lhsT_scale=stationary[1],
-                    rhs=(cr_late[:, cols.start - PE_FIRST : cols.stop - PE_FIRST] if codes is cr_codes and cols.start >= PE_FIRST else codes[blk][:, r : r + width] if codes is xg_last else codes[:, cols]).bitcast(FP8X4),
-                    rhs_scale=scales[:, cols],
+                    lhsT=lhs_codes,
+                    lhsT_scale=lhs_scales,
+                    rhs=codes[:, r : r + width].bitcast(FP8X4),
+                    rhs_scale=scales[:, blk * BLOCK + r : blk * BLOCK + r + width],
                     start=start and (s, r) == steps[0],
                     stop=stop and (s, r) == steps[-1],
                 )
 
+        def block_of(codes, blk):
+            return codes[:, blk * BLOCK : (blk + 1) * BLOCK]
+
         def finish(blk, pair):
-            add_passes(blk, pair, lambda t: wt4_tile(1, t), xg_last, xg_scales[:, 1, :], width=P)
-            add_passes(blk, pair, lambda t: wtd_tile(1, t), xg_last, xg_scales[:, 1, :], stop=True)
-            result = keep.tile([P, 2, BLOCK], F32, name="result%d%d" % (blk, pair), tag="plane%d" % (2 * blk + pair) if 2 * blk + pair < 4 else "result%d%d" % (blk, pair), align_bytes=64)
+            add_passes(blk, pair, wt4_tile(1), xg_late_codes[blk], xg_scales[:, 1, :], width=P)
+            add_passes(blk, pair, wtd_tile(1), xg_late_codes[blk], xg_scales[:, 1, :], stop=True)
+            number = 2 * blk + pair
+            result = sbuf("result%d" % number, [2, BLOCK], F32, bytes_of="plane%d" % number if number < PACK else None)
             for s in range(2):
                 t = 2 * pair + s
-                nc.scalar.activation(out=result[:, s, :], in_=sums[blk, pair][:, s, :], func=ACT.Silu, bias=bias[:, t : t + 1])
-            rows = out[2 * pair * P : 2 * (pair + 1) * P, blk * BLOCK : (blk + 1) * BLOCK]
+                nc.scalar.activation(
+                    out=result[:, s, :], in_=sums[blk, pair][:, s, :], func=ACT.Silu, bias=bias[:, t : t + 1]
+                )
+            rows = out[pair * BLOCK : (pair + 1) * BLOCK, blk * BLOCK : (blk + 1) * BLOCK]
             nc.sync.dma_start(out=rows.rearrange("(s p) j -> p s j", p=P), in_=result[:])
 
         nc.vector.memset(ones[:], 1.0)
-        nc.vector.memset(rows_in[:], 0.0)
-
+        nc.scalar.activation(out=bias_rows[:], in_=ones[:, 0:1].to_broadcast([P, P]), func=ACT.Silu, scale=0.0)
         nc.vector.memset(w_scales[:].bitcast(I32), 0)
 
         nc.sync.dma_start(offsets[:], offs)
-        load_c(0)
-        load_c(1)
-        load_bias()
-        load_c(2)
-        load_wgt(0, J)
+        for j0, width in C_PIECES:
+            load_c(j0, width)
+        nc.sync.dma_start(out=bias_rows[0:N_TILES, :], in_=b.rearrange("(t p) -> t p", p=P))
+        nc.sync.dma_start(out=wgt_sb[:], in_=wgt)
         load_wx_scales(0)
-        load_planes(0)
-        load_wx_scales(1)
-        load_wt4_scales(0)
-        load_planes(1)
-        load_wx_scales(2)
-        load_wt4_scales(1)
+        for u in range(2):
+            load_planes(u)
+            load_wx_scales(u + 1)
+            load_wt4_scales(u)
         load_planes(2)
         load_wx_scales(3)
-        load_wx()
+        nc.sync.dma_start(out=wx_codes[:].bitcast(I32), in_=wx_words[0].rearrange("p n i -> p (n i)").bitcast(I32))
         load_planes(3, 4, 5)
-        load_wtd(0, 0)
-        load_wt4_scales(2, 3)
-        load_wt4()
-        load_planes(6, 7)
-        load_wtd(1, 0)
-        load_wtd(1, 256)
-
-        nc.scalar.activation(out=warm[:], in_=ones[:, 0:1], func=ACT.Silu)
+        nc.sync.dma_start(out=wtd_early[:], in_=wtd_rows[0])
+        load_wt4_scales(2)
+        load_wt4_scales(3)
+        nc.sync.dma_start(out=wt4_codes[:].bitcast(I32), in_=wt4_words.rearrange("a p n -> p a n").bitcast(I32))
+        load_planes(6, LAST_PLANE)
+        for pair in range(2):
+            nc.sync.dma_start(out=wtd_late[pair], in_=wtd_rows[1, :, :, pair * BLOCK : (pair + 1) * BLOCK])
 
         for q in range(P // QUAD):
-            nc.vector.memset(first_row[QUAD * q : QUAD * (q + 1), :], QUAD * q + 0.75)
+            nc.vector.memset(quadrant_base[QUAD * q : QUAD * (q + 1), :], QUAD * q + 0.75)
         nc.vector.tensor_tensor_scan(out=count[:], data0=ones[:], data1=ones[:], initial=-1.0, op0=ALU.mult, op1=ALU.add)
         nc.vector.transpose(out=lane[:], in_=count[:])
-        runs = PACK * P // QUAD + 1
         nc.vector.scalar_tensor_tensor(
-            out=ramp[:].rearrange("p (a b) -> p a b", b=QUAD),
-            in0=count[:, 0:runs].unsqueeze(2).to_broadcast([P, runs, QUAD]),
+            out=ramp[:].rearrange("p (a x) -> p a x", x=QUAD),
+            in0=count[:, 0:ramp_runs].unsqueeze(2).to_broadcast([P, ramp_runs, QUAD]),
             scalar=float(QUAD),
-            in1=count[:].unsqueeze(1).to_broadcast([P, runs, QUAD]),
+            in1=count[:].unsqueeze(1).to_broadcast([P, ramp_runs, QUAD]),
             op0=ALU.mult,
             op1=ALU.add,
         )
         nc.vector.tensor_scalar(
-            out=own_column[:], in0=lane[:, 0:1], scalar1=first_row[:], scalar2=float(PACK), op0=ALU.add, op1=ALU.mult
+            out=own_column[:], in0=lane[:, 0:1], scalar1=quadrant_base[:], scalar2=float(PACK), op0=ALU.add, op1=ALU.mult
         )
         for i in range(PACK):
-            s0 = PACK - 1 - i
+            first = PACK - 1 - i
             nc.vector.tensor_scalar(
-                out=eye[:, i, :], in0=ramp[:, s0 : s0 + PACK * P], scalar1=own_column[:], scalar2=None, op0=ALU.is_equal
+                out=eye[:, i, :],
+                in0=ramp[:, first : first + PACK * P],
+                scalar1=own_column[:],
+                scalar2=None,
+                op0=ALU.is_equal,
             )
-        nc.vector.quantize_mx(out=eye_codes[:].bitcast(FP8X4), scales=eye_scales[:], in_=eye[:].rearrange("p i x -> p (i x)"))
+        nc.vector.quantize_mx(
+            out=eye_codes[:].bitcast(FP8X4), scales=eye_scales[:], in_=eye[:].rearrange("p i x -> p (i x)")
+        )
         nc.vector.tensor_scalar(
-            out=identity[:], in0=ramp[:, PACK - 1 : PACK - 1 + PACK * P : PACK], scalar1=own_column[:], scalar2=None, op0=ALU.is_equal
+            out=identity[:],
+            in0=ramp[:, PACK - 1 : PACK - 1 + PACK * P : PACK],
+            scalar1=own_column[:],
+            scalar2=None,
+            op0=ALU.is_equal,
         )
 
-        first_tier(0, group_on_scalar)
-        quantize_cq(0, 256)
-        first_tier(1, group_on_scalar)
-        quantize_cq(256, 256)
-        turn_bias()
-        second_tier(0)
-        second_tier(1)
-        first_tier(2, group_on_scalar)
-        quantize_cq(512, 512)
-        quantize_cr(0, 256)
-        quantize_cr(256, 256)
-        gather(0, 0, J)
-        gather(1, 0, J)
-        gather(2, 0, J)
-        second_tier_by_transposes(2)
+        for j0, width in C_PIECES[0:2]:
+            first_tier(j0, width)
+        bias_turned = bank(7, [P])
+        nc.tensor.transpose(bias_turned[:], bias_rows[:], identity[:])
+        nc.scalar.copy(out=bias[:], in_=bias_turned[:, 0:N_TILES])
+        for j0, width in C_PIECES[0:2]:
+            subtract_on_vector(j0, width)
+        first_tier(HALF, HALF)
+        for blk in range(2):
+            quantize(block_of(cr_codes[0], blk), block_of(cr_scales, blk), c_grouped[:, blk * BLOCK : (blk + 1) * BLOCK, :])
+
+        for u in range(3):
+            gather(u, 0, J)
+        subtract_by_transposes()
         gather(3, 0, HALF)
         gather(3, HALF, HALF)
-        gather(4, 0, J)
-        gather(5, 0, J)
-        group_xg(group_on_scalar, 0, 0, HALF)
-        quantize_xg(0, 0, HALF)
-        quantize_turned()
-        group_xg(group_on_scalar, 0, HALF, HALF)
-        quantize_xg(0, HALF, HALF)
-        wtd_half(0)
-        wtd_half(256)
-        for blk in range(BLOCKS):
-            gather_last(6, blk)
-        group_xg(group_on_scalar, 1, 0, HALF, 0, 2)
-        group_xg(group_on_scalar, 1, HALF, HALF, 0, 2)
+        gather_late_plane(4)
+        gather_late_plane(5)
+        early_xg(0)
+        nc.vector.quantize_mx(
+            out=cr_codes[1][:].bitcast(FP8X4),
+            scales=cr_scales[:, HALF:J],
+            in_=residual_words[:].rearrange("p j u -> p (j u)").bitcast(BF16),
+        )
+        early_xg(HALF)
+        early_wtd(0)
+        early_wtd(1)
+        gather_late_plane(6)
+
         for blk in range(BLOCKS):
             for pair in range(2):
-                sums[blk, pair] = psum.tile([P, 2, BLOCK], F32, name="bank%d" % (2 * blk + pair))
-                add_passes(blk, pair, wx_tile, cr_codes, cr_scales, start=True)
-                add_passes(blk, pair, wx_tile, cq_codes, cq_scales)
+                sums[blk, pair] = bank(2 * blk + pair, [2, BLOCK])
+                add_passes(blk, pair, wx_tile, block_of(cr_codes[blk // 2], blk % 2), cr_scales, start=True)
+                add_passes(blk, pair, wx_tile, block_of(cq_codes, blk), cq_scales)
         for pair in range(2):
             for blk in range(BLOCKS):
-                add_passes(blk, pair, lambda t: wtd_tile(0, t), xg_codes, xg_scales[:, 0, :])
+                add_passes(blk, pair, wtd_tile(0), block_of(xg_early_codes, blk), xg_scales[:, 0, :])
         for blk in range(BLOCKS):
             for pair in range(2):
-                add_passes(blk, pair, lambda t: wt4_tile(0, t), xg_codes, xg_scales[:, 0, :], width=P)
-        gather_last(7, 0)
-        gather_last(7, 1)
-        group_last(group_on_scalar, 0)
-        group_last(group_on_scalar, 1)
-        group_wtd(group_on_vector, 1, 0)
-        quantize_xg(1, 0, 256)
-        quantize_wtd(1, 0)
+                add_passes(blk, pair, wt4_tile(0), block_of(xg_early_codes, blk), xg_scales[:, 0, :], width=P)
+
+        gather_block(0)
+        gather_block(1)
+        group_block(group_on_vector, 0)
+        group_block(group_on_scalar, 1)
+        group_on_vector(wtd_late_grouped[0][:], wtd_late[0])
+        quantize_block(0)
+        quantize_late_wtd(0)
         finish(0, 0)
-        gather_last(7, 2)
-        quantize_xg(1, 256, 256)
+        gather_block(2)
+        quantize_block(1)
         finish(1, 0)
-        group_wtd(group_on_scalar, 1, 256)
-        quantize_wtd(1, 256)
+        group_on_scalar(wtd_late_grouped[1][:], wtd_late[1])
+        quantize_late_wtd(1)
         finish(0, 1)
         finish(1, 1)
-        group_last(group_on_vector, 2)
-        gather_last(7, 3)
-        quantize_xg(1, 512, 256)
-        group_last(group_on_vector, 3)
-        quantize_xg(1, 768, 256)
-        finish(2, 0)
-        finish(2, 1)
-        finish(3, 0)
-        finish(3, 1)
+        group_block(group_on_vector, 2)
+        gather_block(3)
+        quantize_block(2, bytes_of="wtd_late_grouped1")
+        group_block(group_on_vector, 3)
+        quantize_block(3)
+        for blk in (2, 3):
+            finish(blk, 0)
+            finish(blk, 1)

@@ -25,10 +25,11 @@ BLOCK = 256
 BLOCKS = J // BLOCK
 N_TILES = N // P
 LAST_PLANE = 2 * PACK - 1
+HEADS = P // LIST_ROWS
+HEAD_ROWS = HEADS * J // P
 WX_SCALES = 2
 
 C_PIECES = ((0, BLOCK), (BLOCK, BLOCK), (HALF, HALF))
-LATE_PIECES = ((0, HALF), (HALF, BLOCK), (HALF + BLOCK, BLOCK))
 
 
 def tile_list_dl_silu_kernel(
@@ -49,16 +50,15 @@ def tile_list_dl_silu_kernel(
         wgt_sb = sbuf("wgt_sb", [J], F32)
         planes = [sbuf("plane%d" % u, [T], F32) for u in range(2 * PACK)]
         early_picks = sbuf("early_picks", [PACK, J], F32)
-        late_picks = {0: sbuf("late_picks0", [PACK, HALF], F32)}
-        for j0 in (HALF, HALF + BLOCK):
-            late_picks[j0] = sbuf("late_picks%d" % j0, [2 * PACK - 1, BLOCK], F32)
+        middle_picks = sbuf("middle_picks", [2, J], F32)
+        late_picks = [sbuf("late_picks%d" % blk, [2 if blk < 2 else 1 + PACK, BLOCK], F32) for blk in range(BLOCKS)]
         c_raw = {j0: sbuf("c_raw%d" % j0, [PACK, width], F32) for j0, width in C_PIECES}
         c_grouped = sbuf("c_grouped", [J, PACK], BF16)
         wtd_early = sbuf("wtd_early", [PACK, N], F32)
-        wtd_late = [late_picks[HALF + pair * BLOCK][:, PACK - 1 : 2 * PACK - 1, :] for pair in range(2)]
+        wtd_late = [late_picks[2 + pair][:, 1 : 1 + PACK, :] for pair in range(2)]
         wtd_early_grouped = sbuf("wtd_early_grouped", [N, PACK], BF16)
         wtd_late_grouped = [sbuf("wtd_late_grouped%d" % pair, [BLOCK, PACK], BF16) for pair in range(2)]
-        xg_grouped = [sbuf("xg_grouped%d" % a, [J, PACK], BF16) for a in range(2)]
+        xg_grouped = [sbuf("xg_grouped0", [J, PACK], BF16), sbuf("xg_grouped1", [J, PACK], BF16, bytes_of="wtd_early")]
         bias = sbuf("bias", [N_TILES], F32)
         wt4_codes = sbuf("wt4_codes", [2, 2 * N], U8)
         wx_codes = sbuf("wx_codes", [N], U32)
@@ -81,7 +81,8 @@ def tile_list_dl_silu_kernel(
         ramp_runs = PACK * P // QUAD + 1
         ramp = sbuf("ramp", [ramp_runs * QUAD], F32)
         eye = sbuf("eye", [PACK, PACK * P], BF16)
-        bias_rows = sbuf("bias_rows", [P], F32)
+        small_rows = sbuf("small_rows", [P], F32)
+        spread = sbuf("spread", [J // P, P], F32)
         identity = sbuf("identity", [P], F32)
         eye_codes = sbuf("eye_codes", [PACK * P], U32)
         eye_scales = sbuf("eye_scales", [PACK * P], U8)
@@ -179,27 +180,24 @@ def tile_list_dl_silu_kernel(
                     out=residual_words[:, run * P : (run + 1) * P, :], in_=back[:].rearrange("p u j -> p j u")
                 )
 
-        def picks(a, j0, width):
-            if a == 0:
-                return early_picks[:, :, j0 : j0 + width]
-            first = j0 if j0 >= HALF else 0
-            return late_picks[first][:, 0:PACK, j0 - first : j0 - first + width]
+        def picks(u, j0, width):
+            if u < PACK:
+                return early_picks[:, u, j0 : j0 + width]
+            if u < PACK + 2:
+                return middle_picks[:, u - PACK, j0 : j0 + width]
+            return late_picks[j0 // BLOCK][:, u % 2, :]
 
         def gather(u, j0, width):
             nc.vector.tensor_tensor(
-                out=picks(u // PACK, j0, width)[:, u % PACK, :],
+                out=picks(u, j0, width),
                 in0=planes[u][:].indirect(offsets[:, j0 // LIST_ROWS : (j0 + width) // LIST_ROWS]),
                 in1=wgt_sb[:, j0 : j0 + width],
                 op=ALU.mult,
             )
 
-        def gather_late_plane(u):
-            for j0, width in LATE_PIECES:
-                gather(u, j0, width)
-
         def early_xg(j0):
             cols = slice(j0, j0 + HALF)
-            group_on_scalar(xg_grouped[0][:, cols, :], picks(0, j0, HALF))
+            group_on_scalar(xg_grouped[0][:, cols, :], early_picks[:, :, cols])
             quantize(xg_early_codes[:, cols], xg_scales[:, 0, cols], xg_grouped[0][:, cols, :])
 
         def early_wtd(pair):
@@ -211,7 +209,7 @@ def tile_list_dl_silu_kernel(
             gather(LAST_PLANE, blk * BLOCK, BLOCK)
 
         def group_block(group, blk):
-            group(xg_grouped[1][:, blk * BLOCK : (blk + 1) * BLOCK, :], picks(1, blk * BLOCK, BLOCK))
+            group(xg_grouped[1][:, blk * BLOCK : (blk + 1) * BLOCK, 2:PACK], late_picks[blk][:, 0:2, :])
 
         def quantize_block(blk, bytes_of=None):
             cols = slice(blk * BLOCK, (blk + 1) * BLOCK)
@@ -267,14 +265,16 @@ def tile_list_dl_silu_kernel(
             nc.sync.dma_start(out=rows.rearrange("(s p) j -> p s j", p=P), in_=result[:])
 
         nc.vector.memset(ones[:], 1.0)
-        nc.scalar.activation(out=bias_rows[:], in_=ones[:, 0:1].to_broadcast([P, P]), func=ACT.Silu, scale=0.0)
+        nc.scalar.activation(out=small_rows[:], in_=ones[:, 0:1].to_broadcast([P, P]), func=ACT.Silu, scale=0.0)
         nc.vector.memset(w_scales[:].bitcast(I32), 0)
 
         nc.sync.dma_start(offsets[:], offs)
-        for j0, width in C_PIECES:
+        for j0, width in C_PIECES[0:2]:
             load_c(j0, width)
-        nc.sync.dma_start(out=bias_rows[0:N_TILES, :], in_=b.rearrange("(t p) -> t p", p=P))
-        nc.sync.dma_start(out=wgt_sb[:], in_=wgt)
+        head_rows = wgt.rearrange("(g q) (r s) -> q g r s", q=LIST_ROWS, s=P)[0]
+        nc.sync.dma_start(out=small_rows[0:HEAD_ROWS, :], in_=head_rows)
+        nc.sync.dma_start(out=small_rows[HEAD_ROWS : HEAD_ROWS + N_TILES, :], in_=b.rearrange("(t p) -> t p", p=P))
+        load_c(HALF, HALF)
         load_wx_scales(0)
         for u in range(2):
             load_planes(u)
@@ -329,22 +329,38 @@ def tile_list_dl_silu_kernel(
 
         for j0, width in C_PIECES[0:2]:
             first_tier(j0, width)
-        bias_turned = bank(7, [P])
-        nc.tensor.transpose(bias_turned[:], bias_rows[:], identity[:])
-        nc.scalar.copy(out=bias[:], in_=bias_turned[:, 0:N_TILES])
         for j0, width in C_PIECES[0:2]:
             subtract_on_vector(j0, width)
         first_tier(HALF, HALF)
+
+        small_turned = bank(7, [P])
+        nc.tensor.transpose(small_turned[:], small_rows[:], identity[:])
+        nc.scalar.copy(out=bias[:], in_=small_turned[:, HEAD_ROWS : HEAD_ROWS + N_TILES])
+        by_run = small_turned[:, 0:HEAD_ROWS].rearrange("s (g r) -> s r g", r=J // P)
+        for h in range(2):
+            runs = slice(PACK * h, PACK * (h + 1))
+            nc.scalar.copy(
+                out=spread[:, runs, :].rearrange("s r (g q) -> s r g q", q=LIST_ROWS),
+                in_=by_run[:, runs, :].unsqueeze(3).to_broadcast([P, PACK, HEADS, LIST_ROWS]),
+            )
+        for h in range(2):
+            wgt_half = bank(2 + h, [PACK, P])
+            for r in range(PACK):
+                nc.tensor.transpose(wgt_half[:, r, :], spread[:, PACK * h + r, :], identity[:])
+            nc.scalar.copy(out=wgt_sb[:, h * HALF : (h + 1) * HALF], in_=wgt_half[:].rearrange("p r s -> p (r s)"))
+
         for blk in range(2):
             quantize(block_of(cr_codes[0], blk), block_of(cr_scales, blk), c_grouped[:, blk * BLOCK : (blk + 1) * BLOCK, :])
 
-        for u in range(3):
+        gather(0, 0, HALF)
+        gather(0, HALF, HALF)
+        for u in (1, 2):
             gather(u, 0, J)
         subtract_by_transposes()
         gather(3, 0, HALF)
         gather(3, HALF, HALF)
-        gather_late_plane(4)
-        gather_late_plane(5)
+        gather(4, 0, J)
+        gather(5, 0, J)
         early_xg(0)
         nc.vector.quantize_mx(
             out=cr_codes[1][:].bitcast(FP8X4),
@@ -354,7 +370,10 @@ def tile_list_dl_silu_kernel(
         early_xg(HALF)
         early_wtd(0)
         early_wtd(1)
-        gather_late_plane(6)
+        for blk in range(BLOCKS):
+            gather(6, blk * BLOCK, BLOCK)
+        for j0 in (0, HALF):
+            group_on_scalar(xg_grouped[1][:, j0 : j0 + HALF, 0:2], middle_picks[:, :, j0 : j0 + HALF])
 
         for blk in range(BLOCKS):
             for pair in range(2):
@@ -370,7 +389,7 @@ def tile_list_dl_silu_kernel(
 
         gather_block(0)
         gather_block(1)
-        group_block(group_on_vector, 0)
+        group_block(group_on_scalar, 0)
         group_block(group_on_scalar, 1)
         group_on_vector(wtd_late_grouped[0][:], wtd_late[0])
         quantize_block(0)

@@ -41,7 +41,7 @@ def tile_list_dl_silu_kernel(
         psum = ctx.enter_context(tc.psum_pool(name="psum", bufs=1))
 
         def sbuf(name, shape, dtype, bytes_of=None):
-            return keep.tile([P] + shape, dtype, name=name, tag=bytes_of or name, align_bytes=64)
+            return keep.tile([P] + shape, dtype, name=name, tag=bytes_of or name, align_bytes=256)
 
         def bank(number, shape):
             return psum.tile([P] + shape, F32, name="bank%d" % number)

@@ -111,7 +111,7 @@ def tile_list_dl_silu_kernel(
             )
 
         def by_word(ap, planar):
-            return ap.rearrange("p i (w e) -> p w i e" if planar else "p (w e) i -> p w i e", e=4)
+            return ap.rearrange("p i (w e) -> p w i e" if planar else "p (w e) i -> p w i e", e=2)
 
         def group_on_scalar(grouped, planar):
             nc.scalar.copy(out=by_word(grouped, False), in_=by_word(planar, True))

@@ -28,6 +28,7 @@ LAST_PLANE = 2 * PACK - 1
 HEADS = P // LIST_ROWS
 HEAD_ROWS = HEADS * J // P
 WX_SCALES = 2
+LAST_ROWS = (BLOCKS, BLOCKS + 1, BLOCKS + 2, BLOCKS + 2 + PACK)
 
 C_PIECES = ((0, BLOCK), (BLOCK, BLOCK), (HALF, HALF))
 
@@ -51,11 +52,11 @@ def tile_list_dl_silu_kernel(
         planes = [sbuf("plane%d" % u, [T], F32) for u in range(2 * PACK)]
         early_picks = sbuf("early_picks", [PACK, J], F32)
         middle_picks = sbuf("middle_picks", [2, J], F32)
-        late_picks = [sbuf("late_picks%d" % blk, [2 if blk < 2 else 1 + PACK, BLOCK], F32) for blk in range(BLOCKS)]
+        late_picks = sbuf("late_picks", [LAST_ROWS[-1] + PACK, BLOCK], F32)
         c_raw = {j0: sbuf("c_raw%d" % j0, [PACK, width], F32) for j0, width in C_PIECES}
         c_grouped = sbuf("c_grouped", [J, PACK], BF16)
         wtd_early = sbuf("wtd_early", [PACK, N], F32)
-        wtd_late = [late_picks[2 + pair][:, 1 : 1 + PACK, :] for pair in range(2)]
+        wtd_late = [late_picks[:, first : first + PACK, :] for first in LAST_ROWS[2:]]
         wtd_early_grouped = sbuf("wtd_early_grouped", [N, PACK], BF16)
         wtd_late_grouped = [sbuf("wtd_late_grouped%d" % pair, [BLOCK, PACK], BF16) for pair in range(2)]
         xg_grouped = [sbuf("xg_grouped0", [J, PACK], BF16), sbuf("xg_grouped1", [J, PACK], BF16, bytes_of="wtd_early")]
@@ -185,7 +186,9 @@ def tile_list_dl_silu_kernel(
                 return early_picks[:, u, j0 : j0 + width]
             if u < PACK + 2:
                 return middle_picks[:, u - PACK, j0 : j0 + width]
-            return late_picks[j0 // BLOCK][:, u % 2, :]
+            if u < LAST_PLANE:
+                return late_picks[:, 0:BLOCKS, :].rearrange("p r j -> p (r j)")[:, j0 : j0 + width]
+            return late_picks[:, LAST_ROWS[j0 // BLOCK], :]
 
         def gather(u, j0, width):
             nc.vector.tensor_tensor(
@@ -209,7 +212,9 @@ def tile_list_dl_silu_kernel(
             gather(LAST_PLANE, blk * BLOCK, BLOCK)
 
         def group_block(group, blk):
-            group(xg_grouped[1][:, blk * BLOCK : (blk + 1) * BLOCK, 2:PACK], late_picks[blk][:, 0:2, :])
+            last = LAST_ROWS[blk]
+            both = late_picks[:, blk : last + 1 : last - blk, :]
+            group(xg_grouped[1][:, blk * BLOCK : (blk + 1) * BLOCK, 2:PACK], both)
 
         def quantize_block(blk, bytes_of=None):
             cols = slice(blk * BLOCK, (blk + 1) * BLOCK)
@@ -370,8 +375,7 @@ def tile_list_dl_silu_kernel(
         early_xg(HALF)
         early_wtd(0)
         early_wtd(1)
-        for blk in range(BLOCKS):
-            gather(6, blk * BLOCK, BLOCK)
+        gather(6, 0, J)
         for j0 in (0, HALF):
             group_on_scalar(xg_grouped[1][:, j0 : j0 + HALF, 0:2], middle_picks[:, :, j0 : j0 + HALF])
 

@@ -30,8 +30,6 @@ HEAD_ROWS = HEADS * J // P
 WX_SCALES = 2
 LAST_ROWS = (BLOCKS, BLOCKS + 1, BLOCKS + 2, BLOCKS + 2 + PACK)
 
-C_PIECES = ((0, BLOCK), (BLOCK, BLOCK), (HALF, HALF))
-
 
 def tile_list_dl_silu_kernel(
     tc, xT, wgt, wt4_words, wt4_scales, wtd, c, wx_words, wx_scales, b, offs, out
@@ -53,8 +51,8 @@ def tile_list_dl_silu_kernel(
         early_picks = sbuf("early_picks", [PACK, J], F32)
         middle_picks = sbuf("middle_picks", [2, J], F32)
         late_picks = sbuf("late_picks", [LAST_ROWS[-1] + PACK, BLOCK], F32)
-        c_raw = {j0: sbuf("c_raw%d" % j0, [PACK, width], F32) for j0, width in C_PIECES}
-        c_grouped = sbuf("c_grouped", [J, PACK], BF16)
+        c_raw = [sbuf("c_raw%d" % (blk * BLOCK), [PACK, BLOCK], F32) for blk in range(BLOCKS)]
+        c_grouped = [sbuf("c_grouped%d" % h, [HALF, PACK], BF16) for h in range(2)]
         wtd_early = sbuf("wtd_early", [PACK, N], F32)
         wtd_late = [late_picks[:, first : first + PACK, :] for first in LAST_ROWS[2:]]
         wtd_early_grouped = sbuf("wtd_early_grouped", [N, PACK], BF16)
@@ -83,6 +81,7 @@ def tile_list_dl_silu_kernel(
         ramp = sbuf("ramp", [ramp_runs * QUAD], F32)
         eye = sbuf("eye", [PACK, PACK * P], BF16)
         small_rows = sbuf("small_rows", [P], F32)
+        bias_rows = sbuf("bias_rows", [P], F32)
         spread = sbuf("spread", [J // P, P], F32)
         identity = sbuf("identity", [P], F32)
         eye_codes = sbuf("eye_codes", [PACK * P], U32)
@@ -96,8 +95,9 @@ def tile_list_dl_silu_kernel(
             for u in us:
                 nc.sync.dma_start(out=planes[u][:], in_=x_rows[u // PACK, u % PACK])
 
-        def load_c(j0, width):
-            nc.sync.dma_start(out=c_raw[j0][:], in_=c_rows[:, :, j0 : j0 + width])
+        def load_c(*blks):
+            for blk in blks:
+                nc.sync.dma_start(out=c_raw[blk][:], in_=c_rows[:, :, blk * BLOCK : (blk + 1) * BLOCK])
 
         def load_wx_scales(q):
             nc.sync.dma_start(
@@ -123,10 +123,11 @@ def tile_list_dl_silu_kernel(
         def quantize(codes, scales, grouped):
             nc.vector.quantize_mx(out=codes.bitcast(FP8X4), scales=scales, in_=grouped.rearrange("p w i -> p (w i)"))
 
-        def first_tier(j0, width):
-            cols = slice(j0, j0 + width)
-            group_on_scalar(c_grouped[:, cols, :], c_raw[j0][:])
-            quantize(cq_codes[:, cols], cq_scales[:, cols], c_grouped[:, cols, :])
+        def first_tier(blk):
+            cols = slice(blk * BLOCK, (blk + 1) * BLOCK)
+            grouped = c_grouped[blk // 2][:, blk % 2 * BLOCK : (blk % 2 + 1) * BLOCK, :]
+            group_on_scalar(grouped, c_raw[blk][:])
+            quantize(cq_codes[:, cols], cq_scales[:, cols], grouped)
 
         def first_tier_values(j0):
             values = bank(j0 // P, [PACK, P])
@@ -142,12 +143,15 @@ def tile_list_dl_silu_kernel(
                 )
             return values
 
-        def subtract_on_vector(j0, width):
-            for r in range(0, width, P):
-                values = first_tier_values(j0 + r)
+        def residual_of(blk):
+            return c_grouped[0][:, (1 - blk) * BLOCK : (2 - blk) * BLOCK, :]
+
+        def subtract_on_vector(blk):
+            for r in range(0, BLOCK, P):
+                values = first_tier_values(blk * BLOCK + r)
                 nc.vector.tensor_tensor(
-                    out=by_word(c_grouped[:, j0 + r : j0 + r + P, :], False),
-                    in0=by_word(c_raw[j0][:, :, r : r + P], True),
+                    out=by_word(residual_of(blk)[:, r : r + P, :], False),
+                    in0=by_word(c_raw[blk][:, :, r : r + P], True),
                     in1=by_word(values[:], True),
                     op=ALU.subtract,
                 )
@@ -161,7 +165,8 @@ def tile_list_dl_silu_kernel(
                 nc.scalar.activation(out=negated[:, run], in_=values[:], func=ACT.Copy, scale=-1.0)
             for run in runs:
                 turned = bank(run, [PACK, P])
-                for term, planar in enumerate((c_raw[HALF][:, :, run * P : (run + 1) * P], negated[:, run])):
+                c_run = c_raw[2 + run // 2][:, :, run % 2 * P : (run % 2 + 1) * P]
+                for term, planar in enumerate((c_run, negated[:, run])):
                     for i in range(PACK):
                         nc.tensor.matmul(
                             turned[:, i, :],
@@ -270,21 +275,29 @@ def tile_list_dl_silu_kernel(
             nc.sync.dma_start(out=rows.rearrange("(s p) j -> p s j", p=P), in_=result[:])
 
         nc.vector.memset(ones[:], 1.0)
-        nc.scalar.activation(out=small_rows[:], in_=ones[:, 0:1].to_broadcast([P, P]), func=ACT.Silu, scale=0.0)
+        unloaded = slice(HEAD_ROWS, P)
+        nc.scalar.activation(
+            out=small_rows[unloaded, :],
+            in_=ones[unloaded, 0:1].to_broadcast([P - HEAD_ROWS, P]),
+            func=ACT.Silu,
+            scale=0.0,
+        )
+        nc.vector.memset(bias_rows[:], 0.0)
         nc.vector.memset(w_scales[:].bitcast(I32), 0)
 
-        nc.sync.dma_start(offsets[:], offs)
-        for j0, width in C_PIECES[0:2]:
-            load_c(j0, width)
         head_rows = wgt.rearrange("(g q) (r s) -> q g r s", q=LIST_ROWS, s=P)[0]
         nc.sync.dma_start(out=small_rows[0:HEAD_ROWS, :], in_=head_rows)
-        nc.sync.dma_start(out=small_rows[HEAD_ROWS : HEAD_ROWS + N_TILES, :], in_=b.rearrange("(t p) -> t p", p=P))
-        load_c(HALF, HALF)
+        load_c(0)
+        nc.sync.dma_start(offsets[:], offs)
+        load_planes(0)
+        load_c(1, 2, 3)
+        nc.sync.dma_start(out=bias_rows[0:N_TILES, :], in_=b.rearrange("(t p) -> t p", p=P))
         load_wx_scales(0)
-        for u in range(2):
-            load_planes(u)
-            load_wx_scales(u + 1)
-            load_wt4_scales(u)
+        load_wx_scales(1)
+        load_wt4_scales(0)
+        load_planes(1)
+        load_wx_scales(2)
+        load_wt4_scales(1)
         load_planes(2)
         load_wx_scales(3)
         nc.sync.dma_start(out=wx_codes[:].bitcast(I32), in_=wx_words[0].rearrange("p n i -> p (n i)").bitcast(I32))
@@ -312,6 +325,13 @@ def tile_list_dl_silu_kernel(
         nc.vector.tensor_scalar(
             out=own_column[:], in0=lane[:, 0:1], scalar1=quadrant_base[:], scalar2=float(PACK), op0=ALU.add, op1=ALU.mult
         )
+        nc.vector.tensor_scalar(
+            out=identity[:],
+            in0=ramp[:, PACK - 1 : PACK - 1 + PACK * P : PACK],
+            scalar1=own_column[:],
+            scalar2=None,
+            op0=ALU.is_equal,
+        )
         for i in range(PACK):
             first = PACK - 1 - i
             nc.vector.tensor_scalar(
@@ -324,23 +344,9 @@ def tile_list_dl_silu_kernel(
         nc.vector.quantize_mx(
             out=eye_codes[:].bitcast(FP8X4), scales=eye_scales[:], in_=eye[:].rearrange("p i x -> p (i x)")
         )
-        nc.vector.tensor_scalar(
-            out=identity[:],
-            in0=ramp[:, PACK - 1 : PACK - 1 + PACK * P : PACK],
-            scalar1=own_column[:],
-            scalar2=None,
-            op0=ALU.is_equal,
-        )
-
-        for j0, width in C_PIECES[0:2]:
-            first_tier(j0, width)
-        for j0, width in C_PIECES[0:2]:
-            subtract_on_vector(j0, width)
-        first_tier(HALF, HALF)
 
         small_turned = bank(7, [P])
         nc.tensor.transpose(small_turned[:], small_rows[:], identity[:])
-        nc.scalar.copy(out=bias[:], in_=small_turned[:, HEAD_ROWS : HEAD_ROWS + N_TILES])
         by_run = small_turned[:, 0:HEAD_ROWS].rearrange("s (g r) -> s r g", r=J // P)
         for h in range(2):
             runs = slice(PACK * h, PACK * (h + 1))
@@ -349,16 +355,26 @@ def tile_list_dl_silu_kernel(
                 in_=by_run[:, runs, :].unsqueeze(3).to_broadcast([P, PACK, HEADS, LIST_ROWS]),
             )
         for h in range(2):
-            wgt_half = bank(2 + h, [PACK, P])
+            wgt_half = bank(5 + h, [PACK, P])
             for r in range(PACK):
                 nc.tensor.transpose(wgt_half[:, r, :], spread[:, PACK * h + r, :], identity[:])
             nc.scalar.copy(out=wgt_sb[:, h * HALF : (h + 1) * HALF], in_=wgt_half[:].rearrange("p r s -> p (r s)"))
 
-        for blk in range(2):
-            quantize(block_of(cr_codes[0], blk), block_of(cr_scales, blk), c_grouped[:, blk * BLOCK : (blk + 1) * BLOCK, :])
-
+        first_tier(0)
+        first_tier(1)
         gather(0, 0, HALF)
         gather(0, HALF, HALF)
+        for blk in range(2):
+            subtract_on_vector(blk)
+        first_tier(2)
+        first_tier(3)
+        for blk in range(2):
+            quantize(block_of(cr_codes[0], blk), block_of(cr_scales, blk), residual_of(blk))
+
+        bias_turned = bank(7, [P])
+        nc.tensor.transpose(bias_turned[:], bias_rows[:], identity[:])
+        nc.scalar.copy(out=bias[:], in_=bias_turned[:, 0:N_TILES])
+
         for u in (1, 2):
             gather(u, 0, J)
         subtract_by_transposes()

@@ -81,7 +81,6 @@ def tile_list_dl_silu_kernel(
         ramp = sbuf("ramp", [ramp_runs * QUAD], F32)
         eye = sbuf("eye", [PACK, PACK * P], BF16)
         small_rows = sbuf("small_rows", [P], F32)
-        bias_rows = sbuf("bias_rows", [P], F32)
         spread = sbuf("spread", [J // P, P], F32)
         identity = sbuf("identity", [P], F32)
         eye_codes = sbuf("eye_codes", [PACK * P], U32)
@@ -282,7 +281,6 @@ def tile_list_dl_silu_kernel(
             func=ACT.Silu,
             scale=0.0,
         )
-        nc.vector.memset(bias_rows[:], 0.0)
         nc.vector.memset(w_scales[:].bitcast(I32), 0)
 
         head_rows = wgt.rearrange("(g q) (r s) -> q g r s", q=LIST_ROWS, s=P)[0]
@@ -290,25 +288,31 @@ def tile_list_dl_silu_kernel(
         load_c(0)
         nc.sync.dma_start(offsets[:], offs)
         load_planes(0)
-        load_c(1, 2, 3)
-        nc.sync.dma_start(out=bias_rows[0:N_TILES, :], in_=b.rearrange("(t p) -> t p", p=P))
+        load_c(1)
+        load_c(2)
+        load_c(3)
+        load_planes(1)
         load_wx_scales(0)
         load_wx_scales(1)
-        load_wt4_scales(0)
-        load_planes(1)
-        load_wx_scales(2)
-        load_wt4_scales(1)
         load_planes(2)
+        load_wx_scales(2)
         load_wx_scales(3)
         nc.sync.dma_start(out=wx_codes[:].bitcast(I32), in_=wx_words[0].rearrange("p n i -> p (n i)").bitcast(I32))
-        load_planes(3, 4, 5)
+        load_planes(3)
+        load_planes(4)
+        load_planes(5)
+        load_wt4_scales(0)
+        load_wt4_scales(1)
         nc.sync.dma_start(out=wtd_early[:], in_=wtd_rows[0])
         load_wt4_scales(2)
         load_wt4_scales(3)
         nc.sync.dma_start(out=wt4_codes[:].bitcast(I32), in_=wt4_words.rearrange("a p n -> p a n").bitcast(I32))
-        load_planes(6, LAST_PLANE)
-        for pair in range(2):
-            nc.sync.dma_start(out=wtd_late[pair], in_=wtd_rows[1, :, :, pair * BLOCK : (pair + 1) * BLOCK])
+        load_planes(6)
+        load_planes(7)
+        nc.sync.dma_start(out=wtd_late[0], in_=wtd_rows[1, :, :, 0 * BLOCK : (0 + 1) * BLOCK])
+        nc.sync.dma_start(out=wtd_late[1], in_=wtd_rows[1, :, :, 1 * BLOCK : (1 + 1) * BLOCK])
+        with nc.allow_non_contiguous_dma(reason="one bias value a partition and output tile"):
+            nc.sync.dma_start(out=bias[:], in_=b.rearrange("(t p) -> p t", p=P))
 
         for q in range(P // QUAD):
             nc.vector.memset(quadrant_base[QUAD * q : QUAD * (q + 1), :], QUAD * q + 0.75)
@@ -370,10 +374,6 @@ def tile_list_dl_silu_kernel(
         first_tier(3)
         for blk in range(2):
             quantize(block_of(cr_codes[0], blk), block_of(cr_scales, blk), residual_of(blk))
-
-        bias_turned = bank(7, [P])
-        nc.tensor.transpose(bias_turned[:], bias_rows[:], identity[:])
-        nc.scalar.copy(out=bias[:], in_=bias_turned[:, 0:N_TILES])
 
         for u in (1, 2):
             gather(u, 0, J)

@@ -28,7 +28,8 @@ LAST_PLANE = 2 * PACK - 1
 HEADS = P // LIST_ROWS
 HEAD_ROWS = HEADS * J // P
 WX_SCALES = 2
-LAST_ROWS = (BLOCKS, BLOCKS + 1, BLOCKS + 2, BLOCKS + 2 + PACK)
+LAST_ROWS = (4, 5, 8, 12)
+SPLIT = (3,)
 
 
 def tile_list_dl_silu_kernel(
@@ -50,11 +51,11 @@ def tile_list_dl_silu_kernel(
         planes = [sbuf("plane%d" % u, [T], F32) for u in range(2 * PACK)]
         early_picks = sbuf("early_picks", [PACK, J], F32)
         middle_picks = sbuf("middle_picks", [2, J], F32)
-        late_picks = sbuf("late_picks", [LAST_ROWS[-1] + PACK, BLOCK], F32)
+        late_picks = sbuf("late_picks", [16, BLOCK], F32)
         c_raw = [sbuf("c_raw%d" % (blk * BLOCK), [PACK, BLOCK], F32) for blk in range(BLOCKS)]
         c_grouped = [sbuf("c_grouped%d" % h, [HALF, PACK], BF16) for h in range(2)]
         wtd_early = sbuf("wtd_early", [PACK, N], F32)
-        wtd_late = [late_picks[:, first : first + PACK, :] for first in LAST_ROWS[2:]]
+        wtd_late = [late_picks[:, first : first + PACK, :] for first in (8, 12)]
         wtd_early_grouped = sbuf("wtd_early_grouped", [N, PACK], BF16)
         wtd_late_grouped = [sbuf("wtd_late_grouped%d" % pair, [BLOCK, PACK], BF16) for pair in range(2)]
         xg_grouped = [sbuf("xg_grouped0", [J, PACK], BF16), sbuf("xg_grouped1", [J, PACK], BF16, bytes_of="wtd_early")]
@@ -65,7 +66,9 @@ def tile_list_dl_silu_kernel(
         wtd_codes = [sbuf("wtd_codes%d" % a, [N], U32) for a in range(2)]
         wtd_scales = sbuf("wtd_scales", [2, N], U8)
         xg_early_codes = sbuf("xg_early_codes", [J], U32)
-        xg_late_codes = {}
+        xg_late_codes = [
+            sbuf("xg_late_codes%d" % blk, [BLOCK], U32, bytes_of=held) for blk, held in enumerate((None, None, "wtd_late_grouped1", None))
+        ]
         xg_scales = sbuf("xg_scales", [2, J], U8)
         cq_codes = sbuf("cq_codes", [J], U32)
         cq_scales = sbuf("cq_scales", [J], U8)
@@ -192,7 +195,7 @@ def tile_list_dl_silu_kernel(
                 return middle_picks[:, u - PACK, j0 : j0 + width]
             if u < LAST_PLANE:
                 return late_picks[:, 0:BLOCKS, :].rearrange("p r j -> p (r j)")[:, j0 : j0 + width]
-            return late_picks[:, LAST_ROWS[j0 // BLOCK], :]
+            return late_picks[:, LAST_ROWS[j0 // BLOCK], j0 % BLOCK : j0 % BLOCK + width]
 
         def gather(u, j0, width):
             nc.vector.tensor_tensor(
@@ -212,18 +215,17 @@ def tile_list_dl_silu_kernel(
             group_on_scalar(wtd_early_grouped[:, cols, :], wtd_early[:, :, cols])
             quantize(wtd_codes[0][:, cols], wtd_scales[:, 0, cols], wtd_early_grouped[:, cols, :])
 
-        def gather_block(blk):
-            gather(LAST_PLANE, blk * BLOCK, BLOCK)
+        def gather_block(blk, r=0, width=BLOCK):
+            gather(LAST_PLANE, blk * BLOCK + r, width)
 
-        def group_block(group, blk):
+        def group_block(group, blk, r=0, width=BLOCK):
             last = LAST_ROWS[blk]
-            both = late_picks[:, blk : last + 1 : last - blk, :]
-            group(xg_grouped[1][:, blk * BLOCK : (blk + 1) * BLOCK, 2:PACK], both)
+            both = late_picks[:, blk : last + 1 : last - blk, r : r + width]
+            group(xg_grouped[1][:, blk * BLOCK + r : blk * BLOCK + r + width, 2:PACK], both)
 
-        def quantize_block(blk, bytes_of=None):
-            cols = slice(blk * BLOCK, (blk + 1) * BLOCK)
-            xg_late_codes[blk] = sbuf("xg_late_codes%d" % blk, [BLOCK], U32, bytes_of=bytes_of)
-            quantize(xg_late_codes[blk][:], xg_scales[:, 1, cols], xg_grouped[1][:, cols, :])
+        def quantize_block(blk, r=0, width=BLOCK):
+            cols = slice(blk * BLOCK + r, blk * BLOCK + r + width)
+            quantize(xg_late_codes[blk][:, r : r + width], xg_scales[:, 1, cols], xg_grouped[1][:, cols, :])
 
         def quantize_late_wtd(pair):
             cols = slice(pair * BLOCK, (pair + 1) * BLOCK)
@@ -243,8 +245,8 @@ def tile_list_dl_silu_kernel(
 
         sums = {}
 
-        def add_passes(blk, pair, stationary, codes, scales, width=BLOCK, start=False, stop=False):
-            steps = [(s, r) for s in range(2) for r in range(0, BLOCK, width)]
+        def add_passes(blk, pair, stationary, codes, scales, width=BLOCK, start=False, stop=False, places=(0, BLOCK)):
+            steps = [(s, r) for s in range(2) for r in range(places[0], places[1], width)]
             for s, r in steps:
                 lhs_codes, lhs_scales = stationary(2 * pair + s)
                 nc.tensor.matmul_mx(
@@ -261,17 +263,27 @@ def tile_list_dl_silu_kernel(
             return codes[:, blk * BLOCK : (blk + 1) * BLOCK]
 
         def finish(blk, pair):
-            add_passes(blk, pair, wt4_tile(1), xg_late_codes[blk], xg_scales[:, 1, :], width=P)
-            add_passes(blk, pair, wtd_tile(1), xg_late_codes[blk], xg_scales[:, 1, :], stop=True)
+            codes = xg_late_codes[blk]
+            width = P if blk in SPLIT else BLOCK
+            for r in range(0, BLOCK, width):
+                places = (r, r + width)
+                add_passes(blk, pair, wt4_tile(1), codes, xg_scales[:, 1, :], width=P, places=places)
+                add_passes(
+                    blk, pair, wtd_tile(1), codes, xg_scales[:, 1, :], width=width, stop=r + width == BLOCK, places=places
+                )
             number = 2 * blk + pair
             result = sbuf("result%d" % number, [2, BLOCK], F32, bytes_of="plane%d" % number if number < PACK else None)
+            rows = out[pair * BLOCK : (pair + 1) * BLOCK, blk * BLOCK : (blk + 1) * BLOCK].rearrange("(s p) j -> p s j", p=P)
+            last = number == 2 * BLOCKS - 1
             for s in range(2):
                 t = 2 * pair + s
                 nc.scalar.activation(
                     out=result[:, s, :], in_=sums[blk, pair][:, s, :], func=ACT.Silu, bias=bias[:, t : t + 1]
                 )
-            rows = out[pair * BLOCK : (pair + 1) * BLOCK, blk * BLOCK : (blk + 1) * BLOCK]
-            nc.sync.dma_start(out=rows.rearrange("(s p) j -> p s j", p=P), in_=result[:])
+                if last:
+                    nc.sync.dma_start(out=rows[:, s, :], in_=result[:, s, :])
+            if not last:
+                nc.sync.dma_start(out=rows, in_=result[:])
 
         nc.vector.memset(ones[:], 1.0)
         unloaded = slice(HEAD_ROWS, P)
@@ -285,9 +297,9 @@ def tile_list_dl_silu_kernel(
 
         head_rows = wgt.rearrange("(g q) (r s) -> q g r s", q=LIST_ROWS, s=P)[0]
         nc.sync.dma_start(out=small_rows[0:HEAD_ROWS, :], in_=head_rows)
-        load_c(0)
         nc.sync.dma_start(offsets[:], offs)
         load_planes(0)
+        load_c(0)
         load_c(1)
         load_c(2)
         load_c(3)
@@ -297,9 +309,9 @@ def tile_list_dl_silu_kernel(
         load_planes(2)
         load_wx_scales(2)
         load_wx_scales(3)
-        nc.sync.dma_start(out=wx_codes[:].bitcast(I32), in_=wx_words[0].rearrange("p n i -> p (n i)").bitcast(I32))
         load_planes(3)
         load_planes(4)
+        nc.sync.dma_start(out=wx_codes[:].bitcast(I32), in_=wx_words[0].rearrange("p n i -> p (n i)").bitcast(I32))
         load_planes(5)
         load_wt4_scales(0)
         load_wt4_scales(1)
@@ -352,26 +364,26 @@ def tile_list_dl_silu_kernel(
         small_turned = bank(7, [P])
         nc.tensor.transpose(small_turned[:], small_rows[:], identity[:])
         by_run = small_turned[:, 0:HEAD_ROWS].rearrange("s (g r) -> s r g", r=J // P)
-        for h in range(2):
-            runs = slice(PACK * h, PACK * (h + 1))
+        for blk in range(BLOCKS):
+            runs = slice(2 * blk, 2 * blk + 2)
             nc.scalar.copy(
                 out=spread[:, runs, :].rearrange("s r (g q) -> s r g q", q=LIST_ROWS),
-                in_=by_run[:, runs, :].unsqueeze(3).to_broadcast([P, PACK, HEADS, LIST_ROWS]),
+                in_=by_run[:, runs, :].unsqueeze(3).to_broadcast([P, 2, HEADS, LIST_ROWS]),
             )
-        for h in range(2):
-            wgt_half = bank(5 + h, [PACK, P])
-            for r in range(PACK):
-                nc.tensor.transpose(wgt_half[:, r, :], spread[:, PACK * h + r, :], identity[:])
-            nc.scalar.copy(out=wgt_sb[:, h * HALF : (h + 1) * HALF], in_=wgt_half[:].rearrange("p r s -> p (r s)"))
+        for blk in range(BLOCKS):
+            wgt_block = bank(3 + blk, [2, P])
+            for r in range(2):
+                nc.tensor.transpose(wgt_block[:, r, :], spread[:, 2 * blk + r, :], identity[:])
+            nc.scalar.copy(out=block_of(wgt_sb, blk), in_=wgt_block[:].rearrange("p r s -> p (r s)"))
 
+        for blk in range(BLOCKS):
+            gather(0, blk * BLOCK, BLOCK)
         first_tier(0)
         first_tier(1)
-        gather(0, 0, HALF)
-        gather(0, HALF, HALF)
-        for blk in range(2):
-            subtract_on_vector(blk)
         first_tier(2)
         first_tier(3)
+        for blk in range(2):
+            subtract_on_vector(blk)
         for blk in range(2):
             quantize(block_of(cr_codes[0], blk), block_of(cr_scales, blk), residual_of(blk))
 
@@ -423,10 +435,14 @@ def tile_list_dl_silu_kernel(
         finish(0, 1)
         finish(1, 1)
         group_block(group_on_vector, 2)
-        gather_block(3)
-        quantize_block(2, bytes_of="wtd_late_grouped1")
-        group_block(group_on_vector, 3)
-        quantize_block(3)
-        for blk in (2, 3):
-            finish(blk, 0)
-            finish(blk, 1)
+        gather_block(3, 0, P)
+        quantize_block(2)
+        gather_block(3, P, P)
+        group_block(group_on_vector, 3, 0, P)
+        group_block(group_on_vector, 3, P, P)
+        quantize_block(3, 0, P)
+        quantize_block(3, P, P)
+        finish(2, 0)
+        finish(2, 1)
+        finish(3, 0)
+        finish(3, 1)

@@ -28,7 +28,8 @@ LAST_PLANE = 2 * PACK - 1
 HEADS = P // LIST_ROWS
 HEAD_ROWS = HEADS * J // P
 WX_SCALES = 2
-LAST_ROWS = (4, 5, 8, 12)
+LAST_ROWS = (4, 5, 6, 10)
+ROAD_START = 3 * P
 SPLIT = (3,)
 
 
@@ -51,11 +52,11 @@ def tile_list_dl_silu_kernel(
         planes = [sbuf("plane%d" % u, [T], F32) for u in range(2 * PACK)]
         early_picks = sbuf("early_picks", [PACK, J], F32)
         middle_picks = sbuf("middle_picks", [2, J], F32)
-        late_picks = sbuf("late_picks", [16, BLOCK], F32)
+        late_picks = sbuf("late_picks", [14, BLOCK], F32)
         c_raw = [sbuf("c_raw%d" % (blk * BLOCK), [PACK, BLOCK], F32) for blk in range(BLOCKS)]
         c_grouped = [sbuf("c_grouped%d" % h, [HALF, PACK], BF16) for h in range(2)]
         wtd_early = sbuf("wtd_early", [PACK, N], F32)
-        wtd_late = [late_picks[:, first : first + PACK, :] for first in (8, 12)]
+        wtd_late = [late_picks[:, first : first + PACK, :] for first in LAST_ROWS[2:]]
         wtd_early_grouped = sbuf("wtd_early_grouped", [N, PACK], BF16)
         wtd_late_grouped = [sbuf("wtd_late_grouped%d" % pair, [BLOCK, PACK], BF16) for pair in range(2)]
         xg_grouped = [sbuf("xg_grouped0", [J, PACK], BF16), sbuf("xg_grouped1", [J, PACK], BF16, bytes_of="wtd_early")]
@@ -73,8 +74,8 @@ def tile_list_dl_silu_kernel(
         cq_codes = sbuf("cq_codes", [J], U32)
         cq_scales = sbuf("cq_scales", [J], U8)
         cr_scales = sbuf("cr_scales", [J], U8)
-        cr_codes = [sbuf("cr_codes0", [HALF], U32), sbuf("cr_codes1", [HALF], U32, bytes_of="plane4")]
-        residual_words = sbuf("residual_words", [HALF, 2], F32)
+        cr_codes = [sbuf("cr_codes0", [ROAD_START], U32), sbuf("cr_codes1", [J - ROAD_START], U32, bytes_of="plane4")]
+        residual_words = sbuf("residual_words", [J - ROAD_START, 2], F32)
         ones = sbuf("ones", [QUAD], F32)
         count = sbuf("count", [QUAD], F32)
         lane = sbuf("lane", [QUAD], F32)
@@ -131,8 +132,8 @@ def tile_list_dl_silu_kernel(
             group_on_scalar(grouped, c_raw[blk][:])
             quantize(cq_codes[:, cols], cq_scales[:, cols], grouped)
 
-        def first_tier_values(j0):
-            values = bank(j0 // P, [PACK, P])
+        def first_tier_values(j0, number):
+            values = bank(number, [PACK, P])
             for i in range(PACK):
                 nc.tensor.matmul_mx(
                     out=values[:, i, :],
@@ -148,9 +149,9 @@ def tile_list_dl_silu_kernel(
         def residual_of(blk):
             return c_grouped[0][:, (1 - blk) * BLOCK : (2 - blk) * BLOCK, :]
 
-        def subtract_on_vector(blk):
-            for r in range(0, BLOCK, P):
-                values = first_tier_values(blk * BLOCK + r)
+        def subtract_on_vector(blk, places):
+            for r in range(0, places, P):
+                values = first_tier_values(blk * BLOCK + r, 2 * blk + r // P)
                 nc.vector.tensor_tensor(
                     out=by_word(residual_of(blk)[:, r : r + P, :], False),
                     in0=by_word(c_raw[blk][:, :, r : r + P], True),
@@ -159,16 +160,16 @@ def tile_list_dl_silu_kernel(
                 )
 
         def subtract_by_transposes():
-            runs = range(HALF // P)
+            runs = (3, 4, 5, 6, 7)
             negated = sbuf("negated", [len(runs), PACK, P], F32)
-            rounded = [sbuf("rounded%d" % run, [P, PACK], BF16) for run in runs]
-            for run in runs:
-                values = first_tier_values(HALF + run * P)
-                nc.scalar.activation(out=negated[:, run], in_=values[:], func=ACT.Copy, scale=-1.0)
-            for run in runs:
-                turned = bank(run, [PACK, P])
-                c_run = c_raw[2 + run // 2][:, :, run % 2 * P : (run % 2 + 1) * P]
-                for term, planar in enumerate((c_run, negated[:, run])):
+            rounded = {run: sbuf("rounded%d" % run, [P, PACK], BF16) for run in runs}
+            for run, number in zip(runs, (0, 4, 5, 6, 7)):
+                values = first_tier_values(run * P, number)
+                nc.scalar.activation(out=negated[:, run - 3], in_=values[:], func=ACT.Copy, scale=-1.0)
+            for run, number in zip(runs, (3, 1, 2, 0, 4)):
+                turned = bank(number, [PACK, P])
+                c_run = c_raw[run // 2][:, :, run % 2 * P : (run % 2 + 1) * P]
+                for term, planar in enumerate((c_run, negated[:, run - 3])):
                     for i in range(PACK):
                         nc.tensor.matmul(
                             turned[:, i, :],
@@ -179,13 +180,13 @@ def tile_list_dl_silu_kernel(
                             is_transpose=True,
                         )
                 nc.scalar.copy(out=rounded[run][:], in_=turned[:].rearrange("j i p -> j p i"))
-            for run in runs:
+            for run, number in zip(runs, (5, 6, 7, 3, 1)):
                 words = rounded[run][:].rearrange("j p i -> j (p i)").bitcast(F32)
-                back = bank(HALF // P + run, [2, P])
+                back = bank(number, [2, P])
                 for u in range(2):
                     nc.tensor.transpose(back[:, u, :], words[:, u : 2 * P : 2], identity[:])
                 nc.scalar.copy(
-                    out=residual_words[:, run * P : (run + 1) * P, :], in_=back[:].rearrange("p u j -> p j u")
+                    out=residual_words[:, (run - 3) * P : (run - 2) * P, :], in_=back[:].rearrange("p u j -> p j u")
                 )
 
         def picks(u, j0, width):
@@ -245,7 +246,7 @@ def tile_list_dl_silu_kernel(
 
         sums = {}
 
-        def add_passes(blk, pair, stationary, codes, scales, width=BLOCK, start=False, stop=False, places=(0, BLOCK)):
+        def add_passes(blk, pair, stationary, codes, scales, width=BLOCK, start=False, stop=False, places=(0, BLOCK), shift=0):
             steps = [(s, r) for s in range(2) for r in range(places[0], places[1], width)]
             for s, r in steps:
                 lhs_codes, lhs_scales = stationary(2 * pair + s)
@@ -253,7 +254,7 @@ def tile_list_dl_silu_kernel(
                     out=sums[blk, pair][:, s, r : r + width],
                     lhsT=lhs_codes,
                     lhsT_scale=lhs_scales,
-                    rhs=codes[:, r : r + width].bitcast(FP8X4),
+                    rhs=codes[:, r - shift : r - shift + width].bitcast(FP8X4),
                     rhs_scale=scales[:, blk * BLOCK + r : blk * BLOCK + r + width],
                     start=start and (s, r) == steps[0],
                     stop=stop and (s, r) == steps[-1],
@@ -382,10 +383,10 @@ def tile_list_dl_silu_kernel(
         first_tier(1)
         first_tier(2)
         first_tier(3)
-        for blk in range(2):
-            subtract_on_vector(blk)
-        for blk in range(2):
-            quantize(block_of(cr_codes[0], blk), block_of(cr_scales, blk), residual_of(blk))
+        subtract_on_vector(0, BLOCK)
+        subtract_on_vector(1, P)
+        quantize(cr_codes[0][:, 0:BLOCK], cr_scales[:, 0:BLOCK], residual_of(0))
+        quantize(cr_codes[0][:, BLOCK:ROAD_START], cr_scales[:, BLOCK:ROAD_START], residual_of(1)[:, 0:P, :])
 
         for u in (1, 2):
             gather(u, 0, J)
@@ -395,11 +396,12 @@ def tile_list_dl_silu_kernel(
         gather(4, 0, J)
         gather(5, 0, J)
         early_xg(0)
-        nc.vector.quantize_mx(
-            out=cr_codes[1][:].bitcast(FP8X4),
-            scales=cr_scales[:, HALF:J],
-            in_=residual_words[:].rearrange("p j u -> p (j u)").bitcast(BF16),
-        )
+        for first, last in ((P, J - ROAD_START), (0, P)):
+            nc.vector.quantize_mx(
+                out=cr_codes[1][:, first:last].bitcast(FP8X4),
+                scales=cr_scales[:, ROAD_START + first : ROAD_START + last],
+                in_=residual_words[:, first:last, :].rearrange("p j u -> p (j u)").bitcast(BF16),
+            )
         early_xg(HALF)
         early_wtd(0)
         early_wtd(1)
@@ -410,8 +412,13 @@ def tile_list_dl_silu_kernel(
         for blk in range(BLOCKS):
             for pair in range(2):
                 sums[blk, pair] = bank(2 * blk + pair, [2, BLOCK])
-                add_passes(blk, pair, wx_tile, block_of(cr_codes[blk // 2], blk % 2), cr_scales, start=True)
-                add_passes(blk, pair, wx_tile, block_of(cq_codes, blk), cq_scales)
+                add_passes(blk, pair, wx_tile, block_of(cq_codes, blk), cq_scales, start=True)
+                if blk == 1:
+                    add_passes(blk, pair, wx_tile, cr_codes[0][:, BLOCK:], cr_scales, width=P, places=(0, P), shift=0)
+                    add_passes(blk, pair, wx_tile, cr_codes[1][:, 0:P], cr_scales, width=P, places=(P, BLOCK), shift=P)
+                else:
+                    codes = cr_codes[0][:, 0:BLOCK] if blk == 0 else cr_codes[1][:, (2 * blk - 3) * P : (2 * blk - 1) * P]
+                    add_passes(blk, pair, wx_tile, codes, cr_scales)
         for pair in range(2):
             for blk in range(BLOCKS):
                 add_passes(blk, pair, wtd_tile(0), block_of(xg_early_codes, blk), xg_scales[:, 0, :])

@@ -63,7 +63,6 @@ def tile_list_dl_silu_kernel(
         bias = sbuf("bias", [N_TILES], F32)
         wt4_codes = sbuf("wt4_codes", [2, 2 * N], U8)
         wx_codes = sbuf("wx_codes", [N], U32)
-        w_scales = sbuf("w_scales", [3, N], U8)
         wtd_codes = [sbuf("wtd_codes%d" % a, [N], U32) for a in range(2)]
         wtd_scales = sbuf("wtd_scales", [2, N], U8)
         xg_early_codes = sbuf("xg_early_codes", [J], U32)
@@ -76,17 +75,15 @@ def tile_list_dl_silu_kernel(
         cr_scales = sbuf("cr_scales", [J], U8)
         cr_codes = [sbuf("cr_codes0", [ROAD_START], U32), sbuf("cr_codes1", [J - ROAD_START], U32, bytes_of="plane4")]
         residual_words = sbuf("residual_words", [J - ROAD_START, 2], F32)
-        ones = sbuf("ones", [QUAD], F32)
-        count = sbuf("count", [QUAD], F32)
+        ones = sbuf("ones", [P + 1], F32)
+        count = sbuf("count", [P], F32)
         lane = sbuf("lane", [QUAD], F32)
         quadrant_base = sbuf("quadrant_base", [1], F32)
-        own_column = sbuf("own_column", [1], F32)
-        ramp_runs = PACK * P // QUAD + 1
-        ramp = sbuf("ramp", [ramp_runs * QUAD], F32)
-        eye = sbuf("eye", [PACK, PACK * P], BF16)
+        eye = sbuf("eye", [PACK * (PACK * P + 1)], BF16)
         small_rows = sbuf("small_rows", [P], F32)
         spread = sbuf("spread", [J // P, P], F32)
         identity = sbuf("identity", [P], F32)
+        w_scales = sbuf("w_scales", [3, N], U8, bytes_of="eye")
         eye_codes = sbuf("eye_codes", [PACK * P], U32)
         eye_scales = sbuf("eye_scales", [PACK * P], U8)
 
@@ -286,6 +283,7 @@ def tile_list_dl_silu_kernel(
             if not last:
                 nc.sync.dma_start(out=rows, in_=result[:])
 
+        nc.gpsimd.memset(eye[:].bitcast(I32), 0)
         nc.vector.memset(ones[:], 1.0)
         unloaded = slice(HEAD_ROWS, P)
         nc.scalar.activation(
@@ -294,7 +292,25 @@ def tile_list_dl_silu_kernel(
             func=ACT.Silu,
             scale=0.0,
         )
-        nc.vector.memset(w_scales[:].bitcast(I32), 0)
+
+        for q in range(P // QUAD):
+            nc.vector.memset(quadrant_base[QUAD * q : QUAD * (q + 1), :], float(QUAD * q))
+        nc.vector.tensor_tensor_scan(out=count[:], data0=ones[:, 0:P], data1=ones[:, 0:P], initial=-1.0, op0=ALU.mult, op1=ALU.add)
+        nc.vector.transpose(out=lane[:], in_=count[:, 0:QUAD])
+        nc.vector.tensor_scalar(
+            out=identity[:],
+            in0=count[:],
+            scalar1=quadrant_base[:],
+            scalar2=lane[:, 0:1],
+            op0=ALU.subtract,
+            op1=ALU.is_equal,
+        )
+        nc.vector.tensor_copy(
+            out=eye[:].rearrange("p (i y) -> p i y", i=PACK)[:, :, 0 : PACK * P : PACK],
+            in_=identity[:].unsqueeze(1).to_broadcast([P, PACK, P]),
+        )
+        nc.vector.quantize_mx(out=eye_codes[:].bitcast(FP8X4), scales=eye_scales[:], in_=eye[:, 0 : PACK * PACK * P])
+        nc.gpsimd.memset(w_scales[:].bitcast(I32), 0)
 
         head_rows = wgt.rearrange("(g q) (r s) -> q g r s", q=LIST_ROWS, s=P)[0]
         nc.sync.dma_start(out=small_rows[0:HEAD_ROWS, :], in_=head_rows)
@@ -316,9 +332,9 @@ def tile_list_dl_silu_kernel(
         load_planes(5)
         load_wt4_scales(0)
         load_wt4_scales(1)
-        nc.sync.dma_start(out=wtd_early[:], in_=wtd_rows[0])
         load_wt4_scales(2)
         load_wt4_scales(3)
+        nc.sync.dma_start(out=wtd_early[:], in_=wtd_rows[0])
         nc.sync.dma_start(out=wt4_codes[:].bitcast(I32), in_=wt4_words.rearrange("a p n -> p a n").bitcast(I32))
         load_planes(6)
         load_planes(7)
@@ -326,41 +342,6 @@ def tile_list_dl_silu_kernel(
         nc.sync.dma_start(out=wtd_late[1], in_=wtd_rows[1, :, :, 1 * BLOCK : (1 + 1) * BLOCK])
         with nc.allow_non_contiguous_dma(reason="one bias value a partition and output tile"):
             nc.sync.dma_start(out=bias[:], in_=b.rearrange("(t p) -> p t", p=P))
-
-        for q in range(P // QUAD):
-            nc.vector.memset(quadrant_base[QUAD * q : QUAD * (q + 1), :], QUAD * q + 0.75)
-        nc.vector.tensor_tensor_scan(out=count[:], data0=ones[:], data1=ones[:], initial=-1.0, op0=ALU.mult, op1=ALU.add)
-        nc.vector.transpose(out=lane[:], in_=count[:])
-        nc.vector.scalar_tensor_tensor(
-            out=ramp[:].rearrange("p (a x) -> p a x", x=QUAD),
-            in0=count[:, 0:ramp_runs].unsqueeze(2).to_broadcast([P, ramp_runs, QUAD]),
-            scalar=float(QUAD),
-            in1=count[:].unsqueeze(1).to_broadcast([P, ramp_runs, QUAD]),
-            op0=ALU.mult,
-            op1=ALU.add,
-        )
-        nc.vector.tensor_scalar(
-            out=own_column[:], in0=lane[:, 0:1], scalar1=quadrant_base[:], scalar2=float(PACK), op0=ALU.add, op1=ALU.mult
-        )
-        nc.vector.tensor_scalar(
-            out=identity[:],
-            in0=ramp[:, PACK - 1 : PACK - 1 + PACK * P : PACK],
-            scalar1=own_column[:],
-            scalar2=None,
-            op0=ALU.is_equal,
-        )
-        for i in range(PACK):
-            first = PACK - 1 - i
-            nc.vector.tensor_scalar(
-                out=eye[:, i, :],
-                in0=ramp[:, first : first + PACK * P],
-                scalar1=own_column[:],
-                scalar2=None,
-                op0=ALU.is_equal,
-            )
-        nc.vector.quantize_mx(
-            out=eye_codes[:].bitcast(FP8X4), scales=eye_scales[:], in_=eye[:].rearrange("p i x -> p (i x)")
-        )
 
         small_turned = bank(7, [P])
         nc.tensor.transpose(small_turned[:], small_rows[:], identity[:])
@@ -419,12 +400,16 @@ def tile_list_dl_silu_kernel(
                 else:
                     codes = cr_codes[0][:, 0:BLOCK] if blk == 0 else cr_codes[1][:, (2 * blk - 3) * P : (2 * blk - 1) * P]
                     add_passes(blk, pair, wx_tile, codes, cr_scales)
+        def early_wt4(*blks):
+            for blk in blks:
+                for pair in range(2):
+                    add_passes(blk, pair, wt4_tile(0), block_of(xg_early_codes, blk), xg_scales[:, 0, :], width=P)
+
+        early_wt4(0, 1)
         for pair in range(2):
             for blk in range(BLOCKS):
                 add_passes(blk, pair, wtd_tile(0), block_of(xg_early_codes, blk), xg_scales[:, 0, :])
-        for blk in range(BLOCKS):
-            for pair in range(2):
-                add_passes(blk, pair, wt4_tile(0), block_of(xg_early_codes, blk), xg_scales[:, 0, :], width=P)
+        early_wt4(2, 3)
 
         gather_block(0)
         gather_block(1)

@@ -124,10 +124,12 @@ def tile_list_dl_silu_kernel(
             nc.vector.quantize_mx(out=codes.bitcast(FP8X4), scales=scales, in_=grouped.rearrange("p w i -> p (w i)"))
 
         def first_tier(blk):
-            cols = slice(blk * BLOCK, (blk + 1) * BLOCK)
             grouped = c_grouped[blk // 2][:, blk % 2 * BLOCK : (blk % 2 + 1) * BLOCK, :]
             group_on_scalar(grouped, c_raw[blk][:])
-            quantize(cq_codes[:, cols], cq_scales[:, cols], grouped)
+            width = P if blk < 2 else BLOCK
+            for r in range(0, BLOCK, width):
+                run = slice(blk * BLOCK + r, blk * BLOCK + r + width)
+                quantize(cq_codes[:, run], cq_scales[:, run], grouped[:, r : r + width, :])
 
         def first_tier_values(j0, number):
             values = bank(number, [PACK, P])
@@ -159,7 +161,7 @@ def tile_list_dl_silu_kernel(
         def subtract_by_transposes():
             runs = (3, 4, 5, 6, 7)
             negated = sbuf("negated", [len(runs), PACK, P], F32)
-            rounded = {run: sbuf("rounded%d" % run, [P, PACK], BF16) for run in runs}
+            rounded = {run: sbuf("rounded%d" % run, [2, P, 2], BF16) for run in runs}
             for run, number in zip(runs, (0, 4, 5, 6, 7)):
                 values = first_tier_values(run * P, number)
                 nc.scalar.activation(out=negated[:, run - 3], in_=values[:], func=ACT.Copy, scale=-1.0)
@@ -176,12 +178,12 @@ def tile_list_dl_silu_kernel(
                             stop=(term, i) == (1, PACK - 1),
                             is_transpose=True,
                         )
-                nc.scalar.copy(out=rounded[run][:], in_=turned[:].rearrange("j i p -> j p i"))
+                nc.scalar.copy(out=rounded[run][:], in_=turned[:].rearrange("j (u e) p -> j u p e", e=2))
             for run, number in zip(runs, (5, 6, 7, 3, 1)):
-                words = rounded[run][:].rearrange("j p i -> j (p i)").bitcast(F32)
+                words = rounded[run][:].rearrange("j u p e -> j u (p e)").bitcast(F32)
                 back = bank(number, [2, P])
                 for u in range(2):
-                    nc.tensor.transpose(back[:, u, :], words[:, u : 2 * P : 2], identity[:])
+                    nc.tensor.transpose(back[:, u, :], words[:, u, :], identity[:])
                 nc.scalar.copy(
                     out=residual_words[:, (run - 3) * P : (run - 2) * P, :], in_=back[:].rearrange("p u j -> p j u")
                 )
@@ -283,14 +285,11 @@ def tile_list_dl_silu_kernel(
             if not last:
                 nc.sync.dma_start(out=rows, in_=result[:])
 
-        nc.gpsimd.memset(eye[:].bitcast(I32), 0)
+        nc.gpsimd.memset(small_rows[HEAD_ROWS:P, :], 0.0)
+        nc.gpsimd.memset(eye[:, QUAD:].bitcast(I32), 0)
         nc.vector.memset(ones[:], 1.0)
-        unloaded = slice(HEAD_ROWS, P)
         nc.scalar.activation(
-            out=small_rows[unloaded, :],
-            in_=ones[unloaded, 0:1].to_broadcast([P - HEAD_ROWS, P]),
-            func=ACT.Silu,
-            scale=0.0,
+            out=eye[:, 0:QUAD], in_=ones[:, 0:1].to_broadcast([P, QUAD]), func=ACT.Silu, scale=0.0
         )
 
         for q in range(P // QUAD):
@@ -305,17 +304,21 @@ def tile_list_dl_silu_kernel(
             op0=ALU.subtract,
             op1=ALU.is_equal,
         )
-        nc.vector.tensor_copy(
+        nc.vector.tensor_scalar(
             out=eye[:].rearrange("p (i y) -> p i y", i=PACK)[:, :, 0 : PACK * P : PACK],
-            in_=identity[:].unsqueeze(1).to_broadcast([P, PACK, P]),
+            in0=count[:].unsqueeze(1).to_broadcast([P, PACK, P]),
+            scalar1=quadrant_base[:],
+            scalar2=lane[:, 0:1],
+            op0=ALU.subtract,
+            op1=ALU.is_equal,
         )
         nc.vector.quantize_mx(out=eye_codes[:].bitcast(FP8X4), scales=eye_scales[:], in_=eye[:, 0 : PACK * PACK * P])
         nc.gpsimd.memset(w_scales[:].bitcast(I32), 0)
 
         head_rows = wgt.rearrange("(g q) (r s) -> q g r s", q=LIST_ROWS, s=P)[0]
         nc.sync.dma_start(out=small_rows[0:HEAD_ROWS, :], in_=head_rows)
-        nc.sync.dma_start(offsets[:], offs)
         load_planes(0)
+        nc.sync.dma_start(offsets[:], offs)
         load_c(0)
         load_c(1)
         load_c(2)

@@ -30,7 +30,6 @@ HEAD_ROWS = HEADS * J // P
 WX_SCALES = 2
 LAST_ROWS = (4, 5, 6, 10)
 ROAD_START = 3 * P
-SPLIT = (3,)
 
 
 def tile_list_dl_silu_kernel(
@@ -75,7 +74,7 @@ def tile_list_dl_silu_kernel(
         cr_scales = sbuf("cr_scales", [J], U8)
         cr_codes = [sbuf("cr_codes0", [ROAD_START], U32), sbuf("cr_codes1", [J - ROAD_START], U32, bytes_of="plane4")]
         residual_words = sbuf("residual_words", [J - ROAD_START, 2], F32)
-        ones = sbuf("ones", [P + 1], F32)
+        one = sbuf("one", [1], F32)
         count = sbuf("count", [P], F32)
         lane = sbuf("lane", [QUAD], F32)
         quadrant_base = sbuf("quadrant_base", [1], F32)
@@ -264,13 +263,8 @@ def tile_list_dl_silu_kernel(
 
         def finish(blk, pair):
             codes = xg_late_codes[blk]
-            width = P if blk in SPLIT else BLOCK
-            for r in range(0, BLOCK, width):
-                places = (r, r + width)
-                add_passes(blk, pair, wt4_tile(1), codes, xg_scales[:, 1, :], width=P, places=places)
-                add_passes(
-                    blk, pair, wtd_tile(1), codes, xg_scales[:, 1, :], width=width, stop=r + width == BLOCK, places=places
-                )
+            add_passes(blk, pair, wt4_tile(1), codes, xg_scales[:, 1, :], width=P)
+            add_passes(blk, pair, wtd_tile(1), codes, xg_scales[:, 1, :], stop=True)
             number = 2 * blk + pair
             result = sbuf("result%d" % number, [2, BLOCK], F32, bytes_of="plane%d" % number if number < PACK else None)
             rows = out[pair * BLOCK : (pair + 1) * BLOCK, blk * BLOCK : (blk + 1) * BLOCK].rearrange("(s p) j -> p s j", p=P)
@@ -286,15 +280,16 @@ def tile_list_dl_silu_kernel(
                 nc.sync.dma_start(out=rows, in_=result[:])
 
         nc.gpsimd.memset(small_rows[HEAD_ROWS:P, :], 0.0)
-        nc.gpsimd.memset(eye[:, QUAD:].bitcast(I32), 0)
-        nc.vector.memset(ones[:], 1.0)
+        nc.gpsimd.memset(eye[:, QUAD : PACK * PACK * P].bitcast(I32), 0)
+        nc.vector.memset(one[:], 1.0)
         nc.scalar.activation(
-            out=eye[:, 0:QUAD], in_=ones[:, 0:1].to_broadcast([P, QUAD]), func=ACT.Silu, scale=0.0
+            out=eye[:, 0:QUAD], in_=one[:].to_broadcast([P, QUAD]), func=ACT.Silu, scale=0.0
         )
 
         for q in range(P // QUAD):
             nc.vector.memset(quadrant_base[QUAD * q : QUAD * (q + 1), :], float(QUAD * q))
-        nc.vector.tensor_tensor_scan(out=count[:], data0=ones[:, 0:P], data1=ones[:, 0:P], initial=-1.0, op0=ALU.mult, op1=ALU.add)
+        ones = one[:].to_broadcast([P, P])
+        nc.vector.tensor_tensor_scan(out=count[:], data0=ones, data1=ones, initial=-1.0, op0=ALU.mult, op1=ALU.add)
         nc.vector.transpose(out=lane[:], in_=count[:, 0:QUAD])
         nc.vector.tensor_scalar(
             out=identity[:],

from contextlib import ExitStack

import concourse.mybir as mybir

K, L, N, T, J = 1024, 512, 512, 2048, 1024
FLOPS = 2 * (2 * K + 2 * L) * N * J + 2 * L * L * J

F32 = mybir.dt.float32
BF16 = mybir.dt.bfloat16
I32 = mybir.dt.int32
U32 = mybir.dt.uint32
U16 = mybir.dt.uint16
U8 = mybir.dt.uint8
FP8X4 = mybir.dt.float8_e4m3fn_x4
FP4X4 = mybir.dt.float4_e2m1fn_x4
ALU = mybir.AluOpType
ACT = mybir.ActivationFunctionType

P = 128
QUAD = 32
PACK = 4
LIST_ROWS = 16
HALF = J // 2
BLOCK = 256
BLOCKS = J // BLOCK
N_TILES = N // P
LAST_PLANE = 2 * PACK - 1
HEADS = P // LIST_ROWS
HEAD_ROWS = HEADS * J // P
WX_SCALES = 2
LAST_ROWS = (4, 5, 6, 10)
ROAD_START = 3 * P


def tile_list_dl_silu_kernel(
    tc, xT, wgt, wt4_words, wt4_scales, wtd, c, wx_words, wx_scales, b, offs, out
):
    nc = tc.nc
    with ExitStack() as ctx:
        keep = ctx.enter_context(tc.tile_pool(name="keep", bufs=1))
        psum = ctx.enter_context(tc.psum_pool(name="psum", bufs=1))

        def sbuf(name, shape, dtype, bytes_of=None):
            return keep.tile([P] + shape, dtype, name=name, tag=bytes_of or name, align_bytes=256)

        def bank(number, shape):
            return psum.tile([P] + shape, F32, name="bank%d" % number)

        offsets = keep.tile([P, J // LIST_ROWS], U16, name="offsets")
        wgt_sb = sbuf("wgt_sb", [J], F32)
        planes = [sbuf("plane%d" % u, [T], F32) for u in range(2 * PACK)]
        early_picks = sbuf("early_picks", [PACK, J], F32)
        middle_picks = sbuf("middle_picks", [2, J], F32)
        late_picks = sbuf("late_picks", [14, BLOCK], F32)
        c_raw = [sbuf("c_raw%d" % (blk * BLOCK), [PACK, BLOCK], F32) for blk in range(BLOCKS)]
        c_grouped = [sbuf("c_grouped%d" % h, [HALF, PACK], BF16) for h in range(2)]
        wtd_early = sbuf("wtd_early", [PACK, N], F32)
        wtd_late = [late_picks[:, first : first + PACK, :] for first in LAST_ROWS[2:]]
        wtd_early_grouped = sbuf("wtd_early_grouped", [N, PACK], BF16)
        wtd_late_grouped = [sbuf("wtd_late_grouped%d" % pair, [BLOCK, PACK], BF16) for pair in range(2)]
        xg_grouped = [sbuf("xg_grouped0", [J, PACK], BF16), sbuf("xg_grouped1", [J, PACK], BF16, bytes_of="wtd_early")]
        bias = sbuf("bias", [N_TILES], F32)
        wt4_codes = sbuf("wt4_codes", [2, 2 * N], U8)
        wx_codes = sbuf("wx_codes", [N], U32)
        wtd_codes = [sbuf("wtd_codes%d" % a, [N], U32) for a in range(2)]
        wtd_scales = sbuf("wtd_scales", [2, N], U8)
        xg_early_codes = sbuf("xg_early_codes", [J], U32)
        xg_late_codes = [
            sbuf("xg_late_codes%d" % blk, [BLOCK], U32, bytes_of=held) for blk, held in enumerate((None, None, "wtd_late_grouped1", None))
        ]
        xg_scales = sbuf("xg_scales", [2, J], U8)
        cq_codes = sbuf("cq_codes", [J], U32)
        cq_scales = sbuf("cq_scales", [J], U8)
        cr_scales = sbuf("cr_scales", [J], U8)
        cr_codes = [sbuf("cr_codes0", [ROAD_START], U32), sbuf("cr_codes1", [J - ROAD_START], U32, bytes_of="plane4")]
        residual_words = sbuf("residual_words", [J - ROAD_START, 2], F32)
        one = sbuf("one", [1], F32)
        count = sbuf("count", [P], F32)
        lane = sbuf("lane", [QUAD], F32)
        quadrant_base = sbuf("quadrant_base", [1], F32)
        eye = sbuf("eye", [PACK * (PACK * P + 1)], BF16)
        small_rows = sbuf("small_rows", [P], F32)
        spread = sbuf("spread", [J // P, P], F32)
        identity = sbuf("identity", [P], F32)
        w_scales = sbuf("w_scales", [3, N], U8, bytes_of="eye")
        eye_codes = sbuf("eye_codes", [PACK * P], U32)
        eye_scales = sbuf("eye_scales", [PACK * P], U8)

        x_rows = xT.rearrange("(a p i) t -> a i p t", p=P, i=PACK)
        c_rows = c.rearrange("(p i) j -> p i j", i=PACK)
        wtd_rows = wtd.rearrange("(a p i) n -> a p i n", p=P, i=PACK)

        def load_planes(*us):
            for u in us:
                nc.sync.dma_start(out=planes[u][:], in_=x_rows[u // PACK, u % PACK])

        def load_c(*blks):
            for blk in blks:
                nc.sync.dma_start(out=c_raw[blk][:], in_=c_rows[:, :, blk * BLOCK : (blk + 1) * BLOCK])

        def load_wx_scales(q):
            nc.sync.dma_start(
                out=w_scales[QUAD * q : QUAD * q + 4, WX_SCALES, :].bitcast(I32),
                in_=wx_scales[0, 4 * q : 4 * q + 4, :].bitcast(I32),
            )

        def load_wt4_scales(q):
            nc.sync.dma_start(
                out=w_scales[QUAD * q : QUAD * q + 4, 0:WX_SCALES, :].bitcast(I32),
                in_=wt4_scales[:, 4 * q : 4 * q + 4, :].rearrange("a r n -> r a n").bitcast(I32),
            )

        def by_word(ap, planar):
            return ap.rearrange("p i (w e) -> p w i e" if planar else "p (w e) i -> p w i e", e=2)

        def group_on_scalar(grouped, planar):
            nc.scalar.copy(out=by_word(grouped, False), in_=by_word(planar, True))

        def group_on_vector(grouped, planar):
            nc.vector.tensor_copy(out=by_word(grouped, False), in_=by_word(planar, True))

        def quantize(codes, scales, grouped):
            nc.vector.quantize_mx(out=codes.bitcast(FP8X4), scales=scales, in_=grouped.rearrange("p w i -> p (w i)"))

        def first_tier(blk):
            grouped = c_grouped[blk // 2][:, blk % 2 * BLOCK : (blk % 2 + 1) * BLOCK, :]
            group_on_scalar(grouped, c_raw[blk][:])
            width = P if blk < 2 else BLOCK
            for r in range(0, BLOCK, width):
                run = slice(blk * BLOCK + r, blk * BLOCK + r + width)
                quantize(cq_codes[:, run], cq_scales[:, run], grouped[:, r : r + width, :])

        def first_tier_values(j0, number):
            values = bank(number, [PACK, P])
            for i in range(PACK):
                nc.tensor.matmul_mx(
                    out=values[:, i, :],
                    lhsT=eye_codes[:, i * P : (i + 1) * P].bitcast(FP8X4),
                    lhsT_scale=eye_scales[:, i * P : (i + 1) * P],
                    rhs=cq_codes[:, j0 : j0 + P].bitcast(FP8X4),
                    rhs_scale=cq_scales[:, j0 : j0 + P],
                    start=True,
                    stop=True,
                )
            return values

        def residual_of(blk):
            return c_grouped[0][:, (1 - blk) * BLOCK : (2 - blk) * BLOCK, :]

        def subtract_on_vector(blk, places):
            for r in range(0, places, P):
                values = first_tier_values(blk * BLOCK + r, 2 * blk + r // P)
                nc.vector.tensor_tensor(
                    out=by_word(residual_of(blk)[:, r : r + P, :], False),
                    in0=by_word(c_raw[blk][:, :, r : r + P], True),
                    in1=by_word(values[:], True),
                    op=ALU.subtract,
                )

        def subtract_by_transposes():
            runs = (3, 4, 5, 6, 7)
            negated = sbuf("negated", [len(runs), PACK, P], F32)
            rounded = {run: sbuf("rounded%d" % run, [2, P, 2], BF16) for run in runs}
            for run, number in zip(runs, (0, 4, 5, 6, 7)):
                values = first_tier_values(run * P, number)
                nc.scalar.activation(out=negated[:, run - 3], in_=values[:], func=ACT.Copy, scale=-1.0)
            for run, number in zip(runs, (3, 1, 2, 0, 4)):
                turned = bank(number, [PACK, P])
                c_run = c_raw[run // 2][:, :, run % 2 * P : (run % 2 + 1) * P]
                for term, planar in enumerate((c_run, negated[:, run - 3])):
                    for i in range(PACK):
                        nc.tensor.matmul(
                            turned[:, i, :],
                            planar[:, i, :],
                            identity[:],
                            start=(term, i) == (0, 0),
                            stop=(term, i) == (1, PACK - 1),
                            is_transpose=True,
                        )
                nc.scalar.copy(out=rounded[run][:], in_=turned[:].rearrange("j (u e) p -> j u p e", e=2))
            for run, number in zip(runs, (5, 6, 7, 3, 1)):
                words = rounded[run][:].rearrange("j u p e -> j u (p e)").bitcast(F32)
                back = bank(number, [2, P])
                for u in range(2):
                    nc.tensor.transpose(back[:, u, :], words[:, u, :], identity[:])
                nc.scalar.copy(
                    out=residual_words[:, (run - 3) * P : (run - 2) * P, :], in_=back[:].rearrange("p u j -> p j u")
                )

        def picks(u, j0, width):
            if u < PACK:
                return early_picks[:, u, j0 : j0 + width]
            if u < PACK + 2:
                return middle_picks[:, u - PACK, j0 : j0 + width]
            if u < LAST_PLANE:
                return late_picks[:, 0:BLOCKS, :].rearrange("p r j -> p (r j)")[:, j0 : j0 + width]
            return late_picks[:, LAST_ROWS[j0 // BLOCK], j0 % BLOCK : j0 % BLOCK + width]

        def gather(u, j0, width):
            nc.vector.tensor_tensor(
                out=picks(u, j0, width),
                in0=planes[u][:].indirect(offsets[:, j0 // LIST_ROWS : (j0 + width) // LIST_ROWS]),
                in1=wgt_sb[:, j0 : j0 + width],
                op=ALU.mult,
            )

        def early_xg(j0):
            cols = slice(j0, j0 + HALF)
            group_on_scalar(xg_grouped[0][:, cols, :], early_picks[:, :, cols])
            quantize(xg_early_codes[:, cols], xg_scales[:, 0, cols], xg_grouped[0][:, cols, :])

        def early_wtd(pair):
            cols = slice(pair * BLOCK, (pair + 1) * BLOCK)
            group_on_scalar(wtd_early_grouped[:, cols, :], wtd_early[:, :, cols])
            quantize(wtd_codes[0][:, cols], wtd_scales[:, 0, cols], wtd_early_grouped[:, cols, :])

        def gather_block(blk, r=0, width=BLOCK):
            gather(LAST_PLANE, blk * BLOCK + r, width)

        def group_block(group, blk, r=0, width=BLOCK):
            last = LAST_ROWS[blk]
            both = late_picks[:, blk : last + 1 : last - blk, r : r + width]
            group(xg_grouped[1][:, blk * BLOCK + r : blk * BLOCK + r + width, 2:PACK], both)

        def quantize_block(blk, r=0, width=BLOCK):
            cols = slice(blk * BLOCK + r, blk * BLOCK + r + width)
            quantize(xg_late_codes[blk][:, r : r + width], xg_scales[:, 1, cols], xg_grouped[1][:, cols, :])

        def quantize_late_wtd(pair):
            cols = slice(pair * BLOCK, (pair + 1) * BLOCK)
            quantize(wtd_codes[1][:, cols], wtd_scales[:, 1, cols], wtd_late_grouped[pair][:])

        def wx_tile(t):
            return wx_codes[:, t * P : (t + 1) * P].bitcast(FP8X4), w_scales[:, WX_SCALES, t * P : (t + 1) * P]

        def wtd_tile(a):
            return lambda t: (wtd_codes[a][:, t * P : (t + 1) * P].bitcast(FP8X4), wtd_scales[:, a, t * P : (t + 1) * P])

        def wt4_tile(a):
            return lambda t: (
                wt4_codes[:, a, 2 * t * P : 2 * (t + 1) * P].bitcast(FP4X4),
                w_scales[:, a, t * P : (t + 1) * P],
            )

        sums = {}

        def add_passes(blk, pair, stationary, codes, scales, width=BLOCK, start=False, stop=False, places=(0, BLOCK), shift=0):
            steps = [(s, r) for s in range(2) for r in range(places[0], places[1], width)]
            for s, r in steps:
                lhs_codes, lhs_scales = stationary(2 * pair + s)
                nc.tensor.matmul_mx(
                    out=sums[blk, pair][:, s, r : r + width],
                    lhsT=lhs_codes,
                    lhsT_scale=lhs_scales,
                    rhs=codes[:, r - shift : r - shift + width].bitcast(FP8X4),
                    rhs_scale=scales[:, blk * BLOCK + r : blk * BLOCK + r + width],
                    start=start and (s, r) == steps[0],
                    stop=stop and (s, r) == steps[-1],
                )

        def block_of(codes, blk):
            return codes[:, blk * BLOCK : (blk + 1) * BLOCK]

        def finish(blk, pair):
            codes = xg_late_codes[blk]
            add_passes(blk, pair, wt4_tile(1), codes, xg_scales[:, 1, :], width=P)
            add_passes(blk, pair, wtd_tile(1), codes, xg_scales[:, 1, :], stop=True)
            number = 2 * blk + pair
            result = sbuf("result%d" % number, [2, BLOCK], F32, bytes_of="plane%d" % number if number < PACK else None)
            rows = out[pair * BLOCK : (pair + 1) * BLOCK, blk * BLOCK : (blk + 1) * BLOCK].rearrange("(s p) j -> p s j", p=P)
            last = number == 2 * BLOCKS - 1
            for s in range(2):
                t = 2 * pair + s
                nc.scalar.activation(
                    out=result[:, s, :], in_=sums[blk, pair][:, s, :], func=ACT.Silu, bias=bias[:, t : t + 1]
                )
                if last:
                    nc.sync.dma_start(out=rows[:, s, :], in_=result[:, s, :])
            if not last:
                nc.sync.dma_start(out=rows, in_=result[:])

        nc.gpsimd.memset(small_rows[HEAD_ROWS:P, :], 0.0)
        nc.gpsimd.memset(eye[:, QUAD : PACK * PACK * P].bitcast(I32), 0)
        nc.vector.memset(one[:], 1.0)
        nc.scalar.activation(
            out=eye[:, 0:QUAD], in_=one[:].to_broadcast([P, QUAD]), func=ACT.Silu, scale=0.0
        )

        for q in range(P // QUAD):
            nc.vector.memset(quadrant_base[QUAD * q : QUAD * (q + 1), :], float(QUAD * q))
        ones = one[:].to_broadcast([P, P])
        nc.vector.tensor_tensor_scan(out=count[:], data0=ones, data1=ones, initial=-1.0, op0=ALU.mult, op1=ALU.add)
        nc.vector.transpose(out=lane[:], in_=count[:, 0:QUAD])
        nc.vector.tensor_scalar(
            out=identity[:],
            in0=count[:],
            scalar1=quadrant_base[:],
            scalar2=lane[:, 0:1],
            op0=ALU.subtract,
            op1=ALU.is_equal,
        )
        nc.vector.tensor_scalar(
            out=eye[:].rearrange("p (i y) -> p i y", i=PACK)[:, :, 0 : PACK * P : PACK],
            in0=count[:].unsqueeze(1).to_broadcast([P, PACK, P]),
            scalar1=quadrant_base[:],
            scalar2=lane[:, 0:1],
            op0=ALU.subtract,
            op1=ALU.is_equal,
        )
        nc.vector.quantize_mx(out=eye_codes[:].bitcast(FP8X4), scales=eye_scales[:], in_=eye[:, 0 : PACK * PACK * P])
        nc.gpsimd.memset(w_scales[:].bitcast(I32), 0)

        head_rows = wgt.rearrange("(g q) (r s) -> q g r s", q=LIST_ROWS, s=P)[0]
        nc.sync.dma_start(out=small_rows[0:HEAD_ROWS, :], in_=head_rows)
        load_planes(0)
        nc.sync.dma_start(offsets[:], offs)
        load_c(0)
        load_c(1)
        load_c(2)
        load_c(3)
        load_planes(1)
        load_wx_scales(0)
        load_wx_scales(1)
        load_planes(2)
        load_wx_scales(2)
        load_wx_scales(3)
        load_planes(3)
        load_planes(4)
        nc.sync.dma_start(out=wx_codes[:].bitcast(I32), in_=wx_words[0].rearrange("p n i -> p (n i)").bitcast(I32))
        load_planes(5)
        load_wt4_scales(0)
        load_wt4_scales(1)
        load_wt4_scales(2)
        load_wt4_scales(3)
        nc.sync.dma_start(out=wtd_early[:], in_=wtd_rows[0])
        nc.sync.dma_start(out=wt4_codes[:].bitcast(I32), in_=wt4_words.rearrange("a p n -> p a n").bitcast(I32))
        load_planes(6)
        load_planes(7)
        nc.sync.dma_start(out=wtd_late[0], in_=wtd_rows[1, :, :, 0 * BLOCK : (0 + 1) * BLOCK])
        nc.sync.dma_start(out=wtd_late[1], in_=wtd_rows[1, :, :, 1 * BLOCK : (1 + 1) * BLOCK])
        with nc.allow_non_contiguous_dma(reason="one bias value a partition and output tile"):
            nc.sync.dma_start(out=bias[:], in_=b.rearrange("(t p) -> p t", p=P))

        small_turned = bank(7, [P])
        nc.tensor.transpose(small_turned[:], small_rows[:], identity[:])
        by_run = small_turned[:, 0:HEAD_ROWS].rearrange("s (g r) -> s r g", r=J // P)
        for blk in range(BLOCKS):
            runs = slice(2 * blk, 2 * blk + 2)
            nc.scalar.copy(
                out=spread[:, runs, :].rearrange("s r (g q) -> s r g q", q=LIST_ROWS),
                in_=by_run[:, runs, :].unsqueeze(3).to_broadcast([P, 2, HEADS, LIST_ROWS]),
            )
        for blk in range(BLOCKS):
            wgt_block = bank(3 + blk, [2, P])
            for r in range(2):
                nc.tensor.transpose(wgt_block[:, r, :], spread[:, 2 * blk + r, :], identity[:])
            nc.scalar.copy(out=block_of(wgt_sb, blk), in_=wgt_block[:].rearrange("p r s -> p (r s)"))

        for blk in range(BLOCKS):
            gather(0, blk * BLOCK, BLOCK)
        first_tier(0)
        first_tier(1)
        first_tier(2)
        first_tier(3)
        subtract_on_vector(0, BLOCK)
        subtract_on_vector(1, P)
        quantize(cr_codes[0][:, 0:BLOCK], cr_scales[:, 0:BLOCK], residual_of(0))
        quantize(cr_codes[0][:, BLOCK:ROAD_START], cr_scales[:, BLOCK:ROAD_START], residual_of(1)[:, 0:P, :])

        for u in (1, 2):
            gather(u, 0, J)
        subtract_by_transposes()
        gather(3, 0, HALF)
        gather(3, HALF, HALF)
        gather(4, 0, J)
        gather(5, 0, J)
        early_xg(0)
        for first, last in ((P, J - ROAD_START), (0, P)):
            nc.vector.quantize_mx(
                out=cr_codes[1][:, first:last].bitcast(FP8X4),
                scales=cr_scales[:, ROAD_START + first : ROAD_START + last],
                in_=residual_words[:, first:last, :].rearrange("p j u -> p (j u)").bitcast(BF16),
            )
        early_xg(HALF)
        early_wtd(0)
        early_wtd(1)
        gather(6, 0, J)
        for j0 in (0, HALF):
            group_on_scalar(xg_grouped[1][:, j0 : j0 + HALF, 0:2], middle_picks[:, :, j0 : j0 + HALF])

        for blk in range(BLOCKS):
            for pair in range(2):
                sums[blk, pair] = bank(2 * blk + pair, [2, BLOCK])
                add_passes(blk, pair, wx_tile, block_of(cq_codes, blk), cq_scales, start=True)
                if blk == 1:
                    add_passes(blk, pair, wx_tile, cr_codes[0][:, BLOCK:], cr_scales, width=P, places=(0, P), shift=0)
                    add_passes(blk, pair, wx_tile, cr_codes[1][:, 0:P], cr_scales, width=P, places=(P, BLOCK), shift=P)
                else:
                    codes = cr_codes[0][:, 0:BLOCK] if blk == 0 else cr_codes[1][:, (2 * blk - 3) * P : (2 * blk - 1) * P]
                    add_passes(blk, pair, wx_tile, codes, cr_scales)
        def early_wt4(*blks):
            for blk in blks:
                for pair in range(2):
                    add_passes(blk, pair, wt4_tile(0), block_of(xg_early_codes, blk), xg_scales[:, 0, :], width=P)

        early_wt4(0, 1)
        for pair in range(2):
            for blk in range(BLOCKS):
                add_passes(blk, pair, wtd_tile(0), block_of(xg_early_codes, blk), xg_scales[:, 0, :])
        early_wt4(2, 3)

        gather_block(0)
        gather_block(1)
        group_block(group_on_scalar, 0)
        group_block(group_on_scalar, 1)
        group_on_vector(wtd_late_grouped[0][:], wtd_late[0])
        quantize_block(0)
        quantize_late_wtd(0)
        finish(0, 0)
        gather_block(2)
        quantize_block(1)
        finish(1, 0)
        group_on_scalar(wtd_late_grouped[1][:], wtd_late[1])
        quantize_late_wtd(1)
        finish(0, 1)
        finish(1, 1)
        group_block(group_on_vector, 2)
        gather_block(3, 0, P)
        quantize_block(2)
        gather_block(3, P, P)
        group_block(group_on_vector, 3, 0, P)
        group_block(group_on_vector, 3, P, P)
        quantize_block(3, 0, P)
        quantize_block(3, P, P)
        finish(2, 0)
        finish(2, 1)
        finish(3, 0)
        finish(3, 1)
